import numpy as np
import ml_dtypes


def mxq(x, axis, fmt="e4m3"):
    dtype, down = {"e4m3": (ml_dtypes.float8_e4m3fn, 7), "e5m2": (ml_dtypes.float8_e5m2, 14)}[fmt]
    v = np.moveaxis(np.asarray(x, np.float32).astype(ml_dtypes.bfloat16).astype(np.float64), axis, -1)
    blocks = v.reshape(v.shape[:-1] + (-1, 32))
    amax = np.abs(blocks).max(-1, keepdims=True)
    byte = np.maximum(np.where(amax > 0, np.frexp(amax)[1] - 1 + 127, 0) - down, 1)
    scale = np.exp2(byte - 127.0)
    codes = (blocks / scale).astype(np.float32).astype(dtype).astype(np.float64)
    return np.moveaxis((codes * scale).reshape(v.shape), -1, axis)


WIDE = False


def mx_kscale(k):
    if not WIDE:
        return np.ones(k)
    levels = np.array([10, -10, 5, -5, 0])
    if k % 512:
        return np.exp2(np.random.permutation(np.resize(levels, k // 32))).repeat(32)
    a = np.empty((k // 512, 16))
    for p in range(k // 512):
        a[p, :8] = np.random.permutation(np.resize(levels, 8))
        for g in range(8):
            far = levels[np.abs(levels - a[p, g]) >= 10]
            a[p, g + 8] = far[np.random.randint(len(far))]
    return np.exp2(a.ravel()).repeat(32)


def f64(x):
    return np.asarray(x).astype(np.float64)


def striped(idx):
    return np.tile(idx.reshape(-1, 16).T, (8, 1)).astype(np.uint16)


def unstriped(offs):
    return offs[:16].T.reshape(-1).astype(np.int64)


E2M1 = np.array([0.0, 0.5, 1.0, 1.5, 2.0, 3.0, 4.0, 6.0, -0.0, -0.5, -1.0, -1.5, -2.0, -3.0, -4.0, -6.0])


def pack_weight(w, fmt):
    k, n = w.shape
    w = f64(np.asarray(w, np.float32).astype(ml_dtypes.bfloat16)).reshape(k // 32, 32, n)
    amax = np.abs(w).max(1)
    if fmt == "e4m3":
        byte = np.frexp(amax)[1] - 1 + 127 - 7
    else:
        mant, ex = np.frexp(amax / 6.0)
        byte = np.where(mant > 0.5, ex, ex - 1) + 127
    byte = np.clip(np.where(amax > 0, byte, 1), 1, 254)
    scaled = (w * np.exp2(127.0 - byte)[:, None, :]).reshape(k, n).astype(np.float32)
    by_word = np.ascontiguousarray(scaled.reshape(k // 512, 128, 4, n).transpose(0, 1, 3, 2))
    if fmt == "e4m3":
        words = by_word.astype(ml_dtypes.float8_e4m3fn).view(np.uint8)
    else:
        c = by_word.astype(ml_dtypes.float4_e2m1fn).view(np.uint8) & 0xF
        words = (c[..., 0::2] | (c[..., 1::2] << 4)).reshape(k // 512, 128, 2 * n)
    return np.ascontiguousarray(words), np.ascontiguousarray(byte.astype(np.uint8).reshape(k // 512, 16, n))


def unpack_weight(words, scales, fmt):
    g, _, n = scales.shape
    words = np.ascontiguousarray(words).reshape(g, 128, n, -1)
    if fmt == "e4m3":
        vals = words.view(ml_dtypes.float8_e4m3fn).astype(np.float64)
    else:
        nib = np.empty((g, 128, n, 4), np.uint8)
        nib[..., 0::2] = words & 0xF
        nib[..., 1::2] = words >> 4
        vals = E2M1[nib]
    vals = vals * np.repeat(np.exp2(scales.astype(np.float64) - 127.0), 8, axis=1)[..., None]
    return vals.transpose(0, 1, 3, 2).reshape(g * 512, n)


def gelu(v):
    return 0.5 * v * (1.0 + np.tanh(np.sqrt(2.0 / np.pi) * (v + 0.044715 * v**3)))


def often(T, S):
    return np.random.permutation(T)[(T * np.random.uniform(0, 1, S) ** 4).astype(np.int64)]


def bf(x):
    return np.asarray(x, np.float32).astype(ml_dtypes.bfloat16)


def planes(Y):
    n, m = Y.shape
    b = f64(bf(Y)).reshape(n // 32, 32, m)
    amax = np.abs(b).max(1)
    byte = np.clip(np.where(amax > 0, np.frexp(amax)[1] - 1 + 127 - 7, 1), 1, 254)
    codes = (b * np.exp2(127.0 - byte)[:, None, :]).reshape(n, m).astype(np.float32).astype(ml_dtypes.float8_e4m3fn).view(np.uint8)
    words = codes.reshape(n // 512, 128, 4, m).transpose(0, 1, 3, 2)
    return np.ascontiguousarray(words), np.ascontiguousarray(byte.astype(np.uint8).reshape(n // 512, 16, m))


K, K2, T, T2, S, H, N = 1024, 512, 2048, 1024, 512, 1024, 1024

def setup_inputs():
    n = np.random.standard_normal
    s = mx_kscale(K)[:, None]
    s2 = mx_kscale(K2)[:, None]
    u = mx_kscale(H)[:, None]
    size = np.exp(0.8 * n(N))[None, :]
    tab_words, tab_scales = pack_weight(n((K, T)) * s, "e4m3")
    tab2_words, tab2_scales = pack_weight(n((K2, T2)) * s2, "e2m1")
    w1_words, w1_scales = pack_weight(n((K, H)) / np.sqrt(K) / s, "e2m1")
    w3_words, w3_scales = pack_weight(n((H, N)) * size / np.sqrt(H) / u, "e4m3")
    return {
        "tab_words": tab_words, "tab_scales": tab_scales,
        "tab2_words": tab2_words, "tab2_scales": tab2_scales,
        "offs": striped(often(T, S)),
        "offs2": striped(often(T2, S)),
        "w1_words": w1_words, "w1_scales": w1_scales,
        "w2": (0.7 * n((K2, H)) / np.sqrt(K2) / s2).astype(np.float32),
        "w3_words": w3_words, "w3_scales": w3_scales,
        "w4": (1.4 * n((H, N)) * size / np.sqrt(H) / u).astype(np.float32),
        "gain": (np.exp(0.3 * n(H)) * u[:, 0]).astype(np.float32),
        "travel": (0.5 * n((H, S)) * u).astype(np.float32),
    }

def reference(tab_words, tab_scales, tab2_words, tab2_scales, offs, offs2,
              w1_words, w1_scales, w2, w3_words, w3_scales, w4, gain, travel):
    v = unpack_weight(tab_words, tab_scales, "e4m3")[:, unstriped(offs)]
    v2 = unpack_weight(tab2_words, tab2_scales, "e2m1")[:, unstriped(offs2)]
    w1 = unpack_weight(w1_words, w1_scales, "e2m1")
    w3 = unpack_weight(w3_words, w3_scales, "e4m3")
    slip = w1.T @ v
    site = mxq(f64(w2), 0, "e4m3").T @ v2
    h = np.tanh(slip) * f64(gain)[:, None]
    z = h / (1.0 + np.exp(site)) + f64(travel)
    hq = mxq(h, 0, "e4m3")
    zq = mxq(z, 0, "e4m3")
    y = w3.T @ hq + mxq(f64(w4), 0, "e4m3").T @ zq
    words, scales = planes(y)
    return y, words, scales

@@ -1,0 +1,288 @@
+from contextlib import ExitStack
+
+import concourse.mybir as mybir
+
+F32 = mybir.dt.float32
+BF16 = mybir.dt.bfloat16
+I32 = mybir.dt.int32
+U32 = mybir.dt.uint32
+U16 = mybir.dt.uint16
+U8 = mybir.dt.uint8
+FP8X4 = mybir.dt.float8_e4m3fn_x4
+FP4X4 = mybir.dt.float4_e2m1fn_x4
+ACT = mybir.ActivationFunctionType
+ALU = mybir.AluOpType
+
+P = 128
+PACK = 4
+KP = P * PACK
+K, K2, T, T2, S, H, N = 1024, 512, 2048, 1024, 512, 1024, 1024
+FLOPS = 2 * S * (K * H + K2 * H + 2 * H * N)
+
+
+def tile_list_rupture_site_features_kernel(
+    tc, tab_words, tab_scales, tab2_words, tab2_scales, offs, offs2,
+    w1_words, w1_scales, w2, w3_words, w3_scales, w4, gain, travel,
+    out_0, out_1, out_2,
+):
+    nc = tc.nc
+    with ExitStack() as ctx:
+        lists = ctx.enter_context(tc.tile_pool(name="lists", bufs=1))
+        keep = ctx.enter_context(tc.tile_pool(name="keep", bufs=1))
+        land = ctx.enter_context(tc.tile_pool(name="land", bufs=1))
+        stage = ctx.enter_context(tc.tile_pool(name="stage", bufs=8))
+        psum = ctx.enter_context(tc.psum_pool(name="psum", bufs=8))
+
+        def held(shape, dtype, name):
+            return keep.tile(shape, dtype, name=name, align_bytes=64)
+
+        def landed(shape, dtype, name, lane):
+            return land.tile(shape, dtype, name=name, tag=f"lane{lane}", align_bytes=64)
+
+        def staged(name):
+            return stage.tile([P, PACK * S], BF16, name=name, tag="staged", align_bytes=64)
+
+        def bank(name):
+            return psum.tile([P, S], F32, name=name, tag="bank")
+
+        offs_sb = lists.tile([P, S // 16], U16, name="offs_sb")
+        offs2_sb = lists.tile([P, S // 16], U16, name="offs2_sb")
+
+        tab2_s = landed([P, T2], U8, "tab2_s", "A")
+        tab2_w = landed([P, T2], U16, "tab2_w", "B")
+        tab_s = held([P, 2, T], U8, "tab_s")
+        w1_s = held([P, 2, H], U8, "w1_s")
+        w1_w = held([P, 2, H], U16, "w1_w")
+        gain_sb = held([P, 2, PACK], F32, "gain_sb")
+        warm = held([P, 8], F32, "warm")
+
+        nc.vector.memset(tab2_s[:].bitcast(I32), 0)
+        nc.vector.memset(warm[:], 0.0)
+        nc.vector.memset(w1_s[:].rearrange("p a n -> p (a n)").bitcast(I32), 0)
+        nc.vector.memset(tab_s[:].rearrange("p a n -> p (a n)").bitcast(I32), 0)
+        nc.scalar.activation(out=warm[:], in_=warm[:], func=ACT.Sigmoid)
+
+        def load_rows(src, name, lane):
+            raw = landed([P, PACK, S], F32, name, lane)
+            nc.sync.dma_start(out=raw[:], in_=src.rearrange("(p j) c -> p j c", j=PACK))
+            return raw
+
+        def load_tab(a, lane):
+            words = landed([P, T], I32, f"tab_w{a}", lane)
+            nc.sync.dma_start(out=words[:], in_=tab_words[a].rearrange("p n t -> p (n t)").bitcast(I32))
+            return words
+
+        def load_w3(g, lane):
+            words = landed([P, 2, KP], I32, f"w3_w{g}", lane)
+            nc.sync.dma_start(
+                out=words[:],
+                in_=w3_words[:, :, KP * g : KP * (g + 1), :].rearrange("a p n t -> p a (n t)").bitcast(I32))
+            return words
+
+        def load_w4(a, g, lane):
+            return load_rows(w4[KP * a : KP * (a + 1), KP * g : KP * (g + 1)], f"w4_raw{a}{g}", lane)
+
+        nc.sync.dma_start(offs2_sb[:], offs2)
+        nc.sync.dma_start(offs_sb[:], offs)
+        nc.sync.dma_start(out=tab2_w[:].bitcast(I32), in_=tab2_words[0].bitcast(I32))
+        w2_raw = [None, None]
+        w2_raw[0] = load_rows(w2[:, 0:KP], "w2_raw0", "C")
+        nc.sync.dma_start(out=w1_w[:].bitcast(I32), in_=w1_words.rearrange("a p n -> p a n").bitcast(I32))
+        for q in range(4):
+            nc.scalar.dma_start(out=tab2_s[32 * q : 32 * q + 4, :].bitcast(I32),
+                                in_=tab2_scales[0, 4 * q : 4 * q + 4, :].bitcast(I32))
+        for q in range(4):
+            nc.sync.dma_start(out=tab_s[32 * q : 32 * q + 4, :, :].bitcast(I32),
+                                in_=tab_scales[:, 4 * q : 4 * q + 4, :].rearrange("a r n -> r a n").bitcast(I32))
+        for q in range(4):
+            nc.gpsimd.dma_start(out=w1_s[32 * q : 32 * q + 4, :, :].bitcast(I32),
+                                in_=w1_scales[:, 4 * q : 4 * q + 4, :].rearrange("a r n -> r a n").bitcast(I32))
+        nc.gpsimd.dma_start(out=gain_sb[:], in_=gain.rearrange("(b p t) -> p b t", b=2, t=PACK))
+        tab_w = [None, None]
+        travel_sb = [None, None]
+        w3_w = [None, None]
+        w4_raw = {}
+
+        def deal(dst, src, run):
+            nc.vector.tensor_copy(
+                out=dst.rearrange("p a (t c i) -> p a c t i", t=PACK, i=run),
+                in_=src.rearrange("p a (c i t) -> p a c t i", t=PACK, i=run))
+
+        def round_weight(raw, name):
+            wb = staged(name)
+            nc.scalar.copy(
+                out=wb[:].rearrange("p (u v m j) -> p m u j v", u=2, v=2, j=PACK),
+                in_=raw[:].rearrange("p j (m u v) -> p m u j v", u=2, v=2))
+            return wb
+
+        def quantize(vals, name):
+            codes = held([P, S], U32, name + "_codes")
+            scales = held([P, S], U8, name + "_scales")
+            nc.vector.quantize_mx(out=codes[:].bitcast(FP8X4), scales=scales[:], in_=vals[:])
+            return codes, scales
+
+        def woven(tile_):
+            return tile_[:].rearrange("p (c i t) -> p c t i", i=2, t=PACK)
+
+        def by_pairs(tile_):
+            return tile_[:].rearrange("p t (c i) -> p c t i", i=2)
+
+        v2_s = landed([P, S], U8, "v2_s", "I")
+        v2_w = landed([P, S], U16, "v2_w", "D")
+        nc.vector.tensor_copy(v2_s[:], tab2_s[:].indirect(offs2_sb[:]))
+        nc.vector.tensor_copy(v2_w[:], tab2_w[:].indirect(offs2_sb[:]))
+        w2_raw[1] = load_rows(w2[:, KP : 2 * KP], "w2_raw1", "A")
+        tab_w[0] = load_tab(0, "B")
+        w2_b = [None, None]
+        w2_b[0] = round_weight(w2_raw[0], "w2_b0")
+        tab_w[1] = load_tab(1, "C")
+        w1d_w = held([P, 4, KP], U16, "w1d_w")
+        w1d_s = held([P, 4, KP], U8, "w1d_s")
+        deal(w1d_w[:], w1_w[:].rearrange("p a (b n) -> p (a b) n", b=2), 4)
+        deal(w1d_s[:], w1_s[:].rearrange("p a (b n) -> p (a b) n", b=2), 8)
+        w2_q = [None, None]
+        w2_q[0] = quantize(w2_b[0], "w2q0")
+        w2_b[1] = round_weight(w2_raw[1], "w2_b1")
+        travel_sb[0] = load_rows(travel[0:KP, :], "travel0", "A")
+        v_s = [landed([P, S], U8, f"v_s{a}", "GH"[a]) for a in range(2)]
+        v_w = [landed([P, S], U32, f"v_w{a}", "EF"[a]) for a in range(2)]
+        for a in range(2):
+            nc.vector.tensor_copy(v_s[a][:], tab_s[:, a, :].indirect(offs_sb[:]))
+        w2_q[1] = quantize(w2_b[1], "w2q1")
+
+        damp = [held([P, PACK, S], F32, f"damp{b}") for b in range(2)]
+        sat = [held([P, PACK, S], F32, f"sat{b}") for b in range(2)]
+
+        def site(b):
+            codes, scales = w2_q[b]
+            for t in range(PACK):
+                cols = slice(P * t, P * (t + 1))
+                acc = bank(f"site{b}{t}")
+                nc.tensor.matmul_mx(out=acc[:], lhsT=codes[:, cols].bitcast(FP8X4), lhsT_scale=scales[:, cols],
+                                    rhs=v2_w[:].bitcast(FP4X4), rhs_scale=v2_s[:], start=True, stop=True)
+                nc.scalar.activation(out=damp[b][:, t, :], in_=acc[:], func=ACT.Sigmoid, scale=-1.0)
+
+        def slip(b):
+            for t in range(PACK):
+                cols = slice(P * t, P * (t + 1))
+                acc = bank(f"slip{b}{t}")
+                for a in range(2):
+                    nc.tensor.matmul_mx(out=acc[:], lhsT=w1d_w[:, 2 * a + b, cols].bitcast(FP4X4),
+                                        lhsT_scale=w1d_s[:, 2 * a + b, cols],
+                                        rhs=v_w[a][:].bitcast(FP8X4), rhs_scale=v_s[a][:],
+                                        start=(a == 0), stop=(a == 1))
+                nc.scalar.activation(out=sat[b][:, t, :], in_=acc[:], func=ACT.Tanh)
+
+        site(0)
+        site(1)
+        for a in range(2):
+            nc.vector.tensor_copy(v_w[a][:], tab_w[a][:].bitcast(U32).indirect(offs_sb[:]))
+        w4_raw[0, 0] = load_w4(0, 0, "B")
+        travel_sb[1] = load_rows(travel[KP : 2 * KP, :], "travel1", "C")
+        w4_raw[1, 0] = load_w4(1, 0, "D")
+        w3_s = landed([P, N], U8, "w3_s", "I")
+        nc.vector.memset(w3_s[:].bitcast(I32), 0)
+        for q in range(4):
+            nc.sync.dma_start(out=w3_s[32 * q : 32 * q + 8, :].bitcast(I32),
+                              in_=w3_scales[:, 4 * q : 4 * q + 4, :].bitcast(I32))
+        slip(0)
+        slip(1)
+        w3_w[0] = load_w3(0, "E")
+        w4_raw[0, 1] = load_w4(0, 1, "F")
+        w3_w[1] = load_w3(1, "G")
+        w4_raw[1, 1] = load_w4(1, 1, "H")
+
+        hq = [None, None]
+        zq = [None, None]
+
+        def damped(b):
+            for t in range(PACK):
+                nc.vector.scalar_tensor_tensor(
+                    out=damp[b][:, t, :], in0=sat[b][:, t, :], scalar=gain_sb[:, b, t : t + 1],
+                    in1=damp[b][:, t, :], op0=ALU.mult, op1=ALU.mult)
+
+        def h_scaled(b):
+            rows = stage.tile([P, PACK, S], BF16, name=f"h_rows{b}", tag="staged", align_bytes=64)
+            for t in range(PACK):
+                nc.scalar.activation(out=rows[:, t, :], in_=sat[b][:, t, :], func=ACT.Copy,
+                                     scale=gain_sb[:, b, t : t + 1])
+            return rows
+
+        def weave(rows, name):
+            vals = staged(name)
+            nc.vector.tensor_copy(out=woven(vals), in_=by_pairs(rows))
+            return vals
+
+        def z_rounded(b):
+            zb = staged(f"z_b{b}")
+            nc.vector.tensor_tensor(out=woven(zb), in0=by_pairs(damp[b]), in1=by_pairs(travel_sb[b]), op=ALU.add)
+            return zb
+
+        w3d_s = held([P, 2, KP], U8, "w3d_s")
+        w3d_w = [held([P, 2, KP], I32, f"w3d_w{g}") for g in range(2)]
+        w4_b = {}
+        w4_q = {}
+
+        damped(0)
+        hr0 = h_scaled(0)
+        zb0 = z_rounded(0)
+        hr1 = h_scaled(1)
+        hb0 = weave(hr0, "h_b0")
+        zq[0] = quantize(zb0, "zq0")
+        w4_b[0, 0] = round_weight(w4_raw[0, 0], "w4_b00")
+        damped(1)
+        hq[0] = quantize(hb0, "hq0")
+        w4_b[1, 0] = round_weight(w4_raw[1, 0], "w4_b10")
+        hb1 = weave(hr1, "h_b1")
+        w4_q[0, 0] = quantize(w4_b[0, 0], "w4q00")
+        deal(w3d_s[:], w3_s[:].rearrange("p (g n) -> p g n", g=2), 8)
+        hq[1] = quantize(hb1, "hq1")
+        deal(w3d_w[0][:], w3_w[0][:], 2)
+        zb1 = z_rounded(1)
+        w4_q[1, 0] = quantize(w4_b[1, 0], "w4q10")
+        zq[1] = quantize(zb1, "zq1")
+
+        y_scales = held([P, 2, S], U8, "y_scales")
+
+        def project(g):
+            accs = [bank(f"y{g}{t}") for t in range(PACK)]
+            passes = [(4, 0), (3, 0), (3, 1), (4, 1)]
+            for i, (which, a) in enumerate(passes):
+                for t in range(PACK):
+                    cols = slice(P * t, P * (t + 1))
+                    if which == 3:
+                        lw, ls = w3d_w[g][:, a, cols], w3d_s[4 * a : P, g, cols]
+                        rw, rs = hq[a]
+                    else:
+                        lw, ls = w4_q[a, g][0][:, cols], w4_q[a, g][1][:, cols]
+                        rw, rs = zq[a]
+                    nc.tensor.matmul_mx(out=accs[t][:], lhsT=lw.bitcast(FP8X4), lhsT_scale=ls,
+                                        rhs=rw[:].bitcast(FP8X4), rhs_scale=rs[:],
+                                        start=(i == 0), stop=(i == len(passes) - 1))
+            return accs
+
+        def hand_out(g, accs):
+            y = held([P, PACK, S], F32, f"y{g}")
+            rows = out_0[KP * g : KP * (g + 1), :].rearrange("(p t) s -> p t s", t=PACK)
+            for t in range(PACK):
+                nc.scalar.copy(out=y[:, t, :], in_=accs[t][:])
+                if t % 2 == 1:
+                    nc.sync.dma_start(out=rows[:, t - 1 : t + 1, :], in_=y[:, t - 1 : t + 1, :])
+            yb = weave(y, f"y_b{g}")
+            codes = held([P, S], U32, f"y_codes{g}")
+            nc.vector.quantize_mx(out=codes[:].bitcast(FP8X4), scales=y_scales[:, g, :], in_=yb[:])
+            nc.sync.dma_start(out=out_1[g].rearrange("p m t -> p (m t)").bitcast(I32), in_=codes[:].bitcast(I32))
+
+        accs0 = project(0)
+        for a in range(2):
+            w4_b[a, 1] = round_weight(w4_raw[a, 1], f"w4_b{a}1")
+        deal(w3d_w[1][:], w3_w[1][:], 2)
+        for a in range(2):
+            w4_q[a, 1] = quantize(w4_b[a, 1], f"w4q{a}1")
+        accs1 = project(1)
+        hand_out(0, accs0)
+        hand_out(1, accs1)
+        for q in range(4):
+            nc.scalar.dma_start(
+                out=out_2[:, 4 * q : 4 * q + 4, :].rearrange("g r m -> r g m").bitcast(I32),
+                in_=y_scales[32 * q : 32 * q + 4, :, :].bitcast(I32))

@@ -29,15 +29,11 @@ def tile_list_rupture_site_features_kernel(
     with ExitStack() as ctx:
         lists = ctx.enter_context(tc.tile_pool(name="lists", bufs=1))
         keep = ctx.enter_context(tc.tile_pool(name="keep", bufs=1))
-        land = ctx.enter_context(tc.tile_pool(name="land", bufs=1))
         stage = ctx.enter_context(tc.tile_pool(name="stage", bufs=8))
         psum = ctx.enter_context(tc.psum_pool(name="psum", bufs=8))
 
-        def held(shape, dtype, name):
-            return keep.tile(shape, dtype, name=name, align_bytes=64)
-
-        def landed(shape, dtype, name, lane):
-            return land.tile(shape, dtype, name=name, tag=f"lane{lane}", align_bytes=64)
+        def held(shape, dtype, name, slot=None):
+            return keep.tile(shape, dtype, name=name, tag=slot or name, align_bytes=64)
 
         def staged(name):
             return stage.tile([P, PACK * S], BF16, name=name, tag="staged", align_bytes=64)
@@ -45,63 +41,16 @@ def tile_list_rupture_site_features_kernel(
         def bank(name):
             return psum.tile([P, S], F32, name=name, tag="bank")
 
-        offs_sb = lists.tile([P, S // 16], U16, name="offs_sb")
-        offs2_sb = lists.tile([P, S // 16], U16, name="offs2_sb")
+        def clear(plane):
+            nc.vector.memset(plane.bitcast(I32), 0)
 
-        tab2_s = landed([P, T2], U8, "tab2_s", "A")
-        tab2_w = landed([P, T2], U16, "tab2_w", "B")
-        tab_s = held([P, 2, T], U8, "tab_s")
-        w1_s = held([P, 2, H], U8, "w1_s")
-        w1_w = held([P, 2, H], U16, "w1_w")
-        gain_sb = held([P, 2, PACK], F32, "gain_sb")
-        warm = held([P, 8], F32, "warm")
+        def load_scale_rows(queue, plane, scales):
+            for q in range(4):
+                queue.dma_start(out=plane[32 * q : 32 * q + 4].bitcast(I32),
+                                in_=scales[:, 4 * q : 4 * q + 4, :].rearrange("a r n -> r a n").bitcast(I32))
 
-        nc.vector.memset(tab2_s[:].bitcast(I32), 0)
-        nc.vector.memset(warm[:], 0.0)
-        nc.vector.memset(w1_s[:].rearrange("p a n -> p (a n)").bitcast(I32), 0)
-        nc.vector.memset(tab_s[:].rearrange("p a n -> p (a n)").bitcast(I32), 0)
-        nc.scalar.activation(out=warm[:], in_=warm[:], func=ACT.Sigmoid)
-
-        def load_rows(src, name, lane):
-            raw = landed([P, PACK, S], F32, name, lane)
-            nc.sync.dma_start(out=raw[:], in_=src.rearrange("(p j) c -> p j c", j=PACK))
-            return raw
-
-        def load_tab(a, lane):
-            words = landed([P, T], I32, f"tab_w{a}", lane)
-            nc.sync.dma_start(out=words[:], in_=tab_words[a].rearrange("p n t -> p (n t)").bitcast(I32))
-            return words
-
-        def load_w3(g, lane):
-            words = landed([P, 2, KP], I32, f"w3_w{g}", lane)
-            nc.sync.dma_start(
-                out=words[:],
-                in_=w3_words[:, :, KP * g : KP * (g + 1), :].rearrange("a p n t -> p a (n t)").bitcast(I32))
-            return words
-
-        def load_w4(a, g, lane):
-            return load_rows(w4[KP * a : KP * (a + 1), KP * g : KP * (g + 1)], f"w4_raw{a}{g}", lane)
-
-        nc.sync.dma_start(offs2_sb[:], offs2)
-        nc.sync.dma_start(offs_sb[:], offs)
-        nc.sync.dma_start(out=tab2_w[:].bitcast(I32), in_=tab2_words[0].bitcast(I32))
-        w2_raw = [None, None]
-        w2_raw[0] = load_rows(w2[:, 0:KP], "w2_raw0", "C")
-        nc.sync.dma_start(out=w1_w[:].bitcast(I32), in_=w1_words.rearrange("a p n -> p a n").bitcast(I32))
-        for q in range(4):
-            nc.scalar.dma_start(out=tab2_s[32 * q : 32 * q + 4, :].bitcast(I32),
-                                in_=tab2_scales[0, 4 * q : 4 * q + 4, :].bitcast(I32))
-        for q in range(4):
-            nc.sync.dma_start(out=tab_s[32 * q : 32 * q + 4, :, :].bitcast(I32),
-                                in_=tab_scales[:, 4 * q : 4 * q + 4, :].rearrange("a r n -> r a n").bitcast(I32))
-        for q in range(4):
-            nc.gpsimd.dma_start(out=w1_s[32 * q : 32 * q + 4, :, :].bitcast(I32),
-                                in_=w1_scales[:, 4 * q : 4 * q + 4, :].rearrange("a r n -> r a n").bitcast(I32))
-        nc.gpsimd.dma_start(out=gain_sb[:], in_=gain.rearrange("(b p t) -> p b t", b=2, t=PACK))
-        tab_w = [None, None]
-        travel_sb = [None, None]
-        w3_w = [None, None]
-        w4_raw = {}
+        def load_rows(dst, src):
+            nc.sync.dma_start(out=dst, in_=src.rearrange("(p j) c -> p j c", j=PACK))
 
         def deal(dst, src, run):
             nc.vector.tensor_copy(
@@ -109,11 +58,11 @@ def tile_list_rupture_site_features_kernel(
                 in_=src.rearrange("p a (c i t) -> p a c t i", t=PACK, i=run))
 
         def round_weight(raw, name):
-            wb = staged(name)
+            vals = staged(name)
             nc.scalar.copy(
-                out=wb[:].rearrange("p (u v m j) -> p m u j v", u=2, v=2, j=PACK),
-                in_=raw[:].rearrange("p j (m u v) -> p m u j v", u=2, v=2))
-            return wb
+                out=vals[:].rearrange("p (u v m j) -> p m u j v", u=2, v=2, j=PACK),
+                in_=raw.rearrange("p j (m u v) -> p m u j v", u=2, v=2))
+            return vals
 
         def quantize(vals, name):
             codes = held([P, S], U32, name + "_codes")
@@ -121,37 +70,64 @@ def tile_list_rupture_site_features_kernel(
             nc.vector.quantize_mx(out=codes[:].bitcast(FP8X4), scales=scales[:], in_=vals[:])
             return codes, scales
 
-        def woven(tile_):
-            return tile_[:].rearrange("p (c i t) -> p c t i", i=2, t=PACK)
+        def woven(vals):
+            return vals[:].rearrange("p (c i t) -> p c t i", i=2, t=PACK)
 
-        def by_pairs(tile_):
-            return tile_[:].rearrange("p t (c i) -> p c t i", i=2)
+        def by_pairs(rows):
+            return rows.rearrange("p t (c i) -> p c t i", i=2)
 
-        v2_s = landed([P, S], U8, "v2_s", "I")
-        v2_w = landed([P, S], U16, "v2_w", "D")
-        nc.vector.tensor_copy(v2_s[:], tab2_s[:].indirect(offs2_sb[:]))
+        offs_sb = lists.tile([P, S // 16], U16, name="offs_sb")
+        offs2_sb = lists.tile([P, S // 16], U16, name="offs2_sb")
+        tab2_s = held([P, 1, T2], U8, "tab2_s", "slot_a")
+        tab2_w = held([P, T2], U16, "tab2_w", "slot_b")
+        tab_s = held([P, 2, T], U8, "tab_s", "slot_c")
+        w1_w = held([P, 2, H], U16, "w1_w", "slot_d")
+        warm = held([P, 8], F32, "warm", "slot_e")
+        w2_raw = [held([P, PACK, S], F32, "w2_raw0", "slot_f"), held([P, PACK, S], F32, "w2_raw1", "slot_g")]
+        gain_sb = held([P, 2, PACK], F32, "gain_sb")
+
+        clear(tab2_s[:, 0, :])
+        clear(tab_s[:].rearrange("p a n -> p (a n)"))
+        nc.vector.memset(warm[:], 0.0)
+        nc.scalar.activation(out=warm[:], in_=warm[:], func=ACT.Sigmoid)
+
+        def load_tab(a, slot):
+            words = held([P, T], I32, f"tab_w{a}", slot)
+            nc.sync.dma_start(out=words[:], in_=tab_words[a].rearrange("p n t -> p (n t)").bitcast(I32))
+            return words
+
+        nc.sync.dma_start(offs2_sb[:], offs2)
+        nc.sync.dma_start(out=tab2_w[:].bitcast(I32), in_=tab2_words[0].bitcast(I32))
+        nc.sync.dma_start(out=w1_w[:].bitcast(I32), in_=w1_words.rearrange("a p n -> p a n").bitcast(I32))
+        nc.sync.dma_start(offs_sb[:], offs)
+        load_rows(w2_raw[0][:], w2[:, 0:KP])
+        nc.sync.dma_start(out=gain_sb[:], in_=gain.rearrange("(b p t) -> p b t", b=2, t=PACK))
+        load_scale_rows(nc.sync, tab2_s, tab2_scales)
+        load_rows(w2_raw[1][:], w2[:, KP : 2 * KP])
+        load_scale_rows(nc.sync, tab_s, tab_scales)
+        tab_w = [load_tab(0, "slot_e"), None]
+
+        v2_w = held([P, S], U16, "v2_w")
+        v2_s = held([P, S], U8, "v2_s")
         nc.vector.tensor_copy(v2_w[:], tab2_w[:].indirect(offs2_sb[:]))
-        w2_raw[1] = load_rows(w2[:, KP : 2 * KP], "w2_raw1", "A")
-        tab_w[0] = load_tab(0, "B")
-        w2_b = [None, None]
-        w2_b[0] = round_weight(w2_raw[0], "w2_b0")
-        tab_w[1] = load_tab(1, "C")
-        w1d_w = held([P, 4, KP], U16, "w1d_w")
-        w1d_s = held([P, 4, KP], U8, "w1d_s")
-        deal(w1d_w[:], w1_w[:].rearrange("p a (b n) -> p (a b) n", b=2), 4)
-        deal(w1d_s[:], w1_s[:].rearrange("p a (b n) -> p (a b) n", b=2), 8)
-        w2_q = [None, None]
-        w2_q[0] = quantize(w2_b[0], "w2q0")
-        w2_b[1] = round_weight(w2_raw[1], "w2_b1")
-        travel_sb[0] = load_rows(travel[0:KP, :], "travel0", "A")
-        v_s = [landed([P, S], U8, f"v_s{a}", "GH"[a]) for a in range(2)]
-        v_w = [landed([P, S], U32, f"v_w{a}", "EF"[a]) for a in range(2)]
-        for a in range(2):
-            nc.vector.tensor_copy(v_s[a][:], tab_s[:, a, :].indirect(offs_sb[:]))
-        w2_q[1] = quantize(w2_b[1], "w2q1")
+        w1_s = held([P, 2, H], U8, "w1_s", "slot_b")
+        clear(w1_s[:].rearrange("p a n -> p (a n)"))
+        load_scale_rows(nc.sync, w1_s, w1_scales)
+        nc.vector.tensor_copy(v2_s[:], tab2_s[:, 0, :].indirect(offs2_sb[:]))
+        w3_s = held([P, N], U8, "w3_s", "slot_a")
+        clear(w3_s[:])
 
         damp = [held([P, PACK, S], F32, f"damp{b}") for b in range(2)]
         sat = [held([P, PACK, S], F32, f"sat{b}") for b in range(2)]
+        w2_q, w4_raw, w4_q, hq, zq, travel_sb = {}, {}, {}, {}, {}, {}
+
+        def load_travel(b, slot):
+            travel_sb[b] = held([P, PACK, S], F32, f"travel{b}", slot)
+            load_rows(travel_sb[b][:], travel[KP * b : KP * (b + 1), :])
+
+        def load_w4(a, g, slot):
+            w4_raw[a, g] = held([P, PACK, S], F32, f"w4_raw{a}{g}", slot)
+            load_rows(w4_raw[a, g][:], w4[KP * a : KP * (a + 1), KP * g : KP * (g + 1)])
 
         def site(b):
             codes, scales = w2_q[b]
@@ -173,28 +149,6 @@ def tile_list_rupture_site_features_kernel(
                                         start=(a == 0), stop=(a == 1))
                 nc.scalar.activation(out=sat[b][:, t, :], in_=acc[:], func=ACT.Tanh)
 
-        site(0)
-        site(1)
-        for a in range(2):
-            nc.vector.tensor_copy(v_w[a][:], tab_w[a][:].bitcast(U32).indirect(offs_sb[:]))
-        w4_raw[0, 0] = load_w4(0, 0, "B")
-        travel_sb[1] = load_rows(travel[KP : 2 * KP, :], "travel1", "C")
-        w4_raw[1, 0] = load_w4(1, 0, "D")
-        w3_s = landed([P, N], U8, "w3_s", "I")
-        nc.vector.memset(w3_s[:].bitcast(I32), 0)
-        for q in range(4):
-            nc.sync.dma_start(out=w3_s[32 * q : 32 * q + 8, :].bitcast(I32),
-                              in_=w3_scales[:, 4 * q : 4 * q + 4, :].bitcast(I32))
-        slip(0)
-        slip(1)
-        w3_w[0] = load_w3(0, "E")
-        w4_raw[0, 1] = load_w4(0, 1, "F")
-        w3_w[1] = load_w3(1, "G")
-        w4_raw[1, 1] = load_w4(1, 1, "H")
-
-        hq = [None, None]
-        zq = [None, None]
-
         def damped(b):
             for t in range(PACK):
                 nc.vector.scalar_tensor_tensor(
@@ -210,78 +164,105 @@ def tile_list_rupture_site_features_kernel(
 
         def weave(rows, name):
             vals = staged(name)
-            nc.vector.tensor_copy(out=woven(vals), in_=by_pairs(rows))
+            nc.vector.tensor_copy(out=woven(vals), in_=by_pairs(rows[:]))
             return vals
 
         def z_rounded(b):
-            zb = staged(f"z_b{b}")
-            nc.vector.tensor_tensor(out=woven(zb), in0=by_pairs(damp[b]), in1=by_pairs(travel_sb[b]), op=ALU.add)
-            return zb
+            vals = staged(f"z_b{b}")
+            nc.vector.tensor_tensor(out=woven(vals), in0=by_pairs(damp[b][:]), in1=by_pairs(travel_sb[b][:]), op=ALU.add)
+            return vals
+
+        w2_q[0] = quantize(round_weight(w2_raw[0][:], "w2_b0"), "w2q0")
+        site(0)
+        w2_q[1] = quantize(round_weight(w2_raw[1][:], "w2_b1"), "w2q1")
+        site(1)
+        w1d_w = held([P, 4, KP], U16, "w1d_w")
+        w1d_s = held([P, 4, KP], U8, "w1d_s")
+        deal(w1d_w[:], w1_w[:].rearrange("p a (b n) -> p (a b) n", b=2), 4)
+        tab_w[1] = load_tab(1, "slot_d")
+        for q in range(4):
+            nc.sync.dma_start(out=w3_s[32 * q : 32 * q + 8, :].bitcast(I32),
+                              in_=w3_scales[:, 4 * q : 4 * q + 4, :].bitcast(I32))
+        w3_w = held([P, 2, N], I32, "w3_w", "slot_f")
+        nc.sync.dma_start(out=w3_w[:], in_=w3_words.rearrange("a p n t -> p a (n t)").bitcast(I32))
+        v_s = [held([P, S], U8, f"v_s{a}") for a in range(2)]
+        v_w = [held([P, S], U32, "v_w0", "slot_h"), held([P, S], U32, "v_w1")]
+        for a in range(2):
+            nc.vector.tensor_copy(v_s[a][:], tab_s[:, a, :].indirect(offs_sb[:]))
+        load_travel(0, "slot_c")
+        load_w4(0, 0, "slot_g")
+        deal(w1d_s[:], w1_s[:].rearrange("p a (b n) -> p (a b) n", b=2), 8)
+        for a in range(2):
+            nc.vector.tensor_copy(v_w[a][:], tab_w[a][:].bitcast(U32).indirect(offs_sb[:]))
+        load_w4(1, 0, "slot_e")
+        load_travel(1, "slot_b")
+        load_w4(0, 1, "slot_d")
+        slip(0)
+        slip(1)
+        load_w4(1, 1, "slot_h")
 
         w3d_s = held([P, 2, KP], U8, "w3d_s")
         w3d_w = [held([P, 2, KP], I32, f"w3d_w{g}") for g in range(2)]
-        w4_b = {}
-        w4_q = {}
-
-        damped(0)
-        hr0 = h_scaled(0)
-        zb0 = z_rounded(0)
-        hr1 = h_scaled(1)
-        hb0 = weave(hr0, "h_b0")
-        zq[0] = quantize(zb0, "zq0")
-        w4_b[0, 0] = round_weight(w4_raw[0, 0], "w4_b00")
-        damped(1)
-        hq[0] = quantize(hb0, "hq0")
-        w4_b[1, 0] = round_weight(w4_raw[1, 0], "w4_b10")
-        hb1 = weave(hr1, "h_b1")
-        w4_q[0, 0] = quantize(w4_b[0, 0], "w4q00")
-        deal(w3d_s[:], w3_s[:].rearrange("p (g n) -> p g n", g=2), 8)
-        hq[1] = quantize(hb1, "hq1")
-        deal(w3d_w[0][:], w3_w[0][:], 2)
-        zb1 = z_rounded(1)
-        w4_q[1, 0] = quantize(w4_b[1, 0], "w4q10")
-        zq[1] = quantize(zb1, "zq1")
-
         y_scales = held([P, 2, S], U8, "y_scales")
 
-        def project(g):
-            accs = [bank(f"y{g}{t}") for t in range(PACK)]
-            passes = [(4, 0), (3, 0), (3, 1), (4, 1)]
-            for i, (which, a) in enumerate(passes):
-                for t in range(PACK):
-                    cols = slice(P * t, P * (t + 1))
-                    if which == 3:
-                        lw, ls = w3d_w[g][:, a, cols], w3d_s[4 * a : P, g, cols]
-                        rw, rs = hq[a]
-                    else:
-                        lw, ls = w4_q[a, g][0][:, cols], w4_q[a, g][1][:, cols]
-                        rw, rs = zq[a]
-                    nc.tensor.matmul_mx(out=accs[t][:], lhsT=lw.bitcast(FP8X4), lhsT_scale=ls,
-                                        rhs=rw[:].bitcast(FP8X4), rhs_scale=rs[:],
-                                        start=(i == 0), stop=(i == len(passes) - 1))
-            return accs
+        def w4_piece(a, g):
+            w4_q[a, g] = quantize(round_weight(w4_raw[a, g][:], f"w4_b{a}{g}"), f"w4q{a}{g}")
 
-        def hand_out(g, accs):
+        h_rows = [h_scaled(b) for b in range(2)]
+        w4_piece(0, 0)
+        w4_piece(1, 0)
+        deal(w3d_s[:], w3_s[:].rearrange("p (g n) -> p g n", g=2), 8)
+        for g in range(2):
+            deal(w3d_w[g][:], w3_w[:, :, KP * g : KP * (g + 1)], 2)
+        damped(0)
+        zq[0] = quantize(z_rounded(0), "zq0")
+        for b in range(2):
+            hq[b] = quantize(weave(h_rows[b], f"h_b{b}"), f"hq{b}")
+        damped(1)
+        zq[1] = quantize(z_rounded(1), "zq1")
+        w4_piece(0, 1)
+        w4_piece(1, 1)
+
+        accs = [[bank(f"y{g}{t}") for t in range(PACK)] for g in range(2)]
+
+        def y_pass(g, which, a, start, stop):
+            for t in range(PACK):
+                cols = slice(P * t, P * (t + 1))
+                if which == 3:
+                    lw, ls = w3d_w[g][:, a, cols], w3d_s[4 * a : P, g, cols]
+                    rw, rs = hq[a]
+                else:
+                    lw, ls = w4_q[a, g][0][:, cols], w4_q[a, g][1][:, cols]
+                    rw, rs = zq[a]
+                nc.tensor.matmul_mx(out=accs[g][t][:], lhsT=lw.bitcast(FP8X4), lhsT_scale=ls,
+                                    rhs=rw[:].bitcast(FP8X4), rhs_scale=rs[:], start=start, stop=stop)
+
+        def hand_out(g):
             y = held([P, PACK, S], F32, f"y{g}")
             rows = out_0[KP * g : KP * (g + 1), :].rearrange("(p t) s -> p t s", t=PACK)
             for t in range(PACK):
-                nc.scalar.copy(out=y[:, t, :], in_=accs[t][:])
+                if (g, t) in ((0, 3),):
+                    nc.vector.tensor_copy(out=y[:, t, :], in_=accs[g][t][:])
+                else:
+                    nc.scalar.copy(out=y[:, t, :], in_=accs[g][t][:])
                 if t % 2 == 1:
                     nc.sync.dma_start(out=rows[:, t - 1 : t + 1, :], in_=y[:, t - 1 : t + 1, :])
-            yb = weave(y, f"y_b{g}")
+            vals = weave(y, f"y_b{g}")
             codes = held([P, S], U32, f"y_codes{g}")
-            nc.vector.quantize_mx(out=codes[:].bitcast(FP8X4), scales=y_scales[:, g, :], in_=yb[:])
+            nc.vector.quantize_mx(out=codes[:].bitcast(FP8X4), scales=y_scales[:, g, :], in_=vals[:])
             nc.sync.dma_start(out=out_1[g].rearrange("p m t -> p (m t)").bitcast(I32), in_=codes[:].bitcast(I32))
 
-        accs0 = project(0)
-        for a in range(2):
-            w4_b[a, 1] = round_weight(w4_raw[a, 1], f"w4_b{a}1")
-        deal(w3d_w[1][:], w3_w[1][:], 2)
-        for a in range(2):
-            w4_q[a, 1] = quantize(w4_b[a, 1], f"w4q{a}1")
-        accs1 = project(1)
-        hand_out(0, accs0)
-        hand_out(1, accs1)
+        y_pass(0, 3, 0, True, False)
+        y_pass(1, 3, 0, True, False)
+        y_pass(0, 4, 0, False, False)
+        y_pass(0, 3, 1, False, False)
+        y_pass(1, 3, 1, False, False)
+        y_pass(0, 4, 1, False, True)
+        y_pass(1, 4, 0, False, False)
+        y_pass(1, 4, 1, False, True)
+
+        hand_out(0)
+        hand_out(1)
         for q in range(4):
             nc.scalar.dma_start(
                 out=out_2[:, 4 * q : 4 * q + 4, :].rearrange("g r m -> r g m").bitcast(I32),

@@ -57,15 +57,15 @@ def tile_list_rupture_site_features_kernel(
                 out=dst.rearrange("p a (t c i) -> p a c t i", t=PACK, i=run),
                 in_=src.rearrange("p a (c i t) -> p a c t i", t=PACK, i=run))
 
-        def round_weight(raw, name):
-            vals = staged(name)
-            nc.scalar.copy(
+        def round_weight(raw, name, slot=None, copy=nc.scalar.copy):
+            vals = held([P, PACK * S], BF16, name, slot) if slot else staged(name)
+            copy(
                 out=vals[:].rearrange("p (u v m j) -> p m u j v", u=2, v=2, j=PACK),
                 in_=raw.rearrange("p j (m u v) -> p m u j v", u=2, v=2))
             return vals
 
-        def quantize(vals, name):
-            codes = held([P, S], U32, name + "_codes")
+        def quantize(vals, name, slot=None):
+            codes = held([P, S], U32, name + "_codes", slot)
             scales = held([P, S], U8, name + "_scales")
             nc.vector.quantize_mx(out=codes[:].bitcast(FP8X4), scales=scales[:], in_=vals[:])
             return codes, scales
@@ -107,7 +107,7 @@ def tile_list_rupture_site_features_kernel(
         load_scale_rows(nc.sync, tab_s, tab_scales)
         tab_w = [load_tab(0, "slot_e"), None]
 
-        v2_w = held([P, S], U16, "v2_w")
+        v2_w = held([P, S], U16, "v2_w", "slot_j")
         v2_s = held([P, S], U8, "v2_s")
         nc.vector.tensor_copy(v2_w[:], tab2_w[:].indirect(offs2_sb[:]))
         w1_s = held([P, 2, H], U8, "w1_s", "slot_b")
@@ -117,7 +117,7 @@ def tile_list_rupture_site_features_kernel(
         w3_s = held([P, N], U8, "w3_s", "slot_a")
         clear(w3_s[:])
 
-        damp = [held([P, PACK, S], F32, f"damp{b}") for b in range(2)]
+        damp, part = {}, {}
         sat = [held([P, PACK, S], F32, f"sat{b}") for b in range(2)]
         w2_q, w4_raw, w4_q, hq, zq, travel_sb = {}, {}, {}, {}, {}, {}
 
@@ -129,8 +129,9 @@ def tile_list_rupture_site_features_kernel(
             w4_raw[a, g] = held([P, PACK, S], F32, f"w4_raw{a}{g}", slot)
             load_rows(w4_raw[a, g][:], w4[KP * a : KP * (a + 1), KP * g : KP * (g + 1)])
 
-        def site(b):
+        def site(b, slot):
             codes, scales = w2_q[b]
+            damp[b] = held([P, PACK, S], F32, f"damp{b}", slot)
             for t in range(PACK):
                 cols = slice(P * t, P * (t + 1))
                 acc = bank(f"site{b}{t}")
@@ -142,17 +143,18 @@ def tile_list_rupture_site_features_kernel(
             for t in range(PACK):
                 cols = slice(P * t, P * (t + 1))
                 acc = bank(f"slip{b}{t}")
-                for a in range(2):
+                for a in (1, 0):
                     nc.tensor.matmul_mx(out=acc[:], lhsT=w1d_w[:, 2 * a + b, cols].bitcast(FP4X4),
-                                        lhsT_scale=w1d_s[:, 2 * a + b, cols],
+                                        lhsT_scale=w1d_s[b][:, a, cols],
                                         rhs=v_w[a][:].bitcast(FP8X4), rhs_scale=v_s[a][:],
-                                        start=(a == 0), stop=(a == 1))
+                                        start=(a == 1), stop=(a == 0))
                 nc.scalar.activation(out=sat[b][:, t, :], in_=acc[:], func=ACT.Tanh)
 
-        def damped(b):
+        def damped(b, slot):
+            part[b] = held([P, PACK, S], F32, f"part{b}", slot)
             for t in range(PACK):
                 nc.vector.scalar_tensor_tensor(
-                    out=damp[b][:, t, :], in0=sat[b][:, t, :], scalar=gain_sb[:, b, t : t + 1],
+                    out=part[b][:, t, :], in0=sat[b][:, t, :], scalar=gain_sb[:, b, t : t + 1],
                     in1=damp[b][:, t, :], op0=ALU.mult, op1=ALU.mult)
 
         def h_scaled(b):
@@ -162,22 +164,20 @@ def tile_list_rupture_site_features_kernel(
                                      scale=gain_sb[:, b, t : t + 1])
             return rows
 
-        def weave(rows, name):
-            vals = staged(name)
+        def weave(rows, name, slot=None):
+            vals = held([P, PACK * S], BF16, name, slot) if slot else staged(name)
             nc.vector.tensor_copy(out=woven(vals), in_=by_pairs(rows[:]))
             return vals
 
-        def z_rounded(b):
-            vals = staged(f"z_b{b}")
-            nc.vector.tensor_tensor(out=woven(vals), in0=by_pairs(damp[b][:]), in1=by_pairs(travel_sb[b][:]), op=ALU.add)
+        def z_rounded(b, slot=None):
+            vals = held([P, PACK * S], BF16, f"z_b{b}", slot) if slot else staged(f"z_b{b}")
+            nc.vector.tensor_tensor(out=woven(vals), in0=by_pairs(part[b][:]), in1=by_pairs(travel_sb[b][:]), op=ALU.add)
             return vals
 
-        w2_q[0] = quantize(round_weight(w2_raw[0][:], "w2_b0"), "w2q0")
-        site(0)
-        w2_q[1] = quantize(round_weight(w2_raw[1][:], "w2_b1"), "w2q1")
-        site(1)
+        w2_q[0] = quantize(round_weight(w2_raw[0][:], "w2_b0", "slot_h"), "w2q0", "slot_i")
+        w2_b1 = round_weight(w2_raw[1][:], "w2_b1")
+        site(0, "slot_g")
         w1d_w = held([P, 4, KP], U16, "w1d_w")
-        w1d_s = held([P, 4, KP], U8, "w1d_s")
         deal(w1d_w[:], w1_w[:].rearrange("p a (b n) -> p (a b) n", b=2), 4)
         tab_w[1] = load_tab(1, "slot_d")
         for q in range(4):
@@ -185,41 +185,49 @@ def tile_list_rupture_site_features_kernel(
                               in_=w3_scales[:, 4 * q : 4 * q + 4, :].bitcast(I32))
         w3_w = held([P, 2, N], I32, "w3_w", "slot_f")
         nc.sync.dma_start(out=w3_w[:], in_=w3_words.rearrange("a p n t -> p a (n t)").bitcast(I32))
+        load_travel(0, "slot_h")
+        load_travel(1, "slot_i")
         v_s = [held([P, S], U8, f"v_s{a}") for a in range(2)]
-        v_w = [held([P, S], U32, "v_w0", "slot_h"), held([P, S], U32, "v_w1")]
+        v_w = [held([P, S], U32, f"v_w{a}") for a in range(2)]
         for a in range(2):
             nc.vector.tensor_copy(v_s[a][:], tab_s[:, a, :].indirect(offs_sb[:]))
-        load_travel(0, "slot_c")
-        load_w4(0, 0, "slot_g")
-        deal(w1d_s[:], w1_s[:].rearrange("p a (b n) -> p (a b) n", b=2), 8)
+        w2_q[1] = quantize(w2_b1, "w2q1", "slot_c")
+        site(1, None)
+        load_w4(0, 0, "slot_j")
+        w1d_s = [held([P, 2, KP], U8, "w1d_s0"), None]
+        deal(w1d_s[0][:], w1_s[:, :, 0:KP], 8)
         for a in range(2):
             nc.vector.tensor_copy(v_w[a][:], tab_w[a][:].bitcast(U32).indirect(offs_sb[:]))
+        w1d_s[1] = held([P, 2, KP], U8, "w1d_s1", "slot_d")
+        deal(w1d_s[1][:], w1_s[:, :, KP : 2 * KP], 8)
         load_w4(1, 0, "slot_e")
-        load_travel(1, "slot_b")
-        load_w4(0, 1, "slot_d")
+        load_w4(0, 1, "slot_b")
         slip(0)
+        h_rows = [h_scaled(0), None]
         slip(1)
-        load_w4(1, 1, "slot_h")
+        h_rows[1] = h_scaled(1)
+        load_w4(1, 1, "slot_d")
 
         w3d_s = held([P, 2, KP], U8, "w3d_s")
         w3d_w = [held([P, 2, KP], I32, f"w3d_w{g}") for g in range(2)]
         y_scales = held([P, 2, S], U8, "y_scales")
 
-        def w4_piece(a, g):
-            w4_q[a, g] = quantize(round_weight(w4_raw[a, g][:], f"w4_b{a}{g}"), f"w4q{a}{g}")
+        def w4_piece(a, g, slot=None, copy=nc.scalar.copy):
+            w4_q[a, g] = quantize(round_weight(w4_raw[a, g][:], f"w4_b{a}{g}", slot, copy), f"w4q{a}{g}")
 
-        h_rows = [h_scaled(b) for b in range(2)]
-        w4_piece(0, 0)
-        w4_piece(1, 0)
         deal(w3d_s[:], w3_s[:].rearrange("p (g n) -> p g n", g=2), 8)
         for g in range(2):
             deal(w3d_w[g][:], w3_w[:, :, KP * g : KP * (g + 1)], 2)
-        damped(0)
-        zq[0] = quantize(z_rounded(0), "zq0")
-        for b in range(2):
-            hq[b] = quantize(weave(h_rows[b], f"h_b{b}"), f"hq{b}")
-        damped(1)
-        zq[1] = quantize(z_rounded(1), "zq1")
+        damped(0, "slot_f")
+        hq[0] = quantize(weave(h_rows[0], "h_b0"), "hq0")
+        damped(1, "slot_g")
+        z_b0 = z_rounded(0)
+        hq[1] = quantize(weave(h_rows[1], "h_b1"), "hq1")
+        zq[0] = quantize(z_b0, "zq0")
+        w4_piece(0, 0, "slot_k")
+        z_b1 = z_rounded(1, "slot_k")
+        w4_piece(1, 0)
+        zq[1] = quantize(z_b1, "zq1")
         w4_piece(0, 1)
         w4_piece(1, 1)
 
@@ -238,10 +246,10 @@ def tile_list_rupture_site_features_kernel(
                                     rhs=rw[:].bitcast(FP8X4), rhs_scale=rs[:], start=start, stop=stop)
 
         def hand_out(g):
-            y = held([P, PACK, S], F32, f"y{g}")
+            y = held([P, PACK, S], F32, f"y{g}", "slot_d" if g == 0 else None)
             rows = out_0[KP * g : KP * (g + 1), :].rearrange("(p t) s -> p t s", t=PACK)
             for t in range(PACK):
-                if (g, t) in ((0, 3),):
+                if (g, t) in ((0, 3), (1, 3)):
                     nc.vector.tensor_copy(out=y[:, t, :], in_=accs[g][t][:])
                 else:
                     nc.scalar.copy(out=y[:, t, :], in_=accs[g][t][:])
@@ -252,14 +260,8 @@ def tile_list_rupture_site_features_kernel(
             nc.vector.quantize_mx(out=codes[:].bitcast(FP8X4), scales=y_scales[:, g, :], in_=vals[:])
             nc.sync.dma_start(out=out_1[g].rearrange("p m t -> p (m t)").bitcast(I32), in_=codes[:].bitcast(I32))
 
-        y_pass(0, 3, 0, True, False)
-        y_pass(1, 3, 0, True, False)
-        y_pass(0, 4, 0, False, False)
-        y_pass(0, 3, 1, False, False)
-        y_pass(1, 3, 1, False, False)
-        y_pass(0, 4, 1, False, True)
-        y_pass(1, 4, 0, False, False)
-        y_pass(1, 4, 1, False, True)
+        for g, which, a in ((0, 3, 0), (1, 3, 0), (0, 3, 1), (1, 3, 1), (0, 4, 0), (0, 4, 1), (1, 4, 0), (1, 4, 1)):
+            y_pass(g, which, a, (which, a) == (3, 0), (which, a) == (4, 1))
 
         hand_out(0)
         hand_out(1)

@@ -60,8 +60,8 @@ def tile_list_rupture_site_features_kernel(
         def round_weight(raw, name, slot=None, copy=nc.scalar.copy):
             vals = held([P, PACK * S], BF16, name, slot) if slot else staged(name)
             copy(
-                out=vals[:].rearrange("p (u v m j) -> p m u j v", u=2, v=2, j=PACK),
-                in_=raw.rearrange("p j (m u v) -> p m u j v", u=2, v=2))
+                out=vals[:].rearrange("p (u v m j) -> p u m j v", u=2, v=2, j=PACK),
+                in_=raw.rearrange("p j (m u v) -> p u m j v", u=2, v=2))
             return vals
 
         def quantize(vals, name, slot=None):
@@ -70,15 +70,15 @@ def tile_list_rupture_site_features_kernel(
             nc.vector.quantize_mx(out=codes[:].bitcast(FP8X4), scales=scales[:], in_=vals[:])
             return codes, scales
 
-        def woven(vals):
-            return vals[:].rearrange("p (c i t) -> p c t i", i=2, t=PACK)
+        def woven(vals, run=2):
+            return vals[:].rearrange("p (c i t) -> p c t i", i=run, t=PACK)
 
-        def by_pairs(rows):
-            return rows.rearrange("p t (c i) -> p c t i", i=2)
+        def by_pairs(rows, run=2):
+            return rows.rearrange("p t (c i) -> p c t i", i=run)
 
         offs_sb = lists.tile([P, S // 16], U16, name="offs_sb")
         offs2_sb = lists.tile([P, S // 16], U16, name="offs2_sb")
-        tab2_s = held([P, 1, T2], U8, "tab2_s", "slot_a")
+        tab2_s = held([P, 1, T2], U8, "tab2_s", "slot_i")
         tab2_w = held([P, T2], U16, "tab2_w", "slot_b")
         tab_s = held([P, 2, T], U8, "tab_s", "slot_c")
         w1_w = held([P, 2, H], U16, "w1_w", "slot_d")
@@ -114,8 +114,6 @@ def tile_list_rupture_site_features_kernel(
         clear(w1_s[:].rearrange("p a n -> p (a n)"))
         load_scale_rows(nc.sync, w1_s, w1_scales)
         nc.vector.tensor_copy(v2_s[:], tab2_s[:, 0, :].indirect(offs2_sb[:]))
-        w3_s = held([P, N], U8, "w3_s", "slot_a")
-        clear(w3_s[:])
 
         damp, part = {}, {}
         sat = [held([P, PACK, S], F32, f"sat{b}") for b in range(2)]
@@ -125,9 +123,11 @@ def tile_list_rupture_site_features_kernel(
             travel_sb[b] = held([P, PACK, S], F32, f"travel{b}", slot)
             load_rows(travel_sb[b][:], travel[KP * b : KP * (b + 1), :])
 
-        def load_w4(a, g, slot):
-            w4_raw[a, g] = held([P, PACK, S], F32, f"w4_raw{a}{g}", slot)
-            load_rows(w4_raw[a, g][:], w4[KP * a : KP * (a + 1), KP * g : KP * (g + 1)])
+        def load_w4(a, g, slot, lead=0):
+            rows = held([P, lead + PACK, S], F32, f"w4_raw{a}{g}", slot)
+            w4_raw[a, g] = rows[:, lead : lead + PACK, :]
+            load_rows(w4_raw[a, g], w4[KP * a : KP * (a + 1), KP * g : KP * (g + 1)])
+            return rows
 
         def site(b, slot):
             codes, scales = w2_q[b]
@@ -143,11 +143,12 @@ def tile_list_rupture_site_features_kernel(
             for t in range(PACK):
                 cols = slice(P * t, P * (t + 1))
                 acc = bank(f"slip{b}{t}")
-                for a in (1, 0):
+                order = (0, 1) if b == 0 else (1, 0)
+                for a in order:
                     nc.tensor.matmul_mx(out=acc[:], lhsT=w1d_w[:, 2 * a + b, cols].bitcast(FP4X4),
                                         lhsT_scale=w1d_s[b][:, a, cols],
                                         rhs=v_w[a][:].bitcast(FP8X4), rhs_scale=v_s[a][:],
-                                        start=(a == 1), stop=(a == 0))
+                                        start=(a == order[0]), stop=(a == order[1]))
                 nc.scalar.activation(out=sat[b][:, t, :], in_=acc[:], func=ACT.Tanh)
 
         def damped(b, slot):
@@ -164,9 +165,9 @@ def tile_list_rupture_site_features_kernel(
                                      scale=gain_sb[:, b, t : t + 1])
             return rows
 
-        def weave(rows, name, slot=None):
+        def weave(rows, name, run, slot=None):
             vals = held([P, PACK * S], BF16, name, slot) if slot else staged(name)
-            nc.vector.tensor_copy(out=woven(vals), in_=by_pairs(rows[:]))
+            nc.vector.tensor_copy(out=woven(vals, run), in_=by_pairs(rows, run))
             return vals
 
         def z_rounded(b, slot=None):
@@ -174,8 +175,11 @@ def tile_list_rupture_site_features_kernel(
             nc.vector.tensor_tensor(out=woven(vals), in0=by_pairs(part[b][:]), in1=by_pairs(travel_sb[b][:]), op=ALU.add)
             return vals
 
-        w2_q[0] = quantize(round_weight(w2_raw[0][:], "w2_b0", "slot_h"), "w2q0", "slot_i")
-        w2_b1 = round_weight(w2_raw[1][:], "w2_b1")
+        w2_b0 = round_weight(w2_raw[0][:], "w2_b0", "slot_h")
+        w2_q[0] = quantize(w2_b0, "w2q0", "slot_i")
+        w3_s = held([P, N], U8, "w3_s", "slot_h")
+        clear(w3_s[:])
+        w2_b1 = round_weight(w2_raw[1][:], "w2_b1", "slot_a")
         site(0, "slot_g")
         w1d_w = held([P, 4, KP], U16, "w1d_w")
         deal(w1d_w[:], w1_w[:].rearrange("p a (b n) -> p (a b) n", b=2), 4)
@@ -185,44 +189,44 @@ def tile_list_rupture_site_features_kernel(
                               in_=w3_scales[:, 4 * q : 4 * q + 4, :].bitcast(I32))
         w3_w = held([P, 2, N], I32, "w3_w", "slot_f")
         nc.sync.dma_start(out=w3_w[:], in_=w3_words.rearrange("a p n t -> p a (n t)").bitcast(I32))
-        load_travel(0, "slot_h")
-        load_travel(1, "slot_i")
+        load_travel(0, "slot_i")
         v_s = [held([P, S], U8, f"v_s{a}") for a in range(2)]
         v_w = [held([P, S], U32, f"v_w{a}") for a in range(2)]
         for a in range(2):
             nc.vector.tensor_copy(v_s[a][:], tab_s[:, a, :].indirect(offs_sb[:]))
         w2_q[1] = quantize(w2_b1, "w2q1", "slot_c")
+        load_travel(1, "slot_a")
         site(1, None)
-        load_w4(0, 0, "slot_j")
+        load_w4(1, 0, "slot_j")
         w1d_s = [held([P, 2, KP], U8, "w1d_s0"), None]
         deal(w1d_s[0][:], w1_s[:, :, 0:KP], 8)
         for a in range(2):
             nc.vector.tensor_copy(v_w[a][:], tab_w[a][:].bitcast(U32).indirect(offs_sb[:]))
         w1d_s[1] = held([P, 2, KP], U8, "w1d_s1", "slot_d")
         deal(w1d_s[1][:], w1_s[:, :, KP : 2 * KP], 8)
-        load_w4(1, 0, "slot_e")
+        load_w4(0, 0, "slot_e")
         load_w4(0, 1, "slot_b")
         slip(0)
         h_rows = [h_scaled(0), None]
         slip(1)
         h_rows[1] = h_scaled(1)
-        load_w4(1, 1, "slot_d")
+        shared = load_w4(1, 1, "slot_d", 0)
 
         w3d_s = held([P, 2, KP], U8, "w3d_s")
         w3d_w = [held([P, 2, KP], I32, f"w3d_w{g}") for g in range(2)]
         y_scales = held([P, 2, S], U8, "y_scales")
 
         def w4_piece(a, g, slot=None, copy=nc.scalar.copy):
-            w4_q[a, g] = quantize(round_weight(w4_raw[a, g][:], f"w4_b{a}{g}", slot, copy), f"w4q{a}{g}")
+            w4_q[a, g] = quantize(round_weight(w4_raw[a, g], f"w4_b{a}{g}", slot, copy), f"w4q{a}{g}")
 
         deal(w3d_s[:], w3_s[:].rearrange("p (g n) -> p g n", g=2), 8)
         for g in range(2):
             deal(w3d_w[g][:], w3_w[:, :, KP * g : KP * (g + 1)], 2)
         damped(0, "slot_f")
-        hq[0] = quantize(weave(h_rows[0], "h_b0"), "hq0")
+        hq[0] = quantize(weave(h_rows[0][:], "h_b0", 4), "hq0")
         damped(1, "slot_g")
         z_b0 = z_rounded(0)
-        hq[1] = quantize(weave(h_rows[1], "h_b1"), "hq1")
+        hq[1] = quantize(weave(h_rows[1][:], "h_b1", 4), "hq1")
         zq[0] = quantize(z_b0, "zq0")
         w4_piece(0, 0, "slot_k")
         z_b1 = z_rounded(1, "slot_k")
@@ -246,7 +250,7 @@ def tile_list_rupture_site_features_kernel(
                                     rhs=rw[:].bitcast(FP8X4), rhs_scale=rs[:], start=start, stop=stop)
 
         def hand_out(g):
-            y = held([P, PACK, S], F32, f"y{g}", "slot_d" if g == 0 else None)
+            y = shared[:, 0:PACK, :] if g == 0 else held([P, PACK, S], F32, "y1")[:]
             rows = out_0[KP * g : KP * (g + 1), :].rearrange("(p t) s -> p t s", t=PACK)
             for t in range(PACK):
                 if (g, t) in ((0, 3), (1, 3)):
@@ -255,7 +259,7 @@ def tile_list_rupture_site_features_kernel(
                     nc.scalar.copy(out=y[:, t, :], in_=accs[g][t][:])
                 if t % 2 == 1:
                     nc.sync.dma_start(out=rows[:, t - 1 : t + 1, :], in_=y[:, t - 1 : t + 1, :])
-            vals = weave(y, f"y_b{g}")
+            vals = weave(y, f"y_b{g}", 2)
             codes = held([P, S], U32, f"y_codes{g}")
             nc.vector.quantize_mx(out=codes[:].bitcast(FP8X4), scales=y_scales[:, g, :], in_=vals[:])
             nc.sync.dma_start(out=out_1[g].rearrange("p m t -> p (m t)").bitcast(I32), in_=codes[:].bitcast(I32))

@@ -45,9 +45,9 @@ def tile_list_rupture_site_features_kernel(
             nc.vector.memset(plane.bitcast(I32), 0)
 
         def load_scale_rows(queue, plane, scales):
-            for q in range(4):
-                queue.dma_start(out=plane[32 * q : 32 * q + 4].bitcast(I32),
-                                in_=scales[:, 4 * q : 4 * q + 4, :].rearrange("a r n -> r a n").bitcast(I32))
+            for r in range(4):
+                queue.dma_start(out=plane[r:P:32].bitcast(I32),
+                                in_=scales[:, r:16:4, :].rearrange("a q n -> q a n").bitcast(I32))
 
         def load_rows(dst, src):
             nc.sync.dma_start(out=dst, in_=src.rearrange("(p j) c -> p j c", j=PACK))
@@ -269,7 +269,7 @@ def tile_list_rupture_site_features_kernel(
 
         hand_out(0)
         hand_out(1)
-        for q in range(4):
+        for r in range(4):
             nc.scalar.dma_start(
-                out=out_2[:, 4 * q : 4 * q + 4, :].rearrange("g r m -> r g m").bitcast(I32),
-                in_=y_scales[32 * q : 32 * q + 4, :, :].bitcast(I32))
+                out=out_2[:, r:16:4, :].rearrange("g q m -> q g m").bitcast(I32),
+                in_=y_scales[r:P:32].bitcast(I32))

@@ -29,39 +29,42 @@ def tile_list_rupture_site_features_kernel(
     with ExitStack() as ctx:
         lists = ctx.enter_context(tc.tile_pool(name="lists", bufs=1))
         keep = ctx.enter_context(tc.tile_pool(name="keep", bufs=1))
-        stage = ctx.enter_context(tc.tile_pool(name="stage", bufs=8))
-        psum = ctx.enter_context(tc.psum_pool(name="psum", bufs=8))
+        psum = ctx.enter_context(tc.psum_pool(name="psum", bufs=1))
 
         def held(shape, dtype, name, slot=None):
             return keep.tile(shape, dtype, name=name, tag=slot or name, align_bytes=64)
 
-        def staged(name):
-            return stage.tile([P, PACK * S], BF16, name=name, tag="staged", align_bytes=64)
+        def bank(name, number):
+            return psum.tile([P, S], F32, name=name, tag=f"bank{number}")
 
-        def bank(name):
-            return psum.tile([P, S], F32, name=name, tag="bank")
+        def clear(engine, plane):
+            engine.memset(plane[:].rearrange("p a n -> p (a n)").bitcast(I32), 0)
 
-        def clear(plane):
-            nc.vector.memset(plane.bitcast(I32), 0)
-
-        def load_scale_rows(queue, plane, scales):
+        def load_scale_rows(queue, plane, scales, first=0):
             for r in range(4):
-                queue.dma_start(out=plane[r:P:32].bitcast(I32),
+                queue.dma_start(out=plane[first + r : P : 32].bitcast(I32),
                                 in_=scales[:, r:16:4, :].rearrange("a q n -> q a n").bitcast(I32))
 
-        def load_rows(dst, src):
-            nc.sync.dma_start(out=dst, in_=src.rearrange("(p j) c -> p j c", j=PACK))
+        def load_rows(name, src, slot=None):
+            rows = held([P, PACK, S], F32, name, slot)
+            nc.sync.dma_start(out=rows[:], in_=src.rearrange("(p j) c -> p j c", j=PACK))
+            return rows
 
-        def deal(dst, src, run):
+        def deal(dst, src):
             nc.vector.tensor_copy(
-                out=dst.rearrange("p a (t c i) -> p a c t i", t=PACK, i=run),
-                in_=src.rearrange("p a (c i t) -> p a c t i", t=PACK, i=run))
+                out=dst.rearrange("p a (t m) -> p a t m", t=PACK),
+                in_=src.rearrange("p a (m t) -> p a t m", t=PACK))
 
-        def round_weight(raw, name, slot=None, copy=nc.scalar.copy):
-            vals = held([P, PACK * S], BF16, name, slot) if slot else staged(name)
+        def deal_by_pairs(dst, src):
+            nc.vector.tensor_copy(
+                out=dst.rearrange("p a (t c i) -> p a c t i", t=PACK, i=2),
+                in_=src.rearrange("p a (c i t) -> p a c t i", t=PACK, i=2))
+
+        def round_weight(raw, name, slot, copy):
+            vals = held([P, PACK * S], BF16, name, slot)
             copy(
                 out=vals[:].rearrange("p (u v m j) -> p u m j v", u=2, v=2, j=PACK),
-                in_=raw.rearrange("p j (m u v) -> p u m j v", u=2, v=2))
+                in_=raw[:].rearrange("p j (m u v) -> p u m j v", u=2, v=2))
             return vals
 
         def quantize(vals, name, slot=None):
@@ -70,205 +73,197 @@ def tile_list_rupture_site_features_kernel(
             nc.vector.quantize_mx(out=codes[:].bitcast(FP8X4), scales=scales[:], in_=vals[:])
             return codes, scales
 
-        def woven(vals, run=2):
+        def woven(vals, run):
             return vals[:].rearrange("p (c i t) -> p c t i", i=run, t=PACK)
 
-        def by_pairs(rows, run=2):
-            return rows.rearrange("p t (c i) -> p c t i", i=run)
+        def by_runs(rows, run):
+            return rows[:].rearrange("p t (c i) -> p c t i", i=run)
+
+        def weave(rows, name, run, slot, copy):
+            vals = held([P, PACK * S], BF16, name, slot)
+            copy(out=woven(vals, run), in_=by_runs(rows, run))
+            return vals
 
         offs_sb = lists.tile([P, S // 16], U16, name="offs_sb")
         offs2_sb = lists.tile([P, S // 16], U16, name="offs2_sb")
-        tab2_s = held([P, 1, T2], U8, "tab2_s", "slot_i")
-        tab2_w = held([P, T2], U16, "tab2_w", "slot_b")
-        tab_s = held([P, 2, T], U8, "tab_s", "slot_c")
-        w1_w = held([P, 2, H], U16, "w1_w", "slot_d")
-        warm = held([P, 8], F32, "warm", "slot_e")
-        w2_raw = [held([P, PACK, S], F32, "w2_raw0", "slot_f"), held([P, PACK, S], F32, "w2_raw1", "slot_g")]
+        tab_s = held([P, 2, T], U8, "tab_s")
+        tab2_s = held([P, 1, T2], U8, "tab2_s")
+        w1_s = held([P, 2, H], U8, "w1_s")
+        w3_s = held([P, 1, N], U8, "w3_s")
+        w1_w = held([P, 2, H], U16, "w1_w")
+        tab2_w = held([P, T2], U16, "tab2_w")
         gain_sb = held([P, 2, PACK], F32, "gain_sb")
+        warm = held([P, 8], F32, "warm")
 
-        clear(tab2_s[:, 0, :])
-        clear(tab_s[:].rearrange("p a n -> p (a n)"))
+        clear(nc.vector, tab2_s)
+        clear(nc.vector, tab_s)
+        clear(nc.vector, w1_s)
+        clear(nc.vector, w3_s)
         nc.vector.memset(warm[:], 0.0)
         nc.scalar.activation(out=warm[:], in_=warm[:], func=ACT.Sigmoid)
 
-        def load_tab(a, slot):
-            words = held([P, T], I32, f"tab_w{a}", slot)
+        def load_tab(a):
+            words = held([P, T], I32, f"tab_w{a}")
             nc.sync.dma_start(out=words[:], in_=tab_words[a].rearrange("p n t -> p (n t)").bitcast(I32))
             return words
 
+        def load_w3(g):
+            words = held([P, 2, KP], I32, f"w3_w{g}")
+            nc.sync.dma_start(
+                out=words[:],
+                in_=w3_words[:, :, KP * g : KP * (g + 1), :].rearrange("a p n t -> p a (n t)").bitcast(I32))
+            return words
+
+        def load_w4(a, g):
+            return load_rows(f"w4_raw{a}{g}", w4[KP * a : KP * (a + 1), KP * g : KP * (g + 1)])
+
+        w2_raw, travel_sb, w3_w, w4_raw = {}, {}, {}, {}
         nc.sync.dma_start(offs2_sb[:], offs2)
         nc.sync.dma_start(out=tab2_w[:].bitcast(I32), in_=tab2_words[0].bitcast(I32))
         nc.sync.dma_start(out=w1_w[:].bitcast(I32), in_=w1_words.rearrange("a p n -> p a n").bitcast(I32))
         nc.sync.dma_start(offs_sb[:], offs)
-        load_rows(w2_raw[0][:], w2[:, 0:KP])
-        nc.sync.dma_start(out=gain_sb[:], in_=gain.rearrange("(b p t) -> p b t", b=2, t=PACK))
         load_scale_rows(nc.sync, tab2_s, tab2_scales)
-        load_rows(w2_raw[1][:], w2[:, KP : 2 * KP])
+        w2_raw[0] = load_rows("w2_raw0", w2[:, 0:KP])
         load_scale_rows(nc.sync, tab_s, tab_scales)
-        tab_w = [load_tab(0, "slot_e"), None]
-
-        v2_w = held([P, S], U16, "v2_w", "slot_j")
-        v2_s = held([P, S], U8, "v2_s")
-        nc.vector.tensor_copy(v2_w[:], tab2_w[:].indirect(offs2_sb[:]))
-        w1_s = held([P, 2, H], U8, "w1_s", "slot_b")
-        clear(w1_s[:].rearrange("p a n -> p (a n)"))
+        nc.sync.dma_start(out=gain_sb[:], in_=gain.rearrange("(b p t) -> p b t", b=2, t=PACK))
+        tab_w = [load_tab(0), None]
         load_scale_rows(nc.sync, w1_s, w1_scales)
+        tab_w[1] = load_tab(1)
+        w2_raw[1] = load_rows("w2_raw1", w2[:, KP : 2 * KP])
+        travel_sb[0] = load_rows("travel0", travel[0:KP, :])
+        for q in range(4):
+            nc.sync.dma_start(out=w3_s[32 * q : 32 * q + 8, 0, :].bitcast(I32),
+                              in_=w3_scales[:, 4 * q : 4 * q + 4, :].bitcast(I32))
+        w4_raw[0, 0] = load_w4(0, 0)
+        travel_sb[1] = load_rows("travel1", travel[KP : 2 * KP, :])
+        w3_w[0] = load_w3(0)
+        w4_raw[1, 0] = load_w4(1, 0)
+        w3_w[1] = load_w3(1)
+        w4_raw[0, 1] = load_w4(0, 1)
+        w4_raw[1, 1] = load_w4(1, 1)
+
+        v2_w = held([P, S], U16, "v2_w")
+        v2_s = held([P, S], U8, "v2_s")
+        w1d_w = held([P, 4, KP], U16, "w1d_w")
+        v_s = [held([P, S], U8, f"v_s{a}") for a in range(2)]
+        v_w = [held([P, S], U32, f"v_w{a}") for a in range(2)]
+        w1d_s = [held([P, 2, KP], U8, "w1d_s0"), None]
+        nc.vector.tensor_copy(v2_w[:], tab2_w[:].indirect(offs2_sb[:]))
         nc.vector.tensor_copy(v2_s[:], tab2_s[:, 0, :].indirect(offs2_sb[:]))
+        deal(w1d_w[:], w1_w[:].rearrange("p a (b n) -> p (a b) n", b=2))
+        for a in range(2):
+            nc.vector.tensor_copy(v_s[a][:], tab_s[:, a, :].indirect(offs_sb[:]))
+        nc.vector.tensor_copy(v_w[0][:], tab_w[0][:].bitcast(U32).indirect(offs_sb[:]))
+        deal(w1d_s[0][:], w1_s[:, :, 0:KP])
+        nc.vector.tensor_copy(v_w[1][:], tab_w[1][:].bitcast(U32).indirect(offs_sb[:]))
+        w1d_s[1] = held([P, 2, KP], U8, "w1d_s1", "tab_w1")
+        deal(w1d_s[1][:], w1_s[:, :, KP : 2 * KP])
 
-        damp, part = {}, {}
-        sat = [held([P, PACK, S], F32, f"sat{b}") for b in range(2)]
-        w2_q, w4_raw, w4_q, hq, zq, travel_sb = {}, {}, {}, {}, {}, {}
+        sat, damp, part, h_rows, w2_q, w4_q, hq, zq, w3d_w = {}, {}, {}, {}, {}, {}, {}, {}, {}
 
-        def load_travel(b, slot):
-            travel_sb[b] = held([P, PACK, S], F32, f"travel{b}", slot)
-            load_rows(travel_sb[b][:], travel[KP * b : KP * (b + 1), :])
+        def slip(b):
+            sat[b] = held([P, PACK, S], F32, f"sat{b}")
+            accs = [bank(f"slip{b}{t}", PACK * (1 - b) + t) for t in range(PACK)]
+            for a in range(2):
+                for t in range(PACK):
+                    cols = slice(P * t, P * (t + 1))
+                    nc.tensor.matmul_mx(out=accs[t][:], lhsT=w1d_w[:, 2 * a + b, cols].bitcast(FP4X4),
+                                        lhsT_scale=w1d_s[b][:, a, cols],
+                                        rhs=v_w[a][:].bitcast(FP8X4), rhs_scale=v_s[a][:],
+                                        start=(a == 0), stop=(a == 1))
+            for t in range(PACK):
+                nc.scalar.activation(out=sat[b][:, t, :], in_=accs[t][:], func=ACT.Tanh)
 
-        def load_w4(a, g, slot, lead=0):
-            rows = held([P, lead + PACK, S], F32, f"w4_raw{a}{g}", slot)
-            w4_raw[a, g] = rows[:, lead : lead + PACK, :]
-            load_rows(w4_raw[a, g], w4[KP * a : KP * (a + 1), KP * g : KP * (g + 1)])
-            return rows
-
-        def site(b, slot):
+        def site(b):
             codes, scales = w2_q[b]
-            damp[b] = held([P, PACK, S], F32, f"damp{b}", slot)
+            damp[b] = held([P, PACK, S], F32, f"damp{b}")
             for t in range(PACK):
                 cols = slice(P * t, P * (t + 1))
-                acc = bank(f"site{b}{t}")
+                acc = bank(f"site{b}{t}", PACK * b + t)
                 nc.tensor.matmul_mx(out=acc[:], lhsT=codes[:, cols].bitcast(FP8X4), lhsT_scale=scales[:, cols],
                                     rhs=v2_w[:].bitcast(FP4X4), rhs_scale=v2_s[:], start=True, stop=True)
                 nc.scalar.activation(out=damp[b][:, t, :], in_=acc[:], func=ACT.Sigmoid, scale=-1.0)
 
-        def slip(b):
+        def h_scaled(b, slot):
+            h_rows[b] = held([P, PACK, S], BF16, f"h_rows{b}", slot)
             for t in range(PACK):
-                cols = slice(P * t, P * (t + 1))
-                acc = bank(f"slip{b}{t}")
-                order = (0, 1) if b == 0 else (1, 0)
-                for a in order:
-                    nc.tensor.matmul_mx(out=acc[:], lhsT=w1d_w[:, 2 * a + b, cols].bitcast(FP4X4),
-                                        lhsT_scale=w1d_s[b][:, a, cols],
-                                        rhs=v_w[a][:].bitcast(FP8X4), rhs_scale=v_s[a][:],
-                                        start=(a == order[0]), stop=(a == order[1]))
-                nc.scalar.activation(out=sat[b][:, t, :], in_=acc[:], func=ACT.Tanh)
+                nc.scalar.activation(out=h_rows[b][:, t, :], in_=sat[b][:, t, :], func=ACT.Copy,
+                                     scale=gain_sb[:, b, t : t + 1])
 
-        def damped(b, slot):
-            part[b] = held([P, PACK, S], F32, f"part{b}", slot)
+        def damped(b):
+            part[b] = held([P, PACK, S], F32, f"part{b}", f"w2_raw{b}")
             for t in range(PACK):
                 nc.vector.scalar_tensor_tensor(
                     out=part[b][:, t, :], in0=sat[b][:, t, :], scalar=gain_sb[:, b, t : t + 1],
                     in1=damp[b][:, t, :], op0=ALU.mult, op1=ALU.mult)
 
-        def h_scaled(b):
-            rows = stage.tile([P, PACK, S], BF16, name=f"h_rows{b}", tag="staged", align_bytes=64)
-            for t in range(PACK):
-                nc.scalar.activation(out=rows[:, t, :], in_=sat[b][:, t, :], func=ACT.Copy,
-                                     scale=gain_sb[:, b, t : t + 1])
-            return rows
-
-        def weave(rows, name, run, slot=None):
-            vals = held([P, PACK * S], BF16, name, slot) if slot else staged(name)
-            nc.vector.tensor_copy(out=woven(vals, run), in_=by_pairs(rows, run))
+        def z_rounded(b):
+            vals = held([P, PACK * S], BF16, f"z_b{b}")
+            nc.vector.tensor_tensor(out=woven(vals, 2), in0=by_runs(part[b], 2), in1=by_runs(travel_sb[b], 2),
+                                    op=ALU.add)
             return vals
 
-        def z_rounded(b, slot=None):
-            vals = held([P, PACK * S], BF16, f"z_b{b}", slot) if slot else staged(f"z_b{b}")
-            nc.vector.tensor_tensor(out=woven(vals), in0=by_pairs(part[b][:]), in1=by_pairs(travel_sb[b][:]), op=ALU.add)
-            return vals
+        def deal_w3(g):
+            w3d_w[g] = held([P, 2, KP], I32, f"w3d_w{g}")
+            deal_by_pairs(w3d_w[g][:], w3_w[g][:])
 
-        w2_b0 = round_weight(w2_raw[0][:], "w2_b0", "slot_h")
-        w2_q[0] = quantize(w2_b0, "w2q0", "slot_i")
-        w3_s = held([P, N], U8, "w3_s", "slot_h")
-        clear(w3_s[:])
-        w2_b1 = round_weight(w2_raw[1][:], "w2_b1", "slot_a")
-        site(0, "slot_g")
-        w1d_w = held([P, 4, KP], U16, "w1d_w")
-        deal(w1d_w[:], w1_w[:].rearrange("p a (b n) -> p (a b) n", b=2), 4)
-        tab_w[1] = load_tab(1, "slot_d")
-        for q in range(4):
-            nc.sync.dma_start(out=w3_s[32 * q : 32 * q + 8, :].bitcast(I32),
-                              in_=w3_scales[:, 4 * q : 4 * q + 4, :].bitcast(I32))
-        w3_w = held([P, 2, N], I32, "w3_w", "slot_f")
-        nc.sync.dma_start(out=w3_w[:], in_=w3_words.rearrange("a p n t -> p a (n t)").bitcast(I32))
-        load_travel(0, "slot_i")
-        v_s = [held([P, S], U8, f"v_s{a}") for a in range(2)]
-        v_w = [held([P, S], U32, f"v_w{a}") for a in range(2)]
-        for a in range(2):
-            nc.vector.tensor_copy(v_s[a][:], tab_s[:, a, :].indirect(offs_sb[:]))
-        w2_q[1] = quantize(w2_b1, "w2q1", "slot_c")
-        load_travel(1, "slot_a")
-        site(1, None)
-        load_w4(1, 0, "slot_j")
-        w1d_s = [held([P, 2, KP], U8, "w1d_s0"), None]
-        deal(w1d_s[0][:], w1_s[:, :, 0:KP], 8)
-        for a in range(2):
-            nc.vector.tensor_copy(v_w[a][:], tab_w[a][:].bitcast(U32).indirect(offs_sb[:]))
-        w1d_s[1] = held([P, 2, KP], U8, "w1d_s1", "slot_d")
-        deal(w1d_s[1][:], w1_s[:, :, KP : 2 * KP], 8)
-        load_w4(0, 0, "slot_e")
-        load_w4(0, 1, "slot_b")
+        def w4_rounded(a, g, copy):
+            return round_weight(w4_raw[a, g], f"w4_b{a}{g}", f"w4_b{a}", copy)
+
+        w2_q[0] = quantize(round_weight(w2_raw[0], "w2_b0", None, nc.scalar.copy), "w2q0", "tab_s")
+        site(0)
+        w2_q[1] = quantize(round_weight(w2_raw[1], "w2_b1", None, nc.vector.tensor_copy), "w2q1")
         slip(0)
-        h_rows = [h_scaled(0), None]
+        h_scaled(0, None)
         slip(1)
-        h_rows[1] = h_scaled(1)
-        shared = load_w4(1, 1, "slot_d", 0)
-
+        site(1)
+        h_scaled(1, "w2q1_codes")
+        h_b = [weave(h_rows[b], f"h_b{b}", 4, f"w2_b{b}", (nc.vector.tensor_copy, nc.scalar.copy)[b])
+               for b in range(2)]
+        w4_b = {(a, 0): w4_rounded(a, 0, nc.scalar.copy) for a in range(2)}
         w3d_s = held([P, 2, KP], U8, "w3d_s")
-        w3d_w = [held([P, 2, KP], I32, f"w3d_w{g}") for g in range(2)]
+        deal(w3d_s[:], w3_s[:, 0, :].rearrange("p (g n) -> p g n", g=2))
+        for b in range(2):
+            damped(b)
+            z_b = z_rounded(b)
+            zq[b] = quantize(z_b, f"zq{b}")
+            hq[b] = quantize(h_b[b], f"hq{b}")
+            deal_w3(b)
+            w4_q[b, 0] = quantize(w4_b[b, 0], f"w4q{b}0")
+        for a in range(2):
+            w4_q[a, 1] = quantize(w4_rounded(a, 1, nc.scalar.copy), f"w4q{a}1")
+
         y_scales = held([P, 2, S], U8, "y_scales")
 
-        def w4_piece(a, g, slot=None, copy=nc.scalar.copy):
-            w4_q[a, g] = quantize(round_weight(w4_raw[a, g], f"w4_b{a}{g}", slot, copy), f"w4q{a}{g}")
-
-        deal(w3d_s[:], w3_s[:].rearrange("p (g n) -> p g n", g=2), 8)
-        for g in range(2):
-            deal(w3d_w[g][:], w3_w[:, :, KP * g : KP * (g + 1)], 2)
-        damped(0, "slot_f")
-        hq[0] = quantize(weave(h_rows[0][:], "h_b0", 4), "hq0")
-        damped(1, "slot_g")
-        z_b0 = z_rounded(0)
-        hq[1] = quantize(weave(h_rows[1][:], "h_b1", 4), "hq1")
-        zq[0] = quantize(z_b0, "zq0")
-        w4_piece(0, 0, "slot_k")
-        z_b1 = z_rounded(1, "slot_k")
-        w4_piece(1, 0)
-        zq[1] = quantize(z_b1, "zq1")
-        w4_piece(0, 1)
-        w4_piece(1, 1)
-
-        accs = [[bank(f"y{g}{t}") for t in range(PACK)] for g in range(2)]
-
-        def y_pass(g, which, a, start, stop):
-            for t in range(PACK):
-                cols = slice(P * t, P * (t + 1))
-                if which == 3:
-                    lw, ls = w3d_w[g][:, a, cols], w3d_s[4 * a : P, g, cols]
-                    rw, rs = hq[a]
-                else:
-                    lw, ls = w4_q[a, g][0][:, cols], w4_q[a, g][1][:, cols]
-                    rw, rs = zq[a]
-                nc.tensor.matmul_mx(out=accs[g][t][:], lhsT=lw.bitcast(FP8X4), lhsT_scale=ls,
-                                    rhs=rw[:].bitcast(FP8X4), rhs_scale=rs[:], start=start, stop=stop)
-
-        def hand_out(g):
-            y = shared[:, 0:PACK, :] if g == 0 else held([P, PACK, S], F32, "y1")[:]
+        def project(g):
+            accs = [bank(f"y{g}{t}", PACK * g + t) for t in range(PACK)]
+            for step in range(4):
+                a = step % 2
+                for t in range(PACK):
+                    cols = slice(P * t, P * (t + 1))
+                    if step < 2:
+                        lw, ls = w3d_w[g][:, a, cols], w3d_s[4 * a : P, g, cols]
+                        rw, rs = hq[a]
+                    else:
+                        lw, ls = w4_q[a, g][0][:, cols], w4_q[a, g][1][:, cols]
+                        rw, rs = zq[a]
+                    nc.tensor.matmul_mx(out=accs[t][:], lhsT=lw.bitcast(FP8X4), lhsT_scale=ls,
+                                        rhs=rw[:].bitcast(FP8X4), rhs_scale=rs[:],
+                                        start=(step == 0), stop=(step == 3))
+            y = held([P, PACK, S], F32, f"y{g}", ("w4_raw01", "tab_w0")[g])
             rows = out_0[KP * g : KP * (g + 1), :].rearrange("(p t) s -> p t s", t=PACK)
             for t in range(PACK):
-                if (g, t) in ((0, 3), (1, 3)):
-                    nc.vector.tensor_copy(out=y[:, t, :], in_=accs[g][t][:])
-                else:
-                    nc.scalar.copy(out=y[:, t, :], in_=accs[g][t][:])
+                copy = nc.vector.tensor_copy if t == PACK - 1 else nc.scalar.copy
+                copy(out=y[:, t, :], in_=accs[t][:])
                 if t % 2 == 1:
                     nc.sync.dma_start(out=rows[:, t - 1 : t + 1, :], in_=y[:, t - 1 : t + 1, :])
-            vals = weave(y, f"y_b{g}", 2)
+            vals = weave(y, f"y_b{g}", 2, f"z_b{g}", nc.vector.tensor_copy)
             codes = held([P, S], U32, f"y_codes{g}")
             nc.vector.quantize_mx(out=codes[:].bitcast(FP8X4), scales=y_scales[:, g, :], in_=vals[:])
             nc.sync.dma_start(out=out_1[g].rearrange("p m t -> p (m t)").bitcast(I32), in_=codes[:].bitcast(I32))
 
-        for g, which, a in ((0, 3, 0), (1, 3, 0), (0, 3, 1), (1, 3, 1), (0, 4, 0), (0, 4, 1), (1, 4, 0), (1, 4, 1)):
-            y_pass(g, which, a, (which, a) == (3, 0), (which, a) == (4, 1))
-
-        hand_out(0)
-        hand_out(1)
+        project(0)
+        project(1)
         for r in range(4):
             nc.scalar.dma_start(
                 out=out_2[:, r:16:4, :].rearrange("g q m -> q g m").bitcast(I32),

@@ -18,6 +18,7 @@ PACK = 4
 KP = P * PACK
 K, K2, T, T2, S, H, N = 1024, 512, 2048, 1024, 512, 1024, 1024
 FLOPS = 2 * S * (K * H + K2 * H + 2 * H * N)
+W3_ROW = 4
 
 
 def tile_list_rupture_site_features_kernel(
@@ -40,8 +41,8 @@ def tile_list_rupture_site_features_kernel(
         def clear(engine, plane):
             engine.memset(plane[:].rearrange("p a n -> p (a n)").bitcast(I32), 0)
 
-        def load_scale_rows(queue, plane, scales, first=0):
-            for r in range(4):
+        def load_scale_rows(queue, plane, scales, first=0, rows=range(4)):
+            for r in rows:
                 queue.dma_start(out=plane[first + r : P : 32].bitcast(I32),
                                 in_=scales[:, r:16:4, :].rearrange("a q n -> q a n").bitcast(I32))
 
@@ -88,8 +89,7 @@ def tile_list_rupture_site_features_kernel(
         offs2_sb = lists.tile([P, S // 16], U16, name="offs2_sb")
         tab_s = held([P, 2, T], U8, "tab_s")
         tab2_s = held([P, 1, T2], U8, "tab2_s")
-        w1_s = held([P, 2, H], U8, "w1_s")
-        w3_s = held([P, 1, N], U8, "w3_s")
+        w_s = held([P, 2, H], U8, "w_s")
         w1_w = held([P, 2, H], U16, "w1_w")
         tab2_w = held([P, T2], U16, "tab2_w")
         gain_sb = held([P, 2, PACK], F32, "gain_sb")
@@ -97,8 +97,7 @@ def tile_list_rupture_site_features_kernel(
 
         clear(nc.vector, tab2_s)
         clear(nc.vector, tab_s)
-        clear(nc.vector, w1_s)
-        clear(nc.vector, w3_s)
+        clear(nc.vector, w_s)
         nc.vector.memset(warm[:], 0.0)
         nc.scalar.activation(out=warm[:], in_=warm[:], func=ACT.Sigmoid)
 
@@ -107,17 +106,10 @@ def tile_list_rupture_site_features_kernel(
             nc.sync.dma_start(out=words[:], in_=tab_words[a].rearrange("p n t -> p (n t)").bitcast(I32))
             return words
 
-        def load_w3(g):
-            words = held([P, 2, KP], I32, f"w3_w{g}")
-            nc.sync.dma_start(
-                out=words[:],
-                in_=w3_words[:, :, KP * g : KP * (g + 1), :].rearrange("a p n t -> p a (n t)").bitcast(I32))
-            return words
-
         def load_w4(a, g):
             return load_rows(f"w4_raw{a}{g}", w4[KP * a : KP * (a + 1), KP * g : KP * (g + 1)])
 
-        w2_raw, travel_sb, w3_w, w4_raw = {}, {}, {}, {}
+        w2_raw, travel_sb, w4_raw = {}, {}, {}
         nc.sync.dma_start(offs2_sb[:], offs2)
         nc.sync.dma_start(out=tab2_w[:].bitcast(I32), in_=tab2_words[0].bitcast(I32))
         nc.sync.dma_start(out=w1_w[:].bitcast(I32), in_=w1_words.rearrange("a p n -> p a n").bitcast(I32))
@@ -125,20 +117,19 @@ def tile_list_rupture_site_features_kernel(
         load_scale_rows(nc.sync, tab2_s, tab2_scales)
         w2_raw[0] = load_rows("w2_raw0", w2[:, 0:KP])
         load_scale_rows(nc.sync, tab_s, tab_scales)
-        nc.sync.dma_start(out=gain_sb[:], in_=gain.rearrange("(b p t) -> p b t", b=2, t=PACK))
+        load_scale_rows(nc.sync, w_s, w3_scales, W3_ROW, range(2))
         tab_w = [load_tab(0), None]
-        load_scale_rows(nc.sync, w1_s, w1_scales)
+        load_scale_rows(nc.sync, w_s, w3_scales, W3_ROW, range(2, 4))
+        load_scale_rows(nc.sync, w_s, w1_scales)
         tab_w[1] = load_tab(1)
+        nc.sync.dma_start(out=gain_sb[:], in_=gain.rearrange("(b p t) -> p b t", b=2, t=PACK))
         w2_raw[1] = load_rows("w2_raw1", w2[:, KP : 2 * KP])
         travel_sb[0] = load_rows("travel0", travel[0:KP, :])
-        for q in range(4):
-            nc.sync.dma_start(out=w3_s[32 * q : 32 * q + 8, 0, :].bitcast(I32),
-                              in_=w3_scales[:, 4 * q : 4 * q + 4, :].bitcast(I32))
+        w3_w = held([P, 2, N], I32, "w3_w")
+        nc.sync.dma_start(out=w3_w[:], in_=w3_words.rearrange("a p n t -> p a (n t)").bitcast(I32))
         w4_raw[0, 0] = load_w4(0, 0)
         travel_sb[1] = load_rows("travel1", travel[KP : 2 * KP, :])
-        w3_w[0] = load_w3(0)
         w4_raw[1, 0] = load_w4(1, 0)
-        w3_w[1] = load_w3(1)
         w4_raw[0, 1] = load_w4(0, 1)
         w4_raw[1, 1] = load_w4(1, 1)
 
@@ -147,17 +138,17 @@ def tile_list_rupture_site_features_kernel(
         w1d_w = held([P, 4, KP], U16, "w1d_w")
         v_s = [held([P, S], U8, f"v_s{a}") for a in range(2)]
         v_w = [held([P, S], U32, f"v_w{a}") for a in range(2)]
-        w1d_s = [held([P, 2, KP], U8, "w1d_s0"), None]
+        wd_s = [held([P, 2, KP], U8, "wd_s0"), None]
         nc.vector.tensor_copy(v2_w[:], tab2_w[:].indirect(offs2_sb[:]))
         nc.vector.tensor_copy(v2_s[:], tab2_s[:, 0, :].indirect(offs2_sb[:]))
         deal(w1d_w[:], w1_w[:].rearrange("p a (b n) -> p (a b) n", b=2))
         for a in range(2):
             nc.vector.tensor_copy(v_s[a][:], tab_s[:, a, :].indirect(offs_sb[:]))
         nc.vector.tensor_copy(v_w[0][:], tab_w[0][:].bitcast(U32).indirect(offs_sb[:]))
-        deal(w1d_s[0][:], w1_s[:, :, 0:KP])
+        deal(wd_s[0][:], w_s[:, :, 0:KP])
         nc.vector.tensor_copy(v_w[1][:], tab_w[1][:].bitcast(U32).indirect(offs_sb[:]))
-        w1d_s[1] = held([P, 2, KP], U8, "w1d_s1", "tab_w1")
-        deal(w1d_s[1][:], w1_s[:, :, KP : 2 * KP])
+        wd_s[1] = held([P, 2, KP], U8, "wd_s1", "tab_w1")
+        deal(wd_s[1][:], w_s[:, :, KP : 2 * KP])
 
         sat, damp, part, h_rows, w2_q, w4_q, hq, zq, w3d_w = {}, {}, {}, {}, {}, {}, {}, {}, {}
 
@@ -168,7 +159,7 @@ def tile_list_rupture_site_features_kernel(
                 for t in range(PACK):
                     cols = slice(P * t, P * (t + 1))
                     nc.tensor.matmul_mx(out=accs[t][:], lhsT=w1d_w[:, 2 * a + b, cols].bitcast(FP4X4),
-                                        lhsT_scale=w1d_s[b][:, a, cols],
+                                        lhsT_scale=wd_s[b][:, a, cols],
                                         rhs=v_w[a][:].bitcast(FP8X4), rhs_scale=v_s[a][:],
                                         start=(a == 0), stop=(a == 1))
             for t in range(PACK):
@@ -191,24 +182,24 @@ def tile_list_rupture_site_features_kernel(
                                      scale=gain_sb[:, b, t : t + 1])
 
         def damped(b):
-            part[b] = held([P, PACK, S], F32, f"part{b}", f"w2_raw{b}")
+            part[b] = held([P, PACK, S], F32, f"part{b}", ("w2_raw1", "travel0")[b])
             for t in range(PACK):
                 nc.vector.scalar_tensor_tensor(
                     out=part[b][:, t, :], in0=sat[b][:, t, :], scalar=gain_sb[:, b, t : t + 1],
                     in1=damp[b][:, t, :], op0=ALU.mult, op1=ALU.mult)
 
         def z_rounded(b):
-            vals = held([P, PACK * S], BF16, f"z_b{b}")
+            vals = held([P, PACK * S], BF16, f"z_b{b}", ("w3_w", None)[b])
             nc.vector.tensor_tensor(out=woven(vals, 2), in0=by_runs(part[b], 2), in1=by_runs(travel_sb[b], 2),
                                     op=ALU.add)
             return vals
 
         def deal_w3(g):
             w3d_w[g] = held([P, 2, KP], I32, f"w3d_w{g}")
-            deal_by_pairs(w3d_w[g][:], w3_w[g][:])
+            deal_by_pairs(w3d_w[g][:], w3_w[:, :, KP * g : KP * (g + 1)])
 
         def w4_rounded(a, g, copy):
-            return round_weight(w4_raw[a, g], f"w4_b{a}{g}", f"w4_b{a}", copy)
+            return round_weight(w4_raw[a, g], f"w4_b{a}{g}", None, copy)
 
         w2_q[0] = quantize(round_weight(w2_raw[0], "w2_b0", None, nc.scalar.copy), "w2q0", "tab_s")
         site(0)
@@ -218,18 +209,17 @@ def tile_list_rupture_site_features_kernel(
         slip(1)
         site(1)
         h_scaled(1, "w2q1_codes")
-        h_b = [weave(h_rows[b], f"h_b{b}", 4, f"w2_b{b}", (nc.vector.tensor_copy, nc.scalar.copy)[b])
-               for b in range(2)]
         w4_b = {(a, 0): w4_rounded(a, 0, nc.scalar.copy) for a in range(2)}
-        w3d_s = held([P, 2, KP], U8, "w3d_s")
-        deal(w3d_s[:], w3_s[:, 0, :].rearrange("p (g n) -> p g n", g=2))
+        for g in range(2):
+            deal_w3(g)
         for b in range(2):
             damped(b)
+            h_b = weave(h_rows[b], f"h_b{b}", 4, f"w2_b{1 - b}", nc.vector.tensor_copy)
             z_b = z_rounded(b)
+            hq[b] = quantize(h_b, f"hq{b}")
             zq[b] = quantize(z_b, f"zq{b}")
-            hq[b] = quantize(h_b[b], f"hq{b}")
-            deal_w3(b)
-            w4_q[b, 0] = quantize(w4_b[b, 0], f"w4q{b}0")
+        for a in range(2):
+            w4_q[a, 0] = quantize(w4_b[a, 0], f"w4q{a}0")
         for a in range(2):
             w4_q[a, 1] = quantize(w4_rounded(a, 1, nc.scalar.copy), f"w4q{a}1")
 
@@ -242,7 +232,7 @@ def tile_list_rupture_site_features_kernel(
                 for t in range(PACK):
                     cols = slice(P * t, P * (t + 1))
                     if step < 2:
-                        lw, ls = w3d_w[g][:, a, cols], w3d_s[4 * a : P, g, cols]
+                        lw, ls = w3d_w[g][:, a, cols], wd_s[g][W3_ROW:P, a, cols]
                         rw, rs = hq[a]
                     else:
                         lw, ls = w4_q[a, g][0][:, cols], w4_q[a, g][1][:, cols]
@@ -250,14 +240,14 @@ def tile_list_rupture_site_features_kernel(
                     nc.tensor.matmul_mx(out=accs[t][:], lhsT=lw.bitcast(FP8X4), lhsT_scale=ls,
                                         rhs=rw[:].bitcast(FP8X4), rhs_scale=rs[:],
                                         start=(step == 0), stop=(step == 3))
-            y = held([P, PACK, S], F32, f"y{g}", ("w4_raw01", "tab_w0")[g])
+            y = held([P, PACK, S], F32, f"y{g}", ("w4_raw11", "tab_w0")[g])
             rows = out_0[KP * g : KP * (g + 1), :].rearrange("(p t) s -> p t s", t=PACK)
             for t in range(PACK):
-                copy = nc.vector.tensor_copy if t == PACK - 1 else nc.scalar.copy
+                copy = nc.vector.tensor_copy if (g == 0 and t >= 2) else nc.scalar.copy
                 copy(out=y[:, t, :], in_=accs[t][:])
                 if t % 2 == 1:
                     nc.sync.dma_start(out=rows[:, t - 1 : t + 1, :], in_=y[:, t - 1 : t + 1, :])
-            vals = weave(y, f"y_b{g}", 2, f"z_b{g}", nc.vector.tensor_copy)
+            vals = weave(y, f"y_b{g}", 2, f"h_rows{0}" if g == 0 else "z_b1", nc.vector.tensor_copy)
             codes = held([P, S], U32, f"y_codes{g}")
             nc.vector.quantize_mx(out=codes[:].bitcast(FP8X4), scales=y_scales[:, g, :], in_=vals[:])
             nc.sync.dma_start(out=out_1[g].rearrange("p m t -> p (m t)").bitcast(I32), in_=codes[:].bitcast(I32))

@@ -30,6 +30,7 @@ def tile_list_rupture_site_features_kernel(
     with ExitStack() as ctx:
         lists = ctx.enter_context(tc.tile_pool(name="lists", bufs=1))
         keep = ctx.enter_context(tc.tile_pool(name="keep", bufs=1))
+        late = ctx.enter_context(tc.tile_pool(name="late", bufs=1))
         psum = ctx.enter_context(tc.psum_pool(name="psum", bufs=1))
 
         def held(shape, dtype, name, slot=None):
@@ -61,29 +62,24 @@ def tile_list_rupture_site_features_kernel(
                 out=dst.rearrange("p a (t c i) -> p a c t i", t=PACK, i=2),
                 in_=src.rearrange("p a (c i t) -> p a c t i", t=PACK, i=2))
 
-        def round_weight(raw, name, slot, copy):
-            vals = held([P, PACK * S], BF16, name, slot)
-            copy(
-                out=vals[:].rearrange("p (u v m j) -> p u m j v", u=2, v=2, j=PACK),
+        def round_weight(raw, vals):
+            nc.scalar.copy(
+                out=vals.rearrange("p (u v m j) -> p u m j v", u=2, v=2, j=PACK),
                 in_=raw[:].rearrange("p j (m u v) -> p u m j v", u=2, v=2))
-            return vals
 
         def quantize(vals, name, slot=None):
-            codes = held([P, S], U32, name + "_codes", slot)
-            scales = held([P, S], U8, name + "_scales")
+            width = vals.shape[1] // PACK
+            codes = held([P, width], U32, name + "_codes", slot)
+            scales = held([P, width], U8, name + "_scales")
             nc.vector.quantize_mx(out=codes[:].bitcast(FP8X4), scales=scales[:], in_=vals[:])
             return codes, scales
 
         def woven(vals, run):
-            return vals[:].rearrange("p (c i t) -> p c t i", i=run, t=PACK)
+            return vals.rearrange("p (c i t) -> p c t i", i=run, t=PACK)
 
         def by_runs(rows, run):
-            return rows[:].rearrange("p t (c i) -> p c t i", i=run)
+            return rows.rearrange("p t (c i) -> p c t i", i=run)
 
-        def weave(rows, name, run, slot, copy):
-            vals = held([P, PACK * S], BF16, name, slot)
-            copy(out=woven(vals, run), in_=by_runs(rows, run))
-            return vals
 
         offs_sb = lists.tile([P, S // 16], U16, name="offs_sb")
         offs2_sb = lists.tile([P, S // 16], U16, name="offs2_sb")
@@ -95,14 +91,14 @@ def tile_list_rupture_site_features_kernel(
         gain_sb = held([P, 2, PACK], F32, "gain_sb")
         warm = held([P, 8], F32, "warm")
 
-        clear(nc.vector, tab2_s)
         clear(nc.vector, tab_s)
+        clear(nc.vector, tab2_s)
         clear(nc.vector, w_s)
         nc.vector.memset(warm[:], 0.0)
         nc.scalar.activation(out=warm[:], in_=warm[:], func=ACT.Sigmoid)
 
         def load_tab(a):
-            words = held([P, T], I32, f"tab_w{a}")
+            words = held([P, T], I32, "tab_w0") if a == 0 else late.tile([P, T], I32, name="tab_w1", offset=0, align_bytes=64)
             nc.sync.dma_start(out=words[:], in_=tab_words[a].rearrange("p n t -> p (n t)").bitcast(I32))
             return words
 
@@ -112,14 +108,15 @@ def tile_list_rupture_site_features_kernel(
         w2_raw, travel_sb, w4_raw = {}, {}, {}
         nc.sync.dma_start(offs2_sb[:], offs2)
         nc.sync.dma_start(out=tab2_w[:].bitcast(I32), in_=tab2_words[0].bitcast(I32))
-        nc.sync.dma_start(out=w1_w[:].bitcast(I32), in_=w1_words.rearrange("a p n -> p a n").bitcast(I32))
         nc.sync.dma_start(offs_sb[:], offs)
-        load_scale_rows(nc.sync, tab2_s, tab2_scales)
-        w2_raw[0] = load_rows("w2_raw0", w2[:, 0:KP])
         load_scale_rows(nc.sync, tab_s, tab_scales)
-        load_scale_rows(nc.sync, w_s, w3_scales, W3_ROW, range(2))
+        w2_raw[0] = load_rows("w2_raw0", w2[:, 0:KP])
+        load_scale_rows(nc.sync, tab2_s, tab2_scales)
+        nc.sync.dma_start(out=w1_w[:].bitcast(I32), in_=w1_words.rearrange("a p n -> p a n").bitcast(I32))
+        load_scale_rows(nc.sync, w_s, w3_scales, W3_ROW, range(1))
         tab_w = [load_tab(0), None]
-        load_scale_rows(nc.sync, w_s, w3_scales, W3_ROW, range(2, 4))
+        load_scale_rows(nc.sync, w_s, w3_scales, W3_ROW, range(1, 3))
+        load_scale_rows(nc.gpsimd, w_s, w3_scales, W3_ROW, range(3, 4))
         load_scale_rows(nc.sync, w_s, w1_scales)
         tab_w[1] = load_tab(1)
         nc.sync.dma_start(out=gain_sb[:], in_=gain.rearrange("(b p t) -> p b t", b=2, t=PACK))
@@ -135,30 +132,19 @@ def tile_list_rupture_site_features_kernel(
 
         v2_w = held([P, S], U16, "v2_w")
         v2_s = held([P, S], U8, "v2_s")
-        w1d_w = held([P, 4, KP], U16, "w1d_w")
         v_s = [held([P, S], U8, f"v_s{a}") for a in range(2)]
         v_w = [held([P, S], U32, f"v_w{a}") for a in range(2)]
-        wd_s = [held([P, 2, KP], U8, "wd_s0"), None]
-        nc.vector.tensor_copy(v2_w[:], tab2_w[:].indirect(offs2_sb[:]))
-        nc.vector.tensor_copy(v2_s[:], tab2_s[:, 0, :].indirect(offs2_sb[:]))
-        deal(w1d_w[:], w1_w[:].rearrange("p a (b n) -> p (a b) n", b=2))
-        for a in range(2):
-            nc.vector.tensor_copy(v_s[a][:], tab_s[:, a, :].indirect(offs_sb[:]))
-        nc.vector.tensor_copy(v_w[0][:], tab_w[0][:].bitcast(U32).indirect(offs_sb[:]))
-        deal(wd_s[0][:], w_s[:, :, 0:KP])
-        nc.vector.tensor_copy(v_w[1][:], tab_w[1][:].bitcast(U32).indirect(offs_sb[:]))
-        wd_s[1] = held([P, 2, KP], U8, "wd_s1", "tab_w1")
-        deal(wd_s[1][:], w_s[:, :, KP : 2 * KP])
+        w1d_w = [held([P, 2, KP], U16, "w1d_w0"), late.tile([P, 2, KP], U16, name="w1d_w1", offset=0, align_bytes=64)]
+        wd_s = [held([P, 2, KP], U8, "wd_s0"), late.tile([P, 2, KP], U8, name="wd_s1", offset=2048, align_bytes=64)]
+        sat, damp, part, w2_q, w4_q, hq, zq, w3d_w = {}, {}, {}, {}, {}, {}, {}, {}
 
-        sat, damp, part, h_rows, w2_q, w4_q, hq, zq, w3d_w = {}, {}, {}, {}, {}, {}, {}, {}, {}
-
-        def slip(b):
-            sat[b] = held([P, PACK, S], F32, f"sat{b}")
+        def slip(b, slot):
+            sat[b] = held([P, PACK, S], F32, f"sat{b}", slot)
             accs = [bank(f"slip{b}{t}", PACK * (1 - b) + t) for t in range(PACK)]
             for a in range(2):
                 for t in range(PACK):
                     cols = slice(P * t, P * (t + 1))
-                    nc.tensor.matmul_mx(out=accs[t][:], lhsT=w1d_w[:, 2 * a + b, cols].bitcast(FP4X4),
+                    nc.tensor.matmul_mx(out=accs[t][:], lhsT=w1d_w[b][:, a, cols].bitcast(FP4X4),
                                         lhsT_scale=wd_s[b][:, a, cols],
                                         rhs=v_w[a][:].bitcast(FP8X4), rhs_scale=v_s[a][:],
                                         start=(a == 0), stop=(a == 1))
@@ -175,85 +161,120 @@ def tile_list_rupture_site_features_kernel(
                                     rhs=v2_w[:].bitcast(FP4X4), rhs_scale=v2_s[:], start=True, stop=True)
                 nc.scalar.activation(out=damp[b][:, t, :], in_=acc[:], func=ACT.Sigmoid, scale=-1.0)
 
-        def h_scaled(b, slot):
-            h_rows[b] = held([P, PACK, S], BF16, f"h_rows{b}", slot)
-            for t in range(PACK):
-                nc.scalar.activation(out=h_rows[b][:, t, :], in_=sat[b][:, t, :], func=ACT.Copy,
-                                     scale=gain_sb[:, b, t : t + 1])
-
-        def damped(b):
-            part[b] = held([P, PACK, S], F32, f"part{b}", ("w2_raw1", "travel0")[b])
-            for t in range(PACK):
+        def damped(b, slot, slices=range(PACK)):
+            if b not in part:
+                part[b] = held([P, PACK, S], F32, f"part{b}", slot)
+            for t in slices:
                 nc.vector.scalar_tensor_tensor(
                     out=part[b][:, t, :], in0=sat[b][:, t, :], scalar=gain_sb[:, b, t : t + 1],
                     in1=damp[b][:, t, :], op0=ALU.mult, op1=ALU.mult)
 
+        def h_rounded(b, slot):
+            vals = held([P, PACK * S], BF16, f"h_b{b}", slot)
+            gains = gain_sb[:, b, :].unsqueeze(1).unsqueeze(3).to_broadcast([P, S // 2, PACK, 2])
+            nc.vector.tensor_tensor(out=woven(vals[:], 2), in0=by_runs(sat[b][:], 2), in1=gains, op=ALU.mult)
+            return vals
+
         def z_rounded(b):
-            vals = held([P, PACK * S], BF16, f"z_b{b}", ("w3_w", None)[b])
-            nc.vector.tensor_tensor(out=woven(vals, 2), in0=by_runs(part[b], 2), in1=by_runs(travel_sb[b], 2),
+            vals = held([P, PACK * S], BF16, f"z_b{b}")
+            nc.vector.tensor_tensor(out=woven(vals[:], 2), in0=by_runs(part[b][:], 2), in1=by_runs(travel_sb[b][:], 2),
                                     op=ALU.add)
             return vals
 
-        def deal_w3(g):
+        def rounded(raws, name, slot):
+            vals = held([P, len(raws) * PACK * S], BF16, name, slot)
+            for i, raw in enumerate(raws):
+                round_weight(raw, vals[:, PACK * S * i : PACK * S * (i + 1)])
+            return vals
+
+        nc.vector.tensor_copy(v2_w[:], tab2_w[:].indirect(offs2_sb[:]))
+        for a in range(2):
+            nc.vector.tensor_copy(v_s[a][:], tab_s[:, a, :].indirect(offs_sb[:]))
+        nc.vector.tensor_copy(v2_s[:], tab2_s[:, 0, :].indirect(offs2_sb[:]))
+        deal(w1d_w[0][:], w1_w[:, :, 0:KP])
+        w2_q[0] = quantize(rounded([w2_raw[0]], "w2_b0", None), "w2q0", "tab2_s")
+        site(0)
+        nc.vector.tensor_copy(v_w[0][:], tab_w[0][:].bitcast(U32).indirect(offs_sb[:]))
+        deal(wd_s[0][:], w_s[:, :, 0:KP])
+        nc.vector.tensor_copy(v_w[1][:], tab_w[1][:].bitcast(U32).indirect(offs_sb[:]))
+        deal(w1d_w[1][:], w1_w[:, :, KP : 2 * KP])
+        deal(wd_s[1][:], w_s[:, :, KP : 2 * KP])
+
+        slip(0, None)
+        w2_b1 = rounded([w2_raw[1]], "w2_b1", "w1d_w0")
+        damped(0, None)
+        h_b0 = h_rounded(0, None)
+        w2_q[1] = quantize(w2_b1, "w2q1")
+        slip(1, "w2_raw1")
+        site(1)
+        z_b0 = z_rounded(0)
+        hq[0] = quantize(h_b0, "hq0")
+        for g in range(2):
             w3d_w[g] = held([P, 2, KP], I32, f"w3d_w{g}")
             deal_by_pairs(w3d_w[g][:], w3_w[:, :, KP * g : KP * (g + 1)])
-
-        def w4_rounded(a, g, copy):
-            return round_weight(w4_raw[a, g], f"w4_b{a}{g}", None, copy)
-
-        w2_q[0] = quantize(round_weight(w2_raw[0], "w2_b0", None, nc.scalar.copy), "w2q0", "tab_s")
-        site(0)
-        w2_q[1] = quantize(round_weight(w2_raw[1], "w2_b1", None, nc.vector.tensor_copy), "w2q1")
-        slip(0)
-        h_scaled(0, None)
-        slip(1)
-        site(1)
-        h_scaled(1, "w2q1_codes")
-        w4_b = {(a, 0): w4_rounded(a, 0, nc.scalar.copy) for a in range(2)}
-        for g in range(2):
-            deal_w3(g)
-        for b in range(2):
-            damped(b)
-            h_b = weave(h_rows[b], f"h_b{b}", 4, f"w2_b{1 - b}", nc.vector.tensor_copy)
-            z_b = z_rounded(b)
-            hq[b] = quantize(h_b, f"hq{b}")
-            zq[b] = quantize(z_b, f"zq{b}")
+        zq[0] = quantize(z_b0, "zq0")
+        w4_b00 = rounded([w4_raw[0, 0]], "w4_b00", "v2_w")
+        w4_b10 = rounded([w4_raw[1, 0]], "w4_b10", "v2_s")
+        w4_b1 = rounded([w4_raw[0, 1], w4_raw[1, 1]], "w4_b1", "w2q1_codes")
+        h_b1 = h_rounded(1, "w3_w")
+        damped(1, "travel0", range(3))
+        hq[1] = quantize(h_b1, "hq1")
+        damped(1, None, range(3, PACK))
+        w4_q[0, 0] = quantize(w4_b00, "w4q00")
+        z_b1 = z_rounded(1)
+        w4_q[1, 0] = quantize(w4_b10, "w4q10")
+        zq[1] = quantize(z_b1, "zq1")
+        codes, scales = quantize(w4_b1, "w4q1")
         for a in range(2):
-            w4_q[a, 0] = quantize(w4_b[a, 0], f"w4q{a}0")
-        for a in range(2):
-            w4_q[a, 1] = quantize(w4_rounded(a, 1, nc.scalar.copy), f"w4q{a}1")
+            w4_q[a, 1] = codes[:, S * a : S * (a + 1)], scales[:, S * a : S * (a + 1)]
 
         y_scales = held([P, 2, S], U8, "y_scales")
 
-        def project(g):
-            accs = [bank(f"y{g}{t}", PACK * g + t) for t in range(PACK)]
-            for step in range(4):
-                a = step % 2
-                for t in range(PACK):
-                    cols = slice(P * t, P * (t + 1))
-                    if step < 2:
-                        lw, ls = w3d_w[g][:, a, cols], wd_s[g][W3_ROW:P, a, cols]
-                        rw, rs = hq[a]
-                    else:
-                        lw, ls = w4_q[a, g][0][:, cols], w4_q[a, g][1][:, cols]
-                        rw, rs = zq[a]
-                    nc.tensor.matmul_mx(out=accs[t][:], lhsT=lw.bitcast(FP8X4), lhsT_scale=ls,
-                                        rhs=rw[:].bitcast(FP8X4), rhs_scale=rs[:],
-                                        start=(step == 0), stop=(step == 3))
+        accs = [[bank(f"y{g}{t}", PACK * g + t) for t in range(PACK)] for g in range(2)]
+
+        def y_passes(g, a, from_h, start=False, stop=False, slices=range(PACK)):
+            for t in slices:
+                cols = slice(P * t, P * (t + 1))
+                if from_h:
+                    lw, ls = w3d_w[g][:, a, cols], wd_s[g][W3_ROW:P, a, cols]
+                    rw, rs = hq[a]
+                else:
+                    lw, ls = w4_q[a, g][0][:, cols], w4_q[a, g][1][:, cols]
+                    rw, rs = zq[a]
+                nc.tensor.matmul_mx(out=accs[g][t][:], lhsT=lw.bitcast(FP8X4), lhsT_scale=ls,
+                                    rhs=rw[:].bitcast(FP8X4), rhs_scale=rs[:], start=start, stop=stop)
+
+        y_passes(0, 0, True, start=True)
+        y_passes(1, 0, True, start=True)
+        y_passes(0, 1, True)
+        y_passes(1, 1, True)
+        y_passes(0, 0, False)
+        y_passes(0, 1, False, stop=True)
+        for t in range(PACK):
+            y_passes(1, 0, False, slices=[t])
+            y_passes(1, 1, False, stop=True, slices=[t])
+
+        def hand_out(g):
             y = held([P, PACK, S], F32, f"y{g}", ("w4_raw11", "tab_w0")[g])
             rows = out_0[KP * g : KP * (g + 1), :].rearrange("(p t) s -> p t s", t=PACK)
             for t in range(PACK):
                 copy = nc.vector.tensor_copy if (g == 0 and t >= 2) else nc.scalar.copy
-                copy(out=y[:, t, :], in_=accs[t][:])
+                copy(out=y[:, t, :], in_=accs[g][t][:])
                 if t % 2 == 1:
                     nc.sync.dma_start(out=rows[:, t - 1 : t + 1, :], in_=y[:, t - 1 : t + 1, :])
-            vals = weave(y, f"y_b{g}", 2, f"h_rows{0}" if g == 0 else "z_b1", nc.vector.tensor_copy)
+            vals = held([P, PACK * S], BF16, f"y_b{g}", f"z_b{g}")
             codes = held([P, S], U32, f"y_codes{g}")
-            nc.vector.quantize_mx(out=codes[:].bitcast(FP8X4), scales=y_scales[:, g, :], in_=vals[:])
+            halves = [slice(S // 2 * i, S // 2 * (i + 1)) for i in range(2)]
+            for cols in halves:
+                nc.vector.tensor_copy(out=woven(vals[:, PACK * cols.start : PACK * cols.stop], 2),
+                                      in_=by_runs(y[:, :, cols], 2))
+            for cols in halves:
+                nc.vector.quantize_mx(out=codes[:, cols].bitcast(FP8X4), scales=y_scales[:, g, cols],
+                                      in_=vals[:, PACK * cols.start : PACK * cols.stop])
             nc.sync.dma_start(out=out_1[g].rearrange("p m t -> p (m t)").bitcast(I32), in_=codes[:].bitcast(I32))
 
-        project(0)
-        project(1)
+        hand_out(0)
+        hand_out(1)
         for r in range(4):
             nc.scalar.dma_start(
                 out=out_2[:, r:16:4, :].rearrange("g q m -> q g m").bitcast(I32),

@@ -47,8 +47,8 @@ def tile_list_rupture_site_features_kernel(
                 queue.dma_start(out=plane[first + r : P : 32].bitcast(I32),
                                 in_=scales[:, r:16:4, :].rearrange("a q n -> q a n").bitcast(I32))
 
-        def load_rows(name, src, slot=None):
-            rows = held([P, PACK, S], F32, name, slot)
+        def load_rows(name, src):
+            rows = held([P, PACK, src.shape[1]], F32, name)
             nc.sync.dma_start(out=rows[:], in_=src.rearrange("(p j) c -> p j c", j=PACK))
             return rows
 
@@ -62,10 +62,11 @@ def tile_list_rupture_site_features_kernel(
                 out=dst.rearrange("p a (t c i) -> p a c t i", t=PACK, i=2),
                 in_=src.rearrange("p a (c i t) -> p a c t i", t=PACK, i=2))
 
-        def round_weight(raw, vals):
+        def round_weight(raw, vals, first=0):
+            count = raw.shape[2] // PACK
             nc.scalar.copy(
-                out=vals.rearrange("p (u v m j) -> p u m j v", u=2, v=2, j=PACK),
-                in_=raw[:].rearrange("p j (m u v) -> p u m j v", u=2, v=2))
+                out=vals.rearrange("p (u v m j) -> p u m j v", u=2, v=2, j=PACK)[:, :, first : first + count],
+                in_=raw.rearrange("p j (m u v) -> p u m j v", u=2, v=2))
 
         def quantize(vals, name, slot=None):
             width = vals.shape[1] // PACK
@@ -86,7 +87,6 @@ def tile_list_rupture_site_features_kernel(
         tab_s = held([P, 2, T], U8, "tab_s")
         tab2_s = held([P, 1, T2], U8, "tab2_s")
         w_s = held([P, 2, H], U8, "w_s")
-        w1_w = held([P, 2, H], U16, "w1_w")
         tab2_w = held([P, T2], U16, "tab2_w")
         gain_sb = held([P, 2, PACK], F32, "gain_sb")
         warm = held([P, 8], F32, "warm")
@@ -102,33 +102,38 @@ def tile_list_rupture_site_features_kernel(
             nc.sync.dma_start(out=words[:], in_=tab_words[a].rearrange("p n t -> p (n t)").bitcast(I32))
             return words
 
-        def load_w4(a, g):
-            return load_rows(f"w4_raw{a}{g}", w4[KP * a : KP * (a + 1), KP * g : KP * (g + 1)])
+        def load_w1(b):
+            words = held([P, 2, KP], U16, f"w1_w{b}")
+            nc.sync.dma_start(
+                out=words[:].bitcast(I32),
+                in_=w1_words[:, :, 2 * KP * b : 2 * KP * (b + 1)].rearrange("a p n -> p a n").bitcast(I32))
+            return words
 
-        w2_raw, travel_sb, w4_raw = {}, {}, {}
+        w2_raw, travel_sb = {}, {}
         nc.sync.dma_start(offs2_sb[:], offs2)
         nc.sync.dma_start(out=tab2_w[:].bitcast(I32), in_=tab2_words[0].bitcast(I32))
         nc.sync.dma_start(offs_sb[:], offs)
         load_scale_rows(nc.sync, tab_s, tab_scales)
         w2_raw[0] = load_rows("w2_raw0", w2[:, 0:KP])
         load_scale_rows(nc.sync, tab2_s, tab2_scales)
-        nc.sync.dma_start(out=w1_w[:].bitcast(I32), in_=w1_words.rearrange("a p n -> p a n").bitcast(I32))
+        w1_w = [load_w1(0), None]
         load_scale_rows(nc.sync, w_s, w3_scales, W3_ROW, range(1))
         tab_w = [load_tab(0), None]
         load_scale_rows(nc.sync, w_s, w3_scales, W3_ROW, range(1, 3))
         load_scale_rows(nc.gpsimd, w_s, w3_scales, W3_ROW, range(3, 4))
         load_scale_rows(nc.sync, w_s, w1_scales)
         tab_w[1] = load_tab(1)
+        w1_w[1] = load_w1(1)
         nc.sync.dma_start(out=gain_sb[:], in_=gain.rearrange("(b p t) -> p b t", b=2, t=PACK))
         w2_raw[1] = load_rows("w2_raw1", w2[:, KP : 2 * KP])
         travel_sb[0] = load_rows("travel0", travel[0:KP, :])
         w3_w = held([P, 2, N], I32, "w3_w")
         nc.sync.dma_start(out=w3_w[:], in_=w3_words.rearrange("a p n t -> p a (n t)").bitcast(I32))
-        w4_raw[0, 0] = load_w4(0, 0)
+        w4_raw0 = load_rows("w4_raw0", w4[0:KP, :])
         travel_sb[1] = load_rows("travel1", travel[KP : 2 * KP, :])
-        w4_raw[1, 0] = load_w4(1, 0)
-        w4_raw[0, 1] = load_w4(0, 1)
-        w4_raw[1, 1] = load_w4(1, 1)
+        w4_raw10 = load_rows("w4_raw10", w4[KP : 2 * KP, 0:KP])
+        w4_raw11 = [load_rows(f"w4_raw11{i}", w4[KP : 2 * KP, KP + KP // 2 * i : KP + KP // 2 * (i + 1)])
+                    for i in range(2)]
 
         v2_w = held([P, S], U16, "v2_w")
         v2_s = held([P, S], U8, "v2_s")
@@ -181,27 +186,26 @@ def tile_list_rupture_site_features_kernel(
                                     op=ALU.add)
             return vals
 
-        def rounded(raws, name, slot):
-            vals = held([P, len(raws) * PACK * S], BF16, name, slot)
-            for i, raw in enumerate(raws):
-                round_weight(raw, vals[:, PACK * S * i : PACK * S * (i + 1)])
+        def rounded(raw, name, slot):
+            vals = held([P, PACK * S], BF16, name, slot)
+            round_weight(raw, vals[:])
             return vals
 
         nc.vector.tensor_copy(v2_w[:], tab2_w[:].indirect(offs2_sb[:]))
         for a in range(2):
             nc.vector.tensor_copy(v_s[a][:], tab_s[:, a, :].indirect(offs_sb[:]))
         nc.vector.tensor_copy(v2_s[:], tab2_s[:, 0, :].indirect(offs2_sb[:]))
-        deal(w1d_w[0][:], w1_w[:, :, 0:KP])
-        w2_q[0] = quantize(rounded([w2_raw[0]], "w2_b0", None), "w2q0", "tab2_s")
+        deal(w1d_w[0][:], w1_w[0][:])
+        w2_q[0] = quantize(rounded(w2_raw[0][:], "w2_b0", None), "w2q0", "tab2_s")
         site(0)
         nc.vector.tensor_copy(v_w[0][:], tab_w[0][:].bitcast(U32).indirect(offs_sb[:]))
         deal(wd_s[0][:], w_s[:, :, 0:KP])
         nc.vector.tensor_copy(v_w[1][:], tab_w[1][:].bitcast(U32).indirect(offs_sb[:]))
-        deal(w1d_w[1][:], w1_w[:, :, KP : 2 * KP])
+        deal(w1d_w[1][:], w1_w[1][:])
         deal(wd_s[1][:], w_s[:, :, KP : 2 * KP])
 
         slip(0, None)
-        w2_b1 = rounded([w2_raw[1]], "w2_b1", "w1d_w0")
+        w2_b1 = rounded(w2_raw[1][:], "w2_b1", "w1d_w0")
         damped(0, None)
         h_b0 = h_rounded(0, None)
         w2_q[1] = quantize(w2_b1, "w2q1")
@@ -213,9 +217,12 @@ def tile_list_rupture_site_features_kernel(
             w3d_w[g] = held([P, 2, KP], I32, f"w3d_w{g}")
             deal_by_pairs(w3d_w[g][:], w3_w[:, :, KP * g : KP * (g + 1)])
         zq[0] = quantize(z_b0, "zq0")
-        w4_b00 = rounded([w4_raw[0, 0]], "w4_b00", "v2_w")
-        w4_b10 = rounded([w4_raw[1, 0]], "w4_b10", "v2_s")
-        w4_b1 = rounded([w4_raw[0, 1], w4_raw[1, 1]], "w4_b1", "w2q1_codes")
+        w4_b00 = rounded(w4_raw0[:, :, 0:KP], "w4_b00", "v2_w")
+        w4_b1 = held([P, 2 * PACK * S], BF16, "w4_b1", "w2q1_codes")
+        round_weight(w4_raw0[:, :, KP : 2 * KP], w4_b1[:, 0 : PACK * S])
+        w4_b10 = rounded(w4_raw10[:], "w4_b10", "v2_s")
+        for i in range(2):
+            round_weight(w4_raw11[i][:], w4_b1[:, PACK * S : 2 * PACK * S], P // 2 * i)
         h_b1 = h_rounded(1, "w3_w")
         damped(1, "travel0", range(3))
         hq[1] = quantize(h_b1, "hq1")
@@ -255,12 +262,14 @@ def tile_list_rupture_site_features_kernel(
             y_passes(1, 1, False, stop=True, slices=[t])
 
         def hand_out(g):
-            y = held([P, PACK, S], F32, f"y{g}", ("w4_raw11", "tab_w0")[g])
+            y = held([P, PACK, S], F32, f"y{g}", ("w4_raw111", "tab_w0")[g])
             rows = out_0[KP * g : KP * (g + 1), :].rearrange("(p t) s -> p t s", t=PACK)
             for t in range(PACK):
                 copy = nc.vector.tensor_copy if (g == 0 and t >= 2) else nc.scalar.copy
                 copy(out=y[:, t, :], in_=accs[g][t][:])
-                if t % 2 == 1:
+                if g == 0:
+                    nc.sync.dma_start(out=rows[:, t, :], in_=y[:, t, :])
+                elif t % 2 == 1:
                     nc.sync.dma_start(out=rows[:, t - 1 : t + 1, :], in_=y[:, t - 1 : t + 1, :])
             vals = held([P, PACK * S], BF16, f"y_b{g}", f"z_b{g}")
             codes = held([P, S], U32, f"y_codes{g}")
@@ -271,11 +280,13 @@ def tile_list_rupture_site_features_kernel(
             for cols in halves:
                 nc.vector.quantize_mx(out=codes[:, cols].bitcast(FP8X4), scales=y_scales[:, g, cols],
                                       in_=vals[:, PACK * cols.start : PACK * cols.stop])
-            nc.sync.dma_start(out=out_1[g].rearrange("p m t -> p (m t)").bitcast(I32), in_=codes[:].bitcast(I32))
+            for cols in (halves if g == 1 else [slice(0, S)]):
+                nc.sync.dma_start(out=out_1[g, :, cols, :].rearrange("p m t -> p (m t)").bitcast(I32),
+                                  in_=codes[:, cols].bitcast(I32))
 
         hand_out(0)
         hand_out(1)
         for r in range(4):
-            nc.scalar.dma_start(
+            (nc.scalar if r < 3 else nc.sync).dma_start(
                 out=out_2[:, r:16:4, :].rearrange("g q m -> q g m").bitcast(I32),
                 in_=y_scales[r:P:32].bitcast(I32))

@@ -89,13 +89,10 @@ def tile_list_rupture_site_features_kernel(
         w_s = held([P, 2, H], U8, "w_s")
         tab2_w = held([P, T2], U16, "tab2_w")
         gain_sb = held([P, 2, PACK], F32, "gain_sb")
-        warm = held([P, 8], F32, "warm")
 
         clear(nc.vector, tab_s)
         clear(nc.vector, tab2_s)
         clear(nc.vector, w_s)
-        nc.vector.memset(warm[:], 0.0)
-        nc.scalar.activation(out=warm[:], in_=warm[:], func=ACT.Sigmoid)
 
         def load_tab(a):
             words = held([P, T], I32, "tab_w0") if a == 0 else late.tile([P, T], I32, name="tab_w1", offset=0, align_bytes=64)

@@ -18,7 +18,6 @@ PACK = 4
 KP = P * PACK
 K, K2, T, T2, S, H, N = 1024, 512, 2048, 1024, 512, 1024, 1024
 FLOPS = 2 * S * (K * H + K2 * H + 2 * H * N)
-W3_ROW = 4
 
 
 def tile_list_rupture_site_features_kernel(
@@ -30,7 +29,6 @@ def tile_list_rupture_site_features_kernel(
     with ExitStack() as ctx:
         lists = ctx.enter_context(tc.tile_pool(name="lists", bufs=1))
         keep = ctx.enter_context(tc.tile_pool(name="keep", bufs=1))
-        late = ctx.enter_context(tc.tile_pool(name="late", bufs=1))
         psum = ctx.enter_context(tc.psum_pool(name="psum", bufs=1))
 
         def held(shape, dtype, name, slot=None):
@@ -42,10 +40,10 @@ def tile_list_rupture_site_features_kernel(
         def clear(engine, plane):
             engine.memset(plane[:].rearrange("p a n -> p (a n)").bitcast(I32), 0)
 
-        def load_scale_rows(queue, plane, scales, first=0, rows=range(4)):
-            for r in rows:
-                queue.dma_start(out=plane[first + r : P : 32].bitcast(I32),
-                                in_=scales[:, r:16:4, :].rearrange("a q n -> q a n").bitcast(I32))
+        def load_scale_rows(plane, scales):
+            for r in range(4):
+                nc.sync.dma_start(out=plane[r:P:32].bitcast(I32),
+                                  in_=scales[:, r:16:4, :].rearrange("a q n -> q a n").bitcast(I32))
 
         def load_rows(name, src):
             rows = held([P, PACK, src.shape[1]], F32, name)
@@ -86,16 +84,18 @@ def tile_list_rupture_site_features_kernel(
         offs2_sb = lists.tile([P, S // 16], U16, name="offs2_sb")
         tab_s = held([P, 2, T], U8, "tab_s")
         tab2_s = held([P, 1, T2], U8, "tab2_s")
-        w_s = held([P, 2, H], U8, "w_s")
+        w1_s = held([P, 2, H], U8, "w1_s")
+        w3_s = held([P, 1, N], U8, "w3_s")
         tab2_w = held([P, T2], U16, "tab2_w")
         gain_sb = held([P, 2, PACK], F32, "gain_sb")
 
         clear(nc.vector, tab_s)
         clear(nc.vector, tab2_s)
-        clear(nc.vector, w_s)
+        clear(nc.vector, w1_s)
+        clear(nc.vector, w3_s)
 
         def load_tab(a):
-            words = held([P, T], I32, "tab_w0") if a == 0 else late.tile([P, T], I32, name="tab_w1", offset=0, align_bytes=64)
+            words = held([P, T], I32, f"tab_w{a}")
             nc.sync.dma_start(out=words[:], in_=tab_words[a].rearrange("p n t -> p (n t)").bitcast(I32))
             return words
 
@@ -110,25 +110,26 @@ def tile_list_rupture_site_features_kernel(
         nc.sync.dma_start(offs2_sb[:], offs2)
         nc.sync.dma_start(out=tab2_w[:].bitcast(I32), in_=tab2_words[0].bitcast(I32))
         nc.sync.dma_start(offs_sb[:], offs)
-        load_scale_rows(nc.sync, tab_s, tab_scales)
+        load_scale_rows(tab_s, tab_scales)
         w2_raw[0] = load_rows("w2_raw0", w2[:, 0:KP])
-        load_scale_rows(nc.sync, tab2_s, tab2_scales)
+        load_scale_rows(tab2_s, tab2_scales)
         w1_w = [load_w1(0), None]
-        load_scale_rows(nc.sync, w_s, w3_scales, W3_ROW, range(1))
         tab_w = [load_tab(0), None]
-        load_scale_rows(nc.sync, w_s, w3_scales, W3_ROW, range(1, 3))
-        load_scale_rows(nc.gpsimd, w_s, w3_scales, W3_ROW, range(3, 4))
-        load_scale_rows(nc.sync, w_s, w1_scales)
+        load_scale_rows(w1_s, w1_scales)
         tab_w[1] = load_tab(1)
         w1_w[1] = load_w1(1)
+        for q in range(4):
+            nc.sync.dma_start(out=w3_s[32 * q : 32 * q + 8, 0, :].bitcast(I32),
+                              in_=w3_scales[:, 4 * q : 4 * q + 4, :].bitcast(I32))
         nc.sync.dma_start(out=gain_sb[:], in_=gain.rearrange("(b p t) -> p b t", b=2, t=PACK))
         w2_raw[1] = load_rows("w2_raw1", w2[:, KP : 2 * KP])
         travel_sb[0] = load_rows("travel0", travel[0:KP, :])
         w3_w = held([P, 2, N], I32, "w3_w")
         nc.sync.dma_start(out=w3_w[:], in_=w3_words.rearrange("a p n t -> p a (n t)").bitcast(I32))
-        w4_raw0 = load_rows("w4_raw0", w4[0:KP, :])
-        travel_sb[1] = load_rows("travel1", travel[KP : 2 * KP, :])
+        w4_raw00 = load_rows("w4_raw00", w4[0:KP, 0:KP])
         w4_raw10 = load_rows("w4_raw10", w4[KP : 2 * KP, 0:KP])
+        w4_raw01 = load_rows("w4_raw01", w4[0:KP, KP : 2 * KP])
+        travel_sb[1] = load_rows("travel1", travel[KP : 2 * KP, :])
         w4_raw11 = [load_rows(f"w4_raw11{i}", w4[KP : 2 * KP, KP + KP // 2 * i : KP + KP // 2 * (i + 1)])
                     for i in range(2)]
 
@@ -136,8 +137,8 @@ def tile_list_rupture_site_features_kernel(
         v2_s = held([P, S], U8, "v2_s")
         v_s = [held([P, S], U8, f"v_s{a}") for a in range(2)]
         v_w = [held([P, S], U32, f"v_w{a}") for a in range(2)]
-        w1d_w = [held([P, 2, KP], U16, "w1d_w0"), late.tile([P, 2, KP], U16, name="w1d_w1", offset=0, align_bytes=64)]
-        wd_s = [held([P, 2, KP], U8, "wd_s0"), late.tile([P, 2, KP], U8, name="wd_s1", offset=2048, align_bytes=64)]
+        w1d_w = [held([P, 2, KP], U16, f"w1d_w{b}") for b in range(2)]
+        w1d_s = [held([P, 2, KP], U8, f"w1d_s{b}") for b in range(2)]
         sat, damp, part, w2_q, w4_q, hq, zq, w3d_w = {}, {}, {}, {}, {}, {}, {}, {}
 
         def slip(b, slot):
@@ -147,7 +148,7 @@ def tile_list_rupture_site_features_kernel(
                 for t in range(PACK):
                     cols = slice(P * t, P * (t + 1))
                     nc.tensor.matmul_mx(out=accs[t][:], lhsT=w1d_w[b][:, a, cols].bitcast(FP4X4),
-                                        lhsT_scale=wd_s[b][:, a, cols],
+                                        lhsT_scale=w1d_s[b][:, a, cols],
                                         rhs=v_w[a][:].bitcast(FP8X4), rhs_scale=v_s[a][:],
                                         start=(a == 0), stop=(a == 1))
             for t in range(PACK):
@@ -196,10 +197,12 @@ def tile_list_rupture_site_features_kernel(
         w2_q[0] = quantize(rounded(w2_raw[0][:], "w2_b0", None), "w2q0", "tab2_s")
         site(0)
         nc.vector.tensor_copy(v_w[0][:], tab_w[0][:].bitcast(U32).indirect(offs_sb[:]))
-        deal(wd_s[0][:], w_s[:, :, 0:KP])
+        for b in range(2):
+            deal(w1d_s[b][:], w1_s[:, :, KP * b : KP * (b + 1)])
         nc.vector.tensor_copy(v_w[1][:], tab_w[1][:].bitcast(U32).indirect(offs_sb[:]))
         deal(w1d_w[1][:], w1_w[1][:])
-        deal(wd_s[1][:], w_s[:, :, KP : 2 * KP])
+        w3d_s = held([P, 2, KP], U8, "w3d_s")
+        deal(w3d_s[:], w3_s[:, 0, :].rearrange("p (g n) -> p g n", g=2))
 
         slip(0, None)
         w2_b1 = rounded(w2_raw[1][:], "w2_b1", "w1d_w0")
@@ -214,10 +217,10 @@ def tile_list_rupture_site_features_kernel(
             w3d_w[g] = held([P, 2, KP], I32, f"w3d_w{g}")
             deal_by_pairs(w3d_w[g][:], w3_w[:, :, KP * g : KP * (g + 1)])
         zq[0] = quantize(z_b0, "zq0")
-        w4_b00 = rounded(w4_raw0[:, :, 0:KP], "w4_b00", "v2_w")
-        w4_b1 = held([P, 2 * PACK * S], BF16, "w4_b1", "w2q1_codes")
-        round_weight(w4_raw0[:, :, KP : 2 * KP], w4_b1[:, 0 : PACK * S])
+        w4_b00 = rounded(w4_raw00[:], "w4_b00", "v2_w")
         w4_b10 = rounded(w4_raw10[:], "w4_b10", "v2_s")
+        w4_b1 = held([P, 2 * PACK * S], BF16, "w4_b1", "w2q1_codes")
+        round_weight(w4_raw01[:], w4_b1[:, 0 : PACK * S])
         for i in range(2):
             round_weight(w4_raw11[i][:], w4_b1[:, PACK * S : 2 * PACK * S], P // 2 * i)
         h_b1 = h_rounded(1, "w3_w")
@@ -240,7 +243,7 @@ def tile_list_rupture_site_features_kernel(
             for t in slices:
                 cols = slice(P * t, P * (t + 1))
                 if from_h:
-                    lw, ls = w3d_w[g][:, a, cols], wd_s[g][W3_ROW:P, a, cols]
+                    lw, ls = w3d_w[g][:, a, cols], w3d_s[4 * a : P, g, cols]
                     rw, rs = hq[a]
                 else:
                     lw, ls = w4_q[a, g][0][:, cols], w4_q[a, g][1][:, cols]

@@ -16,8 +16,13 @@ ALU = mybir.AluOpType
 P = 128
 PACK = 4
 KP = P * PACK
+QUAD = 32
+LIVE = 4
 K, K2, T, T2, S, H, N = 1024, 512, 2048, 1024, 512, 1024, 1024
 FLOPS = 2 * S * (K * H + K2 * H + 2 * H * N)
+WOVEN = PACK * S
+PAIR = 2
+VECTOR_BANKS = (2, 3)
 
 
 def tile_list_rupture_site_features_kernel(
@@ -37,13 +42,16 @@ def tile_list_rupture_site_features_kernel(
         def bank(name, number):
             return psum.tile([P, S], F32, name=name, tag=f"bank{number}")
 
-        def clear(engine, plane):
-            engine.memset(plane[:].rearrange("p a n -> p (a n)").bitcast(I32), 0)
+        def half(b):
+            return slice(KP * b, KP * (b + 1))
+
+        def clear(plane):
+            nc.vector.memset(plane[:].rearrange("p a n -> p (a n)").bitcast(I32), 0)
 
         def load_scale_rows(plane, scales):
-            for r in range(4):
-                nc.sync.dma_start(out=plane[r:P:32].bitcast(I32),
-                                  in_=scales[:, r:16:4, :].rearrange("a q n -> q a n").bitcast(I32))
+            for r in range(LIVE):
+                nc.sync.dma_start(out=plane[r:P:QUAD].bitcast(I32),
+                                  in_=scales[:, r : LIVE * LIVE : LIVE, :].rearrange("a q n -> q a n").bitcast(I32))
 
         def load_rows(name, src):
             rows = held([P, PACK, src.shape[1]], F32, name)
@@ -57,14 +65,19 @@ def tile_list_rupture_site_features_kernel(
 
         def deal_by_pairs(dst, src):
             nc.vector.tensor_copy(
-                out=dst.rearrange("p a (t c i) -> p a c t i", t=PACK, i=2),
-                in_=src.rearrange("p a (c i t) -> p a c t i", t=PACK, i=2))
+                out=dst.rearrange("p a (t c i) -> p a c t i", t=PACK, i=PAIR),
+                in_=src.rearrange("p a (c i t) -> p a c t i", t=PACK, i=PAIR))
 
         def round_weight(raw, vals, first=0):
             count = raw.shape[2] // PACK
             nc.scalar.copy(
                 out=vals.rearrange("p (u v m j) -> p u m j v", u=2, v=2, j=PACK)[:, :, first : first + count],
                 in_=raw.rearrange("p j (m u v) -> p u m j v", u=2, v=2))
+
+        def rounded(raw, name, slot=None):
+            vals = held([P, WOVEN], BF16, name, slot)
+            round_weight(raw[:], vals[:])
+            return vals
 
         def quantize(vals, name, slot=None):
             width = vals.shape[1] // PACK
@@ -73,12 +86,11 @@ def tile_list_rupture_site_features_kernel(
             nc.vector.quantize_mx(out=codes[:].bitcast(FP8X4), scales=scales[:], in_=vals[:])
             return codes, scales
 
-        def woven(vals, run):
-            return vals.rearrange("p (c i t) -> p c t i", i=run, t=PACK)
+        def woven(vals):
+            return vals.rearrange("p (c i t) -> p c t i", i=PAIR, t=PACK)
 
-        def by_runs(rows, run):
-            return rows.rearrange("p t (c i) -> p c t i", i=run)
-
+        def by_pairs(rows):
+            return rows.rearrange("p t (c i) -> p c t i", i=PAIR)
 
         offs_sb = lists.tile([P, S // 16], U16, name="offs_sb")
         offs2_sb = lists.tile([P, S // 16], U16, name="offs2_sb")
@@ -88,11 +100,8 @@ def tile_list_rupture_site_features_kernel(
         w3_s = held([P, 1, N], U8, "w3_s")
         tab2_w = held([P, T2], U16, "tab2_w")
         gain_sb = held([P, 2, PACK], F32, "gain_sb")
-
-        clear(nc.vector, tab_s)
-        clear(nc.vector, tab2_s)
-        clear(nc.vector, w1_s)
-        clear(nc.vector, w3_s)
+        for plane in (tab_s, tab2_s, w1_s, w3_s):
+            clear(plane)
 
         def load_tab(a):
             words = held([P, T], I32, f"tab_w{a}")
@@ -101,36 +110,35 @@ def tile_list_rupture_site_features_kernel(
 
         def load_w1(b):
             words = held([P, 2, KP], U16, f"w1_w{b}")
-            nc.sync.dma_start(
-                out=words[:].bitcast(I32),
-                in_=w1_words[:, :, 2 * KP * b : 2 * KP * (b + 1)].rearrange("a p n -> p a n").bitcast(I32))
+            nc.sync.dma_start(out=words[:].bitcast(I32),
+                              in_=w1_words[:, :, 2 * KP * b : 2 * KP * (b + 1)].rearrange("a p n -> p a n").bitcast(I32))
             return words
 
-        w2_raw, travel_sb = {}, {}
+        w2_raw, travel_sb, w1_w, tab_w = {}, {}, {}, {}
         nc.sync.dma_start(offs2_sb[:], offs2)
         nc.sync.dma_start(out=tab2_w[:].bitcast(I32), in_=tab2_words[0].bitcast(I32))
         nc.sync.dma_start(offs_sb[:], offs)
         load_scale_rows(tab_s, tab_scales)
-        w2_raw[0] = load_rows("w2_raw0", w2[:, 0:KP])
+        w2_raw[0] = load_rows("w2_raw0", w2[:, half(0)])
         load_scale_rows(tab2_s, tab2_scales)
-        w1_w = [load_w1(0), None]
-        tab_w = [load_tab(0), None]
+        w1_w[0] = load_w1(0)
+        tab_w[0] = load_tab(0)
         load_scale_rows(w1_s, w1_scales)
         tab_w[1] = load_tab(1)
         w1_w[1] = load_w1(1)
-        for q in range(4):
-            nc.sync.dma_start(out=w3_s[32 * q : 32 * q + 8, 0, :].bitcast(I32),
-                              in_=w3_scales[:, 4 * q : 4 * q + 4, :].bitcast(I32))
+        for q in range(P // QUAD):
+            nc.sync.dma_start(out=w3_s[QUAD * q : QUAD * q + 2 * LIVE, 0, :].bitcast(I32),
+                              in_=w3_scales[:, LIVE * q : LIVE * (q + 1), :].bitcast(I32))
         nc.sync.dma_start(out=gain_sb[:], in_=gain.rearrange("(b p t) -> p b t", b=2, t=PACK))
-        w2_raw[1] = load_rows("w2_raw1", w2[:, KP : 2 * KP])
-        travel_sb[0] = load_rows("travel0", travel[0:KP, :])
+        w2_raw[1] = load_rows("w2_raw1", w2[:, half(1)])
+        travel_sb[0] = load_rows("travel0", travel[half(0), :])
         w3_w = held([P, 2, N], I32, "w3_w")
         nc.sync.dma_start(out=w3_w[:], in_=w3_words.rearrange("a p n t -> p a (n t)").bitcast(I32))
-        w4_raw00 = load_rows("w4_raw00", w4[0:KP, 0:KP])
-        w4_raw10 = load_rows("w4_raw10", w4[KP : 2 * KP, 0:KP])
-        w4_raw01 = load_rows("w4_raw01", w4[0:KP, KP : 2 * KP])
-        travel_sb[1] = load_rows("travel1", travel[KP : 2 * KP, :])
-        w4_raw11 = [load_rows(f"w4_raw11{i}", w4[KP : 2 * KP, KP + KP // 2 * i : KP + KP // 2 * (i + 1)])
+        w4_raw00 = load_rows("w4_raw00", w4[half(0), half(0)])
+        w4_raw10 = load_rows("w4_raw10", w4[half(1), half(0)])
+        w4_raw01 = load_rows("w4_raw01", w4[half(0), half(1)])
+        travel_sb[1] = load_rows("travel1", travel[half(1), :])
+        w4_raw11 = [load_rows(f"w4_raw11{i}", w4[half(1), KP + KP // 2 * i : KP + KP // 2 * (i + 1)])
                     for i in range(2)]
 
         v2_w = held([P, S], U16, "v2_w")
@@ -141,7 +149,7 @@ def tile_list_rupture_site_features_kernel(
         w1d_s = [held([P, 2, KP], U8, f"w1d_s{b}") for b in range(2)]
         sat, damp, part, w2_q, w4_q, hq, zq, w3d_w = {}, {}, {}, {}, {}, {}, {}, {}
 
-        def slip(b, slot):
+        def slip(b, slot=None):
             sat[b] = held([P, PACK, S], F32, f"sat{b}", slot)
             accs = [bank(f"slip{b}{t}", PACK * (1 - b) + t) for t in range(PACK)]
             for a in range(2):
@@ -164,29 +172,22 @@ def tile_list_rupture_site_features_kernel(
                                     rhs=v2_w[:].bitcast(FP4X4), rhs_scale=v2_s[:], start=True, stop=True)
                 nc.scalar.activation(out=damp[b][:, t, :], in_=acc[:], func=ACT.Sigmoid, scale=-1.0)
 
-        def damped(b, slot, slices=range(PACK)):
-            if b not in part:
-                part[b] = held([P, PACK, S], F32, f"part{b}", slot)
+        def damped(b, slices):
             for t in slices:
                 nc.vector.scalar_tensor_tensor(
                     out=part[b][:, t, :], in0=sat[b][:, t, :], scalar=gain_sb[:, b, t : t + 1],
                     in1=damp[b][:, t, :], op0=ALU.mult, op1=ALU.mult)
 
-        def h_rounded(b, slot):
-            vals = held([P, PACK * S], BF16, f"h_b{b}", slot)
-            gains = gain_sb[:, b, :].unsqueeze(1).unsqueeze(3).to_broadcast([P, S // 2, PACK, 2])
-            nc.vector.tensor_tensor(out=woven(vals[:], 2), in0=by_runs(sat[b][:], 2), in1=gains, op=ALU.mult)
+        def h_rounded(b, slot=None):
+            vals = held([P, WOVEN], BF16, f"h_b{b}", slot)
+            gains = gain_sb[:, b, :].unsqueeze(1).unsqueeze(3).to_broadcast([P, S // PAIR, PACK, PAIR])
+            nc.vector.tensor_tensor(out=woven(vals[:]), in0=by_pairs(sat[b][:]), in1=gains, op=ALU.mult)
             return vals
 
         def z_rounded(b):
-            vals = held([P, PACK * S], BF16, f"z_b{b}")
-            nc.vector.tensor_tensor(out=woven(vals[:], 2), in0=by_runs(part[b][:], 2), in1=by_runs(travel_sb[b][:], 2),
+            vals = held([P, WOVEN], BF16, f"z_b{b}")
+            nc.vector.tensor_tensor(out=woven(vals[:]), in0=by_pairs(part[b][:]), in1=by_pairs(travel_sb[b][:]),
                                     op=ALU.add)
-            return vals
-
-        def rounded(raw, name, slot):
-            vals = held([P, PACK * S], BF16, name, slot)
-            round_weight(raw, vals[:])
             return vals
 
         nc.vector.tensor_copy(v2_w[:], tab2_w[:].indirect(offs2_sb[:]))
@@ -194,20 +195,21 @@ def tile_list_rupture_site_features_kernel(
             nc.vector.tensor_copy(v_s[a][:], tab_s[:, a, :].indirect(offs_sb[:]))
         nc.vector.tensor_copy(v2_s[:], tab2_s[:, 0, :].indirect(offs2_sb[:]))
         deal(w1d_w[0][:], w1_w[0][:])
-        w2_q[0] = quantize(rounded(w2_raw[0][:], "w2_b0", None), "w2q0", "tab2_s")
+        w2_q[0] = quantize(rounded(w2_raw[0], "w2_b0"), "w2q0", "tab2_s")
         site(0)
         nc.vector.tensor_copy(v_w[0][:], tab_w[0][:].bitcast(U32).indirect(offs_sb[:]))
         for b in range(2):
-            deal(w1d_s[b][:], w1_s[:, :, KP * b : KP * (b + 1)])
+            deal(w1d_s[b][:], w1_s[:, :, half(b)])
         nc.vector.tensor_copy(v_w[1][:], tab_w[1][:].bitcast(U32).indirect(offs_sb[:]))
         deal(w1d_w[1][:], w1_w[1][:])
         w3d_s = held([P, 2, KP], U8, "w3d_s")
         deal(w3d_s[:], w3_s[:, 0, :].rearrange("p (g n) -> p g n", g=2))
 
-        slip(0, None)
-        w2_b1 = rounded(w2_raw[1][:], "w2_b1", "w1d_w0")
-        damped(0, None)
-        h_b0 = h_rounded(0, None)
+        slip(0)
+        w2_b1 = rounded(w2_raw[1], "w2_b1", "w1d_w0")
+        part[0] = held([P, PACK, S], F32, "part0")
+        damped(0, range(PACK))
+        h_b0 = h_rounded(0)
         w2_q[1] = quantize(w2_b1, "w2q1")
         slip(1, "w2_raw1")
         site(1)
@@ -215,78 +217,80 @@ def tile_list_rupture_site_features_kernel(
         hq[0] = quantize(h_b0, "hq0")
         for g in range(2):
             w3d_w[g] = held([P, 2, KP], I32, f"w3d_w{g}")
-            deal_by_pairs(w3d_w[g][:], w3_w[:, :, KP * g : KP * (g + 1)])
+            deal_by_pairs(w3d_w[g][:], w3_w[:, :, half(g)])
         zq[0] = quantize(z_b0, "zq0")
-        w4_b00 = rounded(w4_raw00[:], "w4_b00", "v2_w")
-        w4_b10 = rounded(w4_raw10[:], "w4_b10", "v2_s")
-        w4_b1 = held([P, 2 * PACK * S], BF16, "w4_b1", "w2q1_codes")
-        round_weight(w4_raw01[:], w4_b1[:, 0 : PACK * S])
+
+        w4_b00 = rounded(w4_raw00, "w4_b00", "v2_w")
+        w4_b10 = rounded(w4_raw10, "w4_b10", "v2_s")
+        w4_b01 = rounded(w4_raw01, "w4_b01", "w2q1_codes")
+        w4_b11 = held([P, WOVEN], BF16, "w4_b11", "w2q1_scales")
         for i in range(2):
-            round_weight(w4_raw11[i][:], w4_b1[:, PACK * S : 2 * PACK * S], P // 2 * i)
+            round_weight(w4_raw11[i][:], w4_b11[:], P // 2 * i)
+
         h_b1 = h_rounded(1, "w3_w")
-        damped(1, "travel0", range(3))
+        part[1] = held([P, PACK, S], F32, "part1", "travel0")
+        damped(1, range(PACK - 1))
         hq[1] = quantize(h_b1, "hq1")
-        damped(1, None, range(3, PACK))
+        damped(1, [PACK - 1])
         w4_q[0, 0] = quantize(w4_b00, "w4q00")
         z_b1 = z_rounded(1)
         w4_q[1, 0] = quantize(w4_b10, "w4q10")
         zq[1] = quantize(z_b1, "zq1")
-        codes, scales = quantize(w4_b1, "w4q1")
-        for a in range(2):
-            w4_q[a, 1] = codes[:, S * a : S * (a + 1)], scales[:, S * a : S * (a + 1)]
+        w4_q[0, 1] = quantize(w4_b01, "w4q01", "travel1")
+        w4_q[1, 1] = quantize(w4_b11, "w4q11")
 
         y_scales = held([P, 2, S], U8, "y_scales")
-
-        accs = [[bank(f"y{g}{t}", PACK * g + t) for t in range(PACK)] for g in range(2)]
+        y_accs = [[bank(f"y{g}{t}", PACK * g + t) for t in range(PACK)] for g in range(2)]
 
         def y_passes(g, a, from_h, start=False, stop=False, slices=range(PACK)):
             for t in slices:
                 cols = slice(P * t, P * (t + 1))
                 if from_h:
-                    lw, ls = w3d_w[g][:, a, cols], w3d_s[4 * a : P, g, cols]
+                    lw, ls = w3d_w[g][:, a, cols], w3d_s[LIVE * a : P, g, cols]
                     rw, rs = hq[a]
                 else:
                     lw, ls = w4_q[a, g][0][:, cols], w4_q[a, g][1][:, cols]
                     rw, rs = zq[a]
-                nc.tensor.matmul_mx(out=accs[g][t][:], lhsT=lw.bitcast(FP8X4), lhsT_scale=ls,
+                nc.tensor.matmul_mx(out=y_accs[g][t][:], lhsT=lw.bitcast(FP8X4), lhsT_scale=ls,
                                     rhs=rw[:].bitcast(FP8X4), rhs_scale=rs[:], start=start, stop=stop)
 
-        y_passes(0, 0, True, start=True)
-        y_passes(1, 0, True, start=True)
-        y_passes(0, 1, True)
-        y_passes(1, 1, True)
-        y_passes(0, 0, False)
-        y_passes(0, 1, False, stop=True)
+        for a in range(2):
+            for g in range(2):
+                y_passes(g, a, True, start=(a == 0))
+        for a in range(2):
+            y_passes(0, a, False, stop=(a == 1))
         for t in range(PACK):
-            y_passes(1, 0, False, slices=[t])
-            y_passes(1, 1, False, stop=True, slices=[t])
+            for a in (1, 0):
+                y_passes(1, a, False, stop=(a == 0), slices=[t])
 
-        def hand_out(g):
-            y = held([P, PACK, S], F32, f"y{g}", ("w4_raw111", "tab_w0")[g])
-            rows = out_0[KP * g : KP * (g + 1), :].rearrange("(p t) s -> p t s", t=PACK)
+        def hand_out(g, slot, banks_a_store, code_stores):
+            y = held([P, PACK, S], F32, f"y{g}", slot)
+            rows = out_0[half(g), :].rearrange("(p t) s -> p t s", t=PACK)
             for t in range(PACK):
-                copy = nc.vector.tensor_copy if (g == 0 and t >= 2) else nc.scalar.copy
-                copy(out=y[:, t, :], in_=accs[g][t][:])
-                if g == 0:
+                copy = nc.vector.tensor_copy if (g == 0 and t in VECTOR_BANKS) else nc.scalar.copy
+                copy(out=y[:, t, :], in_=y_accs[g][t][:])
+                if banks_a_store == 1:
                     nc.sync.dma_start(out=rows[:, t, :], in_=y[:, t, :])
-                elif t % 2 == 1:
-                    nc.sync.dma_start(out=rows[:, t - 1 : t + 1, :], in_=y[:, t - 1 : t + 1, :])
-            vals = held([P, PACK * S], BF16, f"y_b{g}", f"z_b{g}")
+                elif (t + 1) % banks_a_store == 0:
+                    done = slice(t + 1 - banks_a_store, t + 1)
+                    nc.sync.dma_start(out=rows[:, done, :], in_=y[:, done, :])
+            vals = held([P, WOVEN], BF16, f"y_b{g}", f"z_b{g}")
             codes = held([P, S], U32, f"y_codes{g}")
-            halves = [slice(S // 2 * i, S // 2 * (i + 1)) for i in range(2)]
-            for cols in halves:
-                nc.vector.tensor_copy(out=woven(vals[:, PACK * cols.start : PACK * cols.stop], 2),
-                                      in_=by_runs(y[:, :, cols], 2))
-            for cols in halves:
+            entries = [slice(S // 2 * i, S // 2 * (i + 1)) for i in range(2)]
+            for cols in entries:
+                nc.vector.tensor_copy(out=woven(vals[:, PACK * cols.start : PACK * cols.stop]),
+                                      in_=by_pairs(y[:, :, cols]))
+            for cols in entries:
                 nc.vector.quantize_mx(out=codes[:, cols].bitcast(FP8X4), scales=y_scales[:, g, cols],
                                       in_=vals[:, PACK * cols.start : PACK * cols.stop])
-            for cols in (halves if g == 1 else [slice(0, S)]):
+            for i in range(code_stores):
+                cols = slice(S // code_stores * i, S // code_stores * (i + 1))
                 nc.sync.dma_start(out=out_1[g, :, cols, :].rearrange("p m t -> p (m t)").bitcast(I32),
                                   in_=codes[:, cols].bitcast(I32))
 
-        hand_out(0)
-        hand_out(1)
-        for r in range(4):
-            (nc.scalar if r < 3 else nc.sync).dma_start(
-                out=out_2[:, r:16:4, :].rearrange("g q m -> q g m").bitcast(I32),
-                in_=y_scales[r:P:32].bitcast(I32))
+        hand_out(0, "w4_raw111", banks_a_store=1, code_stores=1)
+        hand_out(1, "tab_w0", banks_a_store=2, code_stores=2)
+        for r in range(LIVE):
+            queue = nc.scalar if r < LIVE - 1 else nc.sync
+            queue.dma_start(out=out_2[:, r : LIVE * LIVE : LIVE, :].rearrange("g q m -> q g m").bitcast(I32),
+                            in_=y_scales[r:P:QUAD].bitcast(I32))

@@ -22,6 +22,14 @@ K, K2, T, T2, S, H, N = 1024, 512, 2048, 1024, 512, 1024, 1024
 FLOPS = 2 * S * (K * H + K2 * H + 2 * H * N)
 WOVEN = PACK * S
 PAIR = 2
+KIB = 1024
+TAB1_AT, W1W1_AT, W1S1_AT, W3S_AT, W2Q_AT, GAIN_AT = 0, 8 * KIB, 10 * KIB, 11 * KIB, 12 * KIB, 14 * KIB
+W2_AT = GAIN_AT + 64
+TABS_AT = W1W1_AT - KIB // 2
+TAB2S_AT = GAIN_AT - KIB // 2
+PART_AT = W2_AT + 10 * KIB
+LAST_AT = PART_AT + 8 * KIB
+SPREAD = 8
 VECTOR_BANKS = (2, 3)
 
 
@@ -34,10 +42,14 @@ def tile_list_rupture_site_features_kernel(
     with ExitStack() as ctx:
         lists = ctx.enter_context(tc.tile_pool(name="lists", bufs=1))
         keep = ctx.enter_context(tc.tile_pool(name="keep", bufs=1))
+        overlaid = ctx.enter_context(tc.tile_pool(name="overlaid", bufs=1))
         psum = ctx.enter_context(tc.psum_pool(name="psum", bufs=1))
 
         def held(shape, dtype, name, slot=None):
             return keep.tile(shape, dtype, name=name, tag=slot or name, align_bytes=64)
+
+        def placed(shape, dtype, name, offset):
+            return overlaid.tile(shape, dtype, name=name, align_bytes=64, offset=offset)
 
         def bank(name, number):
             return psum.tile([P, S], F32, name=name, tag=f"bank{number}")
@@ -48,18 +60,19 @@ def tile_list_rupture_site_features_kernel(
         def clear(plane):
             nc.vector.memset(plane[:].rearrange("p a n -> p (a n)").bitcast(I32), 0)
 
-        def load_scale_rows(plane, scales):
-            for r in range(LIVE):
+        def load_scale_rows(plane, scales, rows=range(LIVE)):
+            for r in rows:
                 nc.sync.dma_start(out=plane[r:P:QUAD].bitcast(I32),
                                   in_=scales[:, r : LIVE * LIVE : LIVE, :].rearrange("a q n -> q a n").bitcast(I32))
 
-        def load_rows(name, src):
-            rows = held([P, PACK, src.shape[1]], F32, name)
+        def load_rows(name, src, offset=None, slot=None):
+            shape = [P, PACK, src.shape[1]]
+            rows = held(shape, F32, name, slot) if offset is None else placed(shape, F32, name, offset)
             nc.sync.dma_start(out=rows[:], in_=src.rearrange("(p j) c -> p j c", j=PACK))
             return rows
 
-        def deal(dst, src):
-            nc.vector.tensor_copy(
+        def deal(dst, src, copy=nc.vector.tensor_copy):
+            copy(
                 out=dst.rearrange("p a (t m) -> p a t m", t=PACK),
                 in_=src.rearrange("p a (m t) -> p a t m", t=PACK))
 
@@ -79,9 +92,9 @@ def tile_list_rupture_site_features_kernel(
             round_weight(raw[:], vals[:])
             return vals
 
-        def quantize(vals, name, slot=None):
+        def quantize(vals, name, slot=None, offset=None):
             width = vals.shape[1] // PACK
-            codes = held([P, width], U32, name + "_codes", slot)
+            codes = held([P, width], U32, name + "_codes", slot) if offset is None else placed([P, width], U32, name + "_codes", offset)
             scales = held([P, width], U8, name + "_scales")
             nc.vector.quantize_mx(out=codes[:].bitcast(FP8X4), scales=scales[:], in_=vals[:])
             return codes, scales
@@ -94,22 +107,21 @@ def tile_list_rupture_site_features_kernel(
 
         offs_sb = lists.tile([P, S // 16], U16, name="offs_sb")
         offs2_sb = lists.tile([P, S // 16], U16, name="offs2_sb")
-        tab_s = held([P, 2, T], U8, "tab_s")
-        tab2_s = held([P, 1, T2], U8, "tab2_s")
+        tab_s = placed([P, 2, T], U8, "tab_s", TABS_AT)
+        tab2_s = placed([P, 1, T2], U8, "tab2_s", TAB2S_AT)
         w1_s = held([P, 2, H], U8, "w1_s")
-        w3_s = held([P, 1, N], U8, "w3_s")
+        v_s = held([P, 2, S], U8, "v_s")
         tab2_w = held([P, T2], U16, "tab2_w")
-        gain_sb = held([P, 2, PACK], F32, "gain_sb")
-        for plane in (tab_s, tab2_s, w1_s, w3_s):
+        for plane in (tab_s, tab2_s, w1_s, v_s):
             clear(plane)
 
         def load_tab(a):
-            words = held([P, T], I32, f"tab_w{a}")
+            words = placed([P, T], I32, "tab_w1", TAB1_AT) if a else held([P, T], I32, "tab_w0")
             nc.sync.dma_start(out=words[:], in_=tab_words[a].rearrange("p n t -> p (n t)").bitcast(I32))
             return words
 
         def load_w1(b):
-            words = held([P, 2, KP], U16, f"w1_w{b}")
+            words = placed([P, 2, KP], U16, "w1_w1", W1W1_AT) if b else held([P, 2, KP], U16, "w1_w0")
             nc.sync.dma_start(out=words[:].bitcast(I32),
                               in_=w1_words[:, :, 2 * KP * b : 2 * KP * (b + 1)].rearrange("a p n -> p a n").bitcast(I32))
             return words
@@ -118,46 +130,47 @@ def tile_list_rupture_site_features_kernel(
         nc.sync.dma_start(offs2_sb[:], offs2)
         nc.sync.dma_start(out=tab2_w[:].bitcast(I32), in_=tab2_words[0].bitcast(I32))
         nc.sync.dma_start(offs_sb[:], offs)
-        load_scale_rows(tab_s, tab_scales)
+        nc.sync.dma_start(out=tab_s[0:P:SPREAD].bitcast(I32), in_=tab_scales.rearrange("a q n -> q a n").bitcast(I32))
+        load_scale_rows(tab2_s, tab2_scales, range(LIVE - 1))
         w2_raw[0] = load_rows("w2_raw0", w2[:, half(0)])
-        load_scale_rows(tab2_s, tab2_scales)
+        load_scale_rows(tab2_s, tab2_scales, [LIVE - 1])
         w1_w[0] = load_w1(0)
-        tab_w[0] = load_tab(0)
         load_scale_rows(w1_s, w1_scales)
+        tab_w[0] = load_tab(0)
+        v2_w = held([P, S], U16, "v2_w")
+        v_g = held([P, 2, S], U8, "v_g")
+        nc.vector.tensor_copy(v2_w[:], tab2_w[:].indirect(offs2_sb[:]))
+        for a in range(2):
+            nc.vector.tensor_copy(v_g[:, a, :], tab_s[:, a, :].indirect(offs_sb[:]))
+        for r in range(LIVE):
+            nc.sync.dma_start(out=v_s[r:P:QUAD].bitcast(I32), in_=v_g[SPREAD * r : P : QUAD].bitcast(I32))
         tab_w[1] = load_tab(1)
         w1_w[1] = load_w1(1)
+        w3_s = placed([P, 1, N], U8, "w3_s", W1S1_AT)
+        clear(w3_s)
+        v2_s = held([P, S], U8, "v2_s")
+        nc.vector.tensor_copy(v2_s[:], tab2_s[:, 0, :].indirect(offs2_sb[:]))
+        gain_sb = placed([P, 2, PACK], F32, "gain_sb", GAIN_AT)
         for q in range(P // QUAD):
             nc.sync.dma_start(out=w3_s[QUAD * q : QUAD * q + 2 * LIVE, 0, :].bitcast(I32),
                               in_=w3_scales[:, LIVE * q : LIVE * (q + 1), :].bitcast(I32))
         nc.sync.dma_start(out=gain_sb[:], in_=gain.rearrange("(b p t) -> p b t", b=2, t=PACK))
-        w2_raw[1] = load_rows("w2_raw1", w2[:, half(1)])
-        travel_sb[0] = load_rows("travel0", travel[half(0), :])
-        w3_w = held([P, 2, N], I32, "w3_w")
-        nc.sync.dma_start(out=w3_w[:], in_=w3_words.rearrange("a p n t -> p a (n t)").bitcast(I32))
-        w4_raw00 = load_rows("w4_raw00", w4[half(0), half(0)])
-        w4_raw10 = load_rows("w4_raw10", w4[half(1), half(0)])
-        w4_raw01 = load_rows("w4_raw01", w4[half(0), half(1)])
-        travel_sb[1] = load_rows("travel1", travel[half(1), :])
-        w4_raw11 = [load_rows(f"w4_raw11{i}", w4[half(1), KP + KP // 2 * i : KP + KP // 2 * (i + 1)])
-                    for i in range(2)]
+        w2_raw[1] = load_rows("w2_raw1", w2[:, half(1)], W2_AT)
 
-        v2_w = held([P, S], U16, "v2_w")
-        v2_s = held([P, S], U8, "v2_s")
-        v_s = [held([P, S], U8, f"v_s{a}") for a in range(2)]
         v_w = [held([P, S], U32, f"v_w{a}") for a in range(2)]
-        w1d_w = [held([P, 2, KP], U16, f"w1d_w{b}") for b in range(2)]
+        w1d_w = [placed([P, 2, KP], U16, "w1d_w0", LAST_AT + 2 * KIB)]
         w1d_s = [held([P, 2, KP], U8, f"w1d_s{b}") for b in range(2)]
         sat, damp, part, w2_q, w4_q, hq, zq, w3d_w = {}, {}, {}, {}, {}, {}, {}, {}
 
-        def slip(b, slot=None):
-            sat[b] = held([P, PACK, S], F32, f"sat{b}", slot)
+        def slip(b, offset=None):
+            sat[b] = held([P, PACK, S], F32, f"sat{b}") if offset is None else placed([P, PACK, S], F32, f"sat{b}", offset)
             accs = [bank(f"slip{b}{t}", PACK * (1 - b) + t) for t in range(PACK)]
             for a in range(2):
                 for t in range(PACK):
                     cols = slice(P * t, P * (t + 1))
                     nc.tensor.matmul_mx(out=accs[t][:], lhsT=w1d_w[b][:, a, cols].bitcast(FP4X4),
                                         lhsT_scale=w1d_s[b][:, a, cols],
-                                        rhs=v_w[a][:].bitcast(FP8X4), rhs_scale=v_s[a][:],
+                                        rhs=v_w[a][:].bitcast(FP8X4), rhs_scale=v_s[:, a, :],
                                         start=(a == 0), stop=(a == 1))
             for t in range(PACK):
                 nc.scalar.activation(out=sat[b][:, t, :], in_=accs[t][:], func=ACT.Tanh)
@@ -184,41 +197,48 @@ def tile_list_rupture_site_features_kernel(
             nc.vector.tensor_tensor(out=woven(vals[:]), in0=by_pairs(sat[b][:]), in1=gains, op=ALU.mult)
             return vals
 
-        def z_rounded(b):
-            vals = held([P, WOVEN], BF16, f"z_b{b}")
+        def z_rounded(b, offset):
+            vals = placed([P, WOVEN], BF16, f"z_b{b}", offset)
             nc.vector.tensor_tensor(out=woven(vals[:]), in0=by_pairs(part[b][:]), in1=by_pairs(travel_sb[b][:]),
                                     op=ALU.add)
             return vals
 
-        nc.vector.tensor_copy(v2_w[:], tab2_w[:].indirect(offs2_sb[:]))
-        for a in range(2):
-            nc.vector.tensor_copy(v_s[a][:], tab_s[:, a, :].indirect(offs_sb[:]))
-        nc.vector.tensor_copy(v2_s[:], tab2_s[:, 0, :].indirect(offs2_sb[:]))
-        deal(w1d_w[0][:], w1_w[0][:])
-        w2_q[0] = quantize(rounded(w2_raw[0], "w2_b0"), "w2q0", "tab2_s")
-        site(0)
-        nc.vector.tensor_copy(v_w[0][:], tab_w[0][:].bitcast(U32).indirect(offs_sb[:]))
         for b in range(2):
             deal(w1d_s[b][:], w1_s[:, :, half(b)])
+        w2_q[0] = quantize(rounded(w2_raw[0], "w2_b0"), "w2q0", offset=W2Q_AT)
+        deal(w1d_w[0][:], w1_w[0][:])
+        site(0)
+        travel_sb[0] = load_rows("travel0", travel[half(0), :], slot="w2_raw0")
+        w3_w = held([P, 2, N], I32, "w3_w", "w2_b0")
+        nc.sync.dma_start(out=w3_w[:], in_=w3_words.rearrange("a p n t -> p a (n t)").bitcast(I32))
+        nc.vector.tensor_copy(v_w[0][:], tab_w[0][:].bitcast(U32).indirect(offs_sb[:]))
+        w4_raw00 = load_rows("w4_raw00", w4[half(0), half(0)], slot="tab_w0")
         nc.vector.tensor_copy(v_w[1][:], tab_w[1][:].bitcast(U32).indirect(offs_sb[:]))
+        w1d_w.append(held([P, 2, KP], U16, "w1d_w1"))
         deal(w1d_w[1][:], w1_w[1][:])
         w3d_s = held([P, 2, KP], U8, "w3d_s")
         deal(w3d_s[:], w3_s[:, 0, :].rearrange("p (g n) -> p g n", g=2))
 
         slip(0)
-        w2_b1 = rounded(w2_raw[1], "w2_b1", "w1d_w0")
-        part[0] = held([P, PACK, S], F32, "part0")
+        w2_b1 = placed([P, WOVEN], BF16, "w2_b1", LAST_AT + 2 * KIB)
+        round_weight(w2_raw[1][:], w2_b1[:])
+        part[0] = placed([P, PACK, S], F32, "part0", PART_AT)
         damped(0, range(PACK))
+        w4_raw10 = load_rows("w4_raw10", w4[half(1), half(0)], slot="damp0")
         h_b0 = h_rounded(0)
+        w4_raw01 = load_rows("w4_raw01", w4[half(0), half(1)], slot="sat0")
         w2_q[1] = quantize(w2_b1, "w2q1")
-        slip(1, "w2_raw1")
+        slip(1, W2_AT + 4 * S)
         site(1)
-        z_b0 = z_rounded(0)
-        hq[0] = quantize(h_b0, "hq0")
+        hq[0] = quantize(h_b0, "hq0", offset=W2_AT)
+        z_b0 = z_rounded(0, LAST_AT + 2 * KIB)
+        travel_sb[1] = load_rows("travel1", travel[half(1), :], PART_AT)
         for g in range(2):
             w3d_w[g] = held([P, 2, KP], I32, f"w3d_w{g}")
             deal_by_pairs(w3d_w[g][:], w3_w[:, :, half(g)])
         zq[0] = quantize(z_b0, "zq0")
+        w4_raw11 = [load_rows(f"w4_raw11{i}", w4[half(1), KP + KP // 2 * i : KP + KP // 2 * (i + 1)],
+                              LAST_AT + 4 * KIB * i) for i in range(2)]
 
         w4_b00 = rounded(w4_raw00, "w4_b00", "v2_w")
         w4_b10 = rounded(w4_raw10, "w4_b10", "v2_s")
@@ -227,16 +247,23 @@ def tile_list_rupture_site_features_kernel(
         for i in range(2):
             round_weight(w4_raw11[i][:], w4_b11[:], P // 2 * i)
 
-        h_b1 = h_rounded(1, "w3_w")
-        part[1] = held([P, PACK, S], F32, "part1", "travel0")
+        h_b1 = h_rounded(1, "w2_b0")
+        part[1] = held([P, PACK, S], F32, "part1", "w2_raw0")
         damped(1, range(PACK - 1))
         hq[1] = quantize(h_b1, "hq1")
         damped(1, [PACK - 1])
         w4_q[0, 0] = quantize(w4_b00, "w4q00")
-        z_b1 = z_rounded(1)
         w4_q[1, 0] = quantize(w4_b10, "w4q10")
-        zq[1] = quantize(z_b1, "zq1")
-        w4_q[0, 1] = quantize(w4_b01, "w4q01", "travel1")
+        z_b1 = held([P, WOVEN], BF16, "z_b1")
+        zq[1] = held([P, S], U32, "zq1_codes"), held([P, S], U8, "zq1_scales")
+        entries = [slice(S // 2 * e, S // 2 * (e + 1)) for e in range(2)]
+        for cols in entries:
+            nc.vector.tensor_tensor(out=woven(z_b1[:, PACK * cols.start : PACK * cols.stop]),
+                                    in0=by_pairs(part[1][:, :, cols]), in1=by_pairs(travel_sb[1][:, :, cols]), op=ALU.add)
+        for cols in entries:
+            nc.vector.quantize_mx(out=zq[1][0][:, cols].bitcast(FP8X4), scales=zq[1][1][:, cols],
+                                  in_=z_b1[:, PACK * cols.start : PACK * cols.stop])
+        w4_q[0, 1] = quantize(w4_b01, "w4q01", offset=PART_AT)
         w4_q[1, 1] = quantize(w4_b11, "w4q11")
 
         y_scales = held([P, 2, S], U8, "y_scales")
@@ -264,7 +291,7 @@ def tile_list_rupture_site_features_kernel(
                 y_passes(1, a, False, stop=(a == 0), slices=[t])
 
         def hand_out(g, slot, banks_a_store, code_stores):
-            y = held([P, PACK, S], F32, f"y{g}", slot)
+            y = held([P, PACK, S], F32, "y1", slot) if g else placed([P, PACK, S], F32, "y0", LAST_AT)
             rows = out_0[half(g), :].rearrange("(p t) s -> p t s", t=PACK)
             for t in range(PACK):
                 copy = nc.vector.tensor_copy if (g == 0 and t in VECTOR_BANKS) else nc.scalar.copy
@@ -274,7 +301,7 @@ def tile_list_rupture_site_features_kernel(
                 elif (t + 1) % banks_a_store == 0:
                     done = slice(t + 1 - banks_a_store, t + 1)
                     nc.sync.dma_start(out=rows[:, done, :], in_=y[:, done, :])
-            vals = held([P, WOVEN], BF16, f"y_b{g}", f"z_b{g}")
+            vals = held([P, WOVEN], BF16, f"y_b{g}", ("h_b0", "z_b1")[g])
             codes = held([P, S], U32, f"y_codes{g}")
             entries = [slice(S // 2 * i, S // 2 * (i + 1)) for i in range(2)]
             for cols in entries:

@@ -30,7 +30,7 @@ TAB2S_AT = GAIN_AT - KIB // 2
 PART_AT = W2_AT + 10 * KIB
 LAST_AT = PART_AT + 8 * KIB
 SPREAD = 8
-VECTOR_BANKS = (2, 3)
+VECTOR_BANKS = (2,)
 
 
 def tile_list_rupture_site_features_kernel(
@@ -76,8 +76,8 @@ def tile_list_rupture_site_features_kernel(
                 out=dst.rearrange("p a (t m) -> p a t m", t=PACK),
                 in_=src.rearrange("p a (m t) -> p a t m", t=PACK))
 
-        def deal_by_pairs(dst, src):
-            nc.vector.tensor_copy(
+        def deal_by_pairs(dst, src, copy=nc.vector.tensor_copy):
+            copy(
                 out=dst.rearrange("p a (t c i) -> p a c t i", t=PACK, i=PAIR),
                 in_=src.rearrange("p a (c i t) -> p a c t i", t=PACK, i=PAIR))
 
@@ -212,7 +212,7 @@ def tile_list_rupture_site_features_kernel(
         w3_w = held([P, 2, N], I32, "w3_w", "w2_b0")
         nc.sync.dma_start(out=w3_w[:], in_=w3_words.rearrange("a p n t -> p a (n t)").bitcast(I32))
         nc.vector.tensor_copy(v_w[0][:], tab_w[0][:].bitcast(U32).indirect(offs_sb[:]))
-        w4_raw00 = load_rows("w4_raw00", w4[half(0), half(0)], slot="tab_w0")
+        w4_row0 = load_rows("w4_row0", w4[half(0), :], slot="tab_w0")
         nc.vector.tensor_copy(v_w[1][:], tab_w[1][:].bitcast(U32).indirect(offs_sb[:]))
         w1d_w.append(held([P, 2, KP], U16, "w1d_w1"))
         deal(w1d_w[1][:], w1_w[1][:])
@@ -226,84 +226,80 @@ def tile_list_rupture_site_features_kernel(
         damped(0, range(PACK))
         w4_raw10 = load_rows("w4_raw10", w4[half(1), half(0)], slot="damp0")
         h_b0 = h_rounded(0)
-        w4_raw01 = load_rows("w4_raw01", w4[half(0), half(1)], slot="sat0")
+        travel_sb[1] = load_rows("travel1", travel[half(1), :], slot="sat0")
         w2_q[1] = quantize(w2_b1, "w2q1")
         slip(1, W2_AT + 4 * S)
         site(1)
         hq[0] = quantize(h_b0, "hq0", offset=W2_AT)
         z_b0 = z_rounded(0, LAST_AT + 2 * KIB)
-        travel_sb[1] = load_rows("travel1", travel[half(1), :], PART_AT)
-        for g in range(2):
-            w3d_w[g] = held([P, 2, KP], I32, f"w3d_w{g}")
-            deal_by_pairs(w3d_w[g][:], w3_w[:, :, half(g)])
-        zq[0] = quantize(z_b0, "zq0")
         w4_raw11 = [load_rows(f"w4_raw11{i}", w4[half(1), KP + KP // 2 * i : KP + KP // 2 * (i + 1)],
-                              LAST_AT + 4 * KIB * i) for i in range(2)]
+                              PART_AT + 4 * KIB * i) for i in range(2)]
+        w3d_w[0] = held([P, 2, KP], I32, "w3d_w0")
+        deal_by_pairs(w3d_w[0][:], w3_w[:, :, half(0)])
+        zq[0] = quantize(z_b0, "zq0")
 
-        w4_b00 = rounded(w4_raw00, "w4_b00", "v2_w")
+        w3d_w[1] = held([P, 2, KP], U32, "w3d_w1", "v2_w")
+        deal_by_pairs(w3d_w[1][:], w3_w[:, :, half(1)].bitcast(U32), nc.scalar.copy)
+        w4_b00 = rounded(w4_row0[:, :, half(0)], "w4_b00", "w2q1_scales")
+        w4_b01 = rounded(w4_row0[:, :, half(1)], "w4_b01", "v_w0")
         w4_b10 = rounded(w4_raw10, "w4_b10", "v2_s")
-        w4_b01 = rounded(w4_raw01, "w4_b01", "w2q1_codes")
-        w4_b11 = held([P, WOVEN], BF16, "w4_b11", "w2q1_scales")
+        w4_b11 = held([P, WOVEN], BF16, "w4_b11", "w2q1_codes")
         for i in range(2):
             round_weight(w4_raw11[i][:], w4_b11[:], P // 2 * i)
 
-        h_b1 = h_rounded(1, "w2_b0")
+        h_b1 = h_rounded(1, "h_b0")
         part[1] = held([P, PACK, S], F32, "part1", "w2_raw0")
         damped(1, range(PACK - 1))
         hq[1] = quantize(h_b1, "hq1")
         damped(1, [PACK - 1])
         w4_q[0, 0] = quantize(w4_b00, "w4q00")
-        w4_q[1, 0] = quantize(w4_b10, "w4q10")
         z_b1 = held([P, WOVEN], BF16, "z_b1")
         zq[1] = held([P, S], U32, "zq1_codes"), held([P, S], U8, "zq1_scales")
         entries = [slice(S // 2 * e, S // 2 * (e + 1)) for e in range(2)]
         for cols in entries:
             nc.vector.tensor_tensor(out=woven(z_b1[:, PACK * cols.start : PACK * cols.stop]),
                                     in0=by_pairs(part[1][:, :, cols]), in1=by_pairs(travel_sb[1][:, :, cols]), op=ALU.add)
+        w4_q[1, 0] = quantize(w4_b10, "w4q10")
         for cols in entries:
             nc.vector.quantize_mx(out=zq[1][0][:, cols].bitcast(FP8X4), scales=zq[1][1][:, cols],
                                   in_=z_b1[:, PACK * cols.start : PACK * cols.stop])
-        w4_q[0, 1] = quantize(w4_b01, "w4q01", offset=PART_AT)
+        w4_q[0, 1] = quantize(w4_b01, "w4q01", "w2_raw0")
+
         w4_q[1, 1] = quantize(w4_b11, "w4q11")
-
         y_scales = held([P, 2, S], U8, "y_scales")
-        y_accs = [[bank(f"y{g}{t}", PACK * g + t) for t in range(PACK)] for g in range(2)]
+        y0_accs = [bank(f"y0{t}", t) for t in range(PACK)]
+        y1_accs = [[bank(f"y1{e}{u}", PACK + 2 * e + u) for u in range(2)] for e in range(2)]
 
-        def y_passes(g, a, from_h, start=False, stop=False, slices=range(PACK)):
-            for t in slices:
-                cols = slice(P * t, P * (t + 1))
-                if from_h:
-                    lw, ls = w3d_w[g][:, a, cols], w3d_s[LIVE * a : P, g, cols]
-                    rw, rs = hq[a]
-                else:
-                    lw, ls = w4_q[a, g][0][:, cols], w4_q[a, g][1][:, cols]
-                    rw, rs = zq[a]
-                nc.tensor.matmul_mx(out=y_accs[g][t][:], lhsT=lw.bitcast(FP8X4), lhsT_scale=ls,
-                                    rhs=rw[:].bitcast(FP8X4), rhs_scale=rs[:], start=start, stop=stop)
+        def y_pass(acc, g, a, from_h, t, cols, start, stop):
+            mine = slice(P * t, P * (t + 1))
+            if from_h:
+                lw, ls = w3d_w[g][:, a, mine], w3d_s[LIVE * a : P, g, mine]
+                rw, rs = hq[a]
+            else:
+                lw, ls = w4_q[a, g][0][:, mine], w4_q[a, g][1][:, mine]
+                rw, rs = zq[a]
+            nc.tensor.matmul_mx(out=acc, lhsT=lw.bitcast(FP8X4), lhsT_scale=ls,
+                                rhs=rw[:, cols].bitcast(FP8X4), rhs_scale=rs[:, cols], start=start, stop=stop)
 
-        for a in range(2):
-            for g in range(2):
-                y_passes(g, a, True, start=(a == 0))
-        for a in range(2):
-            y_passes(0, a, False, stop=(a == 1))
-        for t in range(PACK):
-            for a in (1, 0):
-                y_passes(1, a, False, stop=(a == 0), slices=[t])
-
-        def hand_out(g, slot, banks_a_store, code_stores):
-            y = held([P, PACK, S], F32, "y1", slot) if g else placed([P, PACK, S], F32, "y0", LAST_AT)
-            rows = out_0[half(g), :].rearrange("(p t) s -> p t s", t=PACK)
+        def y0_passes(a, from_h, start=False, stop=False):
             for t in range(PACK):
-                copy = nc.vector.tensor_copy if (g == 0 and t in VECTOR_BANKS) else nc.scalar.copy
-                copy(out=y[:, t, :], in_=y_accs[g][t][:])
-                if banks_a_store == 1:
-                    nc.sync.dma_start(out=rows[:, t, :], in_=y[:, t, :])
-                elif (t + 1) % banks_a_store == 0:
-                    done = slice(t + 1 - banks_a_store, t + 1)
-                    nc.sync.dma_start(out=rows[:, done, :], in_=y[:, done, :])
-            vals = held([P, WOVEN], BF16, f"y_b{g}", ("h_b0", "z_b1")[g])
+                y_pass(y0_accs[t][:], 0, a, from_h, t, slice(0, S), start, stop)
+
+        def y1_passes(a, from_h, start=False, stop=False, halves=range(2), slices=range(PACK)):
+            for e in halves:
+                for t in slices:
+                    y_pass(y1_accs[e][t // 2][:, entries[t % 2]], 1, a, from_h, t, entries[e],
+                           start and t % 2 == 0, stop and t % 2 == 1)
+
+        for a in range(2):
+            y0_passes(a, True, start=(a == 0))
+            y1_passes(a, True, start=(a == 0))
+        for a in range(2):
+            y0_passes(a, False, stop=(a == 1))
+
+        def planes(g, y, slot, code_stores):
+            vals = held([P, WOVEN], BF16, f"y_b{g}", slot)
             codes = held([P, S], U32, f"y_codes{g}")
-            entries = [slice(S // 2 * i, S // 2 * (i + 1)) for i in range(2)]
             for cols in entries:
                 nc.vector.tensor_copy(out=woven(vals[:, PACK * cols.start : PACK * cols.stop]),
                                       in_=by_pairs(y[:, :, cols]))
@@ -315,8 +311,25 @@ def tile_list_rupture_site_features_kernel(
                 nc.sync.dma_start(out=out_1[g, :, cols, :].rearrange("p m t -> p (m t)").bitcast(I32),
                                   in_=codes[:, cols].bitcast(I32))
 
-        hand_out(0, "w4_raw111", banks_a_store=1, code_stores=1)
-        hand_out(1, "tab_w0", banks_a_store=2, code_stores=2)
+        rows = [out_0[half(g), :].rearrange("(p t) s -> p t s", t=PACK) for g in range(2)]
+        y0 = held([P, PACK, S], F32, "y0", "sat0")
+        for t in range(PACK):
+            copy = nc.vector.tensor_copy if t in VECTOR_BANKS else nc.scalar.copy
+            copy(out=y0[:, t, :], in_=y0_accs[t][:])
+            nc.sync.dma_start(out=rows[0][:, t, :], in_=y0[:, t, :])
+        for u in range(2):
+            for e in range(2):
+                for a in range(2):
+                    y1_passes(a, False, stop=(a == 1), halves=[e], slices=[2 * u, 2 * u + 1])
+        y1 = held([P, PACK, S], F32, "y1", "damp1")
+        for u in range(2):
+            for e in range(2):
+                pair = slice(2 * u, 2 * u + 2)
+                nc.scalar.copy(out=y1[:, pair, entries[e]], in_=y1_accs[e][u][:].rearrange("p (v s) -> p v s", v=2))
+                if e == 1:
+                    nc.sync.dma_start(out=rows[1][:, pair, :], in_=y1[:, pair, :])
+        planes(0, y0, "w2_b0", 1)
+        planes(1, y1, "z_b1", 2)
         for r in range(LIVE):
             queue = nc.scalar if r < LIVE - 1 else nc.sync
             queue.dma_start(out=out_2[:, r : LIVE * LIVE : LIVE, :].rearrange("g q m -> q g m").bitcast(I32),

@@ -23,14 +23,21 @@ FLOPS = 2 * S * (K * H + K2 * H + 2 * H * N)
 WOVEN = PACK * S
 PAIR = 2
 KIB = 1024
-TAB1_AT, W1W1_AT, W1S1_AT, W3S_AT, W2Q_AT, GAIN_AT = 0, 8 * KIB, 10 * KIB, 11 * KIB, 12 * KIB, 14 * KIB
-W2_AT = GAIN_AT + 64
-TABS_AT = W1W1_AT - KIB // 2
-TAB2S_AT = GAIN_AT - KIB // 2
-PART_AT = W2_AT + 10 * KIB
-LAST_AT = PART_AT + 8 * KIB
+ALIGN = 64
 SPREAD = 8
-VECTOR_BANKS = (2,)
+SCALAR_LAST = 16
+
+TAB1_AT = 0
+W1_HALF1_AT = TAB1_AT + 8 * KIB
+W3_SCALES_AT = W1_HALF1_AT + 2 * KIB
+TAB_SCALES_AT = W1_HALF1_AT - KIB // 2
+W2_CODES0_AT = W3_SCALES_AT + 2 * KIB
+GAIN_AT = W2_CODES0_AT + 2 * KIB
+W2_HALF1_AT = GAIN_AT + ALIGN
+TAB2_SCALES_AT = GAIN_AT - KIB // 2
+SAT1_AT = W2_HALF1_AT + 2 * KIB
+PART0_AT = SAT1_AT + 8 * KIB
+CHAIN_AT = PART0_AT + 14 * KIB
 
 
 def tile_list_rupture_site_features_kernel(
@@ -46,10 +53,13 @@ def tile_list_rupture_site_features_kernel(
         psum = ctx.enter_context(tc.psum_pool(name="psum", bufs=1))
 
         def held(shape, dtype, name, slot=None):
-            return keep.tile(shape, dtype, name=name, tag=slot or name, align_bytes=64)
+            return keep.tile(shape, dtype, name=name, tag=slot or name, align_bytes=ALIGN)
 
         def placed(shape, dtype, name, offset):
-            return overlaid.tile(shape, dtype, name=name, align_bytes=64, offset=offset)
+            return overlaid.tile(shape, dtype, name=name, align_bytes=ALIGN, offset=offset)
+
+        def held_or_placed(shape, dtype, name, slot, offset):
+            return held(shape, dtype, name, slot) if offset is None else placed(shape, dtype, name, offset)
 
         def bank(name, number):
             return psum.tile([P, S], F32, name=name, tag=f"bank{number}")
@@ -66,13 +76,12 @@ def tile_list_rupture_site_features_kernel(
                                   in_=scales[:, r : LIVE * LIVE : LIVE, :].rearrange("a q n -> q a n").bitcast(I32))
 
         def load_rows(name, src, offset=None, slot=None):
-            shape = [P, PACK, src.shape[1]]
-            rows = held(shape, F32, name, slot) if offset is None else placed(shape, F32, name, offset)
+            rows = held_or_placed([P, PACK, src.shape[1]], F32, name, slot, offset)
             nc.sync.dma_start(out=rows[:], in_=src.rearrange("(p j) c -> p j c", j=PACK))
             return rows
 
-        def deal(dst, src, copy=nc.vector.tensor_copy):
-            copy(
+        def deal(dst, src):
+            nc.vector.tensor_copy(
                 out=dst.rearrange("p a (t m) -> p a t m", t=PACK),
                 in_=src.rearrange("p a (m t) -> p a t m", t=PACK))
 
@@ -94,7 +103,7 @@ def tile_list_rupture_site_features_kernel(
 
         def quantize(vals, name, slot=None, offset=None):
             width = vals.shape[1] // PACK
-            codes = held([P, width], U32, name + "_codes", slot) if offset is None else placed([P, width], U32, name + "_codes", offset)
+            codes = held_or_placed([P, width], U32, name + "_codes", slot, offset)
             scales = held([P, width], U8, name + "_scales")
             nc.vector.quantize_mx(out=codes[:].bitcast(FP8X4), scales=scales[:], in_=vals[:])
             return codes, scales
@@ -107,8 +116,8 @@ def tile_list_rupture_site_features_kernel(
 
         offs_sb = lists.tile([P, S // 16], U16, name="offs_sb")
         offs2_sb = lists.tile([P, S // 16], U16, name="offs2_sb")
-        tab_s = placed([P, 2, T], U8, "tab_s", TABS_AT)
-        tab2_s = placed([P, 1, T2], U8, "tab2_s", TAB2S_AT)
+        tab_s = placed([P, 2, T], U8, "tab_s", TAB_SCALES_AT)
+        tab2_s = placed([P, 1, T2], U8, "tab2_s", TAB2_SCALES_AT)
         w1_s = held([P, 2, H], U8, "w1_s")
         v_s = held([P, 2, S], U8, "v_s")
         tab2_w = held([P, T2], U16, "tab2_w")
@@ -121,7 +130,7 @@ def tile_list_rupture_site_features_kernel(
             return words
 
         def load_w1(b):
-            words = placed([P, 2, KP], U16, "w1_w1", W1W1_AT) if b else held([P, 2, KP], U16, "w1_w0")
+            words = placed([P, 2, KP], U16, "w1_w1", W1_HALF1_AT) if b else held([P, 2, KP], U16, "w1_w0")
             nc.sync.dma_start(out=words[:].bitcast(I32),
                               in_=w1_words[:, :, 2 * KP * b : 2 * KP * (b + 1)].rearrange("a p n -> p a n").bitcast(I32))
             return words
@@ -130,7 +139,8 @@ def tile_list_rupture_site_features_kernel(
         nc.sync.dma_start(offs2_sb[:], offs2)
         nc.sync.dma_start(out=tab2_w[:].bitcast(I32), in_=tab2_words[0].bitcast(I32))
         nc.sync.dma_start(offs_sb[:], offs)
-        nc.sync.dma_start(out=tab_s[0:P:SPREAD].bitcast(I32), in_=tab_scales.rearrange("a q n -> q a n").bitcast(I32))
+        nc.sync.dma_start(out=tab_s[0:P:SPREAD].bitcast(I32),
+                          in_=tab_scales.rearrange("a q n -> q a n").bitcast(I32))
         load_scale_rows(tab2_s, tab2_scales, range(LIVE - 1))
         w2_raw[0] = load_rows("w2_raw0", w2[:, half(0)])
         load_scale_rows(tab2_s, tab2_scales, [LIVE - 1])
@@ -146,7 +156,7 @@ def tile_list_rupture_site_features_kernel(
             nc.sync.dma_start(out=v_s[r:P:QUAD].bitcast(I32), in_=v_g[SPREAD * r : P : QUAD].bitcast(I32))
         tab_w[1] = load_tab(1)
         w1_w[1] = load_w1(1)
-        w3_s = placed([P, 1, N], U8, "w3_s", W1S1_AT)
+        w3_s = placed([P, 1, N], U8, "w3_s", W3_SCALES_AT)
         clear(w3_s)
         v2_s = held([P, S], U8, "v2_s")
         nc.vector.tensor_copy(v2_s[:], tab2_s[:, 0, :].indirect(offs2_sb[:]))
@@ -155,15 +165,15 @@ def tile_list_rupture_site_features_kernel(
             nc.sync.dma_start(out=w3_s[QUAD * q : QUAD * q + 2 * LIVE, 0, :].bitcast(I32),
                               in_=w3_scales[:, LIVE * q : LIVE * (q + 1), :].bitcast(I32))
         nc.sync.dma_start(out=gain_sb[:], in_=gain.rearrange("(b p t) -> p b t", b=2, t=PACK))
-        w2_raw[1] = load_rows("w2_raw1", w2[:, half(1)], W2_AT)
+        w2_raw[1] = load_rows("w2_raw1", w2[:, half(1)], W2_HALF1_AT)
 
         v_w = [held([P, S], U32, f"v_w{a}") for a in range(2)]
-        w1d_w = [placed([P, 2, KP], U16, "w1d_w0", LAST_AT + 2 * KIB)]
+        w1d_w = [placed([P, 2, KP], U16, "w1d_w0", CHAIN_AT)]
         w1d_s = [held([P, 2, KP], U8, f"w1d_s{b}") for b in range(2)]
         sat, damp, part, w2_q, w4_q, hq, zq, w3d_w = {}, {}, {}, {}, {}, {}, {}, {}
 
         def slip(b, offset=None):
-            sat[b] = held([P, PACK, S], F32, f"sat{b}") if offset is None else placed([P, PACK, S], F32, f"sat{b}", offset)
+            sat[b] = held_or_placed([P, PACK, S], F32, f"sat{b}", None, offset)
             accs = [bank(f"slip{b}{t}", PACK * (1 - b) + t) for t in range(PACK)]
             for a in range(2):
                 for t in range(PACK):
@@ -197,20 +207,21 @@ def tile_list_rupture_site_features_kernel(
             nc.vector.tensor_tensor(out=woven(vals[:]), in0=by_pairs(sat[b][:]), in1=gains, op=ALU.mult)
             return vals
 
-        def z_rounded(b, offset):
-            vals = placed([P, WOVEN], BF16, f"z_b{b}", offset)
-            nc.vector.tensor_tensor(out=woven(vals[:]), in0=by_pairs(part[b][:]), in1=by_pairs(travel_sb[b][:]),
+        def z_rounded(vals, b, cols):
+            nc.vector.tensor_tensor(out=woven(vals[:, PACK * cols.start : PACK * cols.stop]),
+                                    in0=by_pairs(part[b][:, :, cols]), in1=by_pairs(travel_sb[b][:, :, cols]),
                                     op=ALU.add)
-            return vals
 
         for b in range(2):
             deal(w1d_s[b][:], w1_s[:, :, half(b)])
-        w2_q[0] = quantize(rounded(w2_raw[0], "w2_b0"), "w2q0", offset=W2Q_AT)
+        w2_q[0] = quantize(rounded(w2_raw[0], "w2_b0"), "w2q0", offset=W2_CODES0_AT)
         deal(w1d_w[0][:], w1_w[0][:])
         site(0)
         travel_sb[0] = load_rows("travel0", travel[half(0), :], slot="w2_raw0")
-        w3_w = held([P, 2, N], I32, "w3_w", "w2_b0")
-        nc.sync.dma_start(out=w3_w[:], in_=w3_words.rearrange("a p n t -> p a (n t)").bitcast(I32))
+        w3_rows = w3_words.rearrange("a p n t -> a p (n t)").bitcast(I32)
+        w3_w = held([P, 3, KP], I32, "w3_w", "w2_b0")
+        nc.sync.dma_start(out=w3_w[:, 0:2, :].rearrange("p g n -> p (g n)"), in_=w3_rows[0])
+        nc.sync.dma_start(out=w3_w[:, 2, :], in_=w3_rows[1][:, half(0)])
         nc.vector.tensor_copy(v_w[0][:], tab_w[0][:].bitcast(U32).indirect(offs_sb[:]))
         w4_row0 = load_rows("w4_row0", w4[half(0), :], slot="tab_w0")
         nc.vector.tensor_copy(v_w[1][:], tab_w[1][:].bitcast(U32).indirect(offs_sb[:]))
@@ -220,52 +231,64 @@ def tile_list_rupture_site_features_kernel(
         deal(w3d_s[:], w3_s[:, 0, :].rearrange("p (g n) -> p g n", g=2))
 
         slip(0)
-        w2_b1 = placed([P, WOVEN], BF16, "w2_b1", LAST_AT + 2 * KIB)
+        w2_b1 = placed([P, WOVEN], BF16, "w2_b1", CHAIN_AT)
         round_weight(w2_raw[1][:], w2_b1[:])
-        part[0] = placed([P, PACK, S], F32, "part0", PART_AT)
+        part[0] = placed([P, PACK, S], F32, "part0", PART0_AT)
         damped(0, range(PACK))
-        w4_raw10 = load_rows("w4_raw10", w4[half(1), half(0)], slot="damp0")
+        travel_sb[1] = load_rows("travel1", travel[half(1), :], slot="damp0")
         h_b0 = h_rounded(0)
-        travel_sb[1] = load_rows("travel1", travel[half(1), :], slot="sat0")
+        w4_raw10 = load_rows("w4_raw10", w4[half(1), half(0)], slot="sat0")
         w2_q[1] = quantize(w2_b1, "w2q1")
-        slip(1, W2_AT + 4 * S)
+        slip(1, SAT1_AT)
         site(1)
-        hq[0] = quantize(h_b0, "hq0", offset=W2_AT)
-        z_b0 = z_rounded(0, LAST_AT + 2 * KIB)
-        w4_raw11 = [load_rows(f"w4_raw11{i}", w4[half(1), KP + KP // 2 * i : KP + KP // 2 * (i + 1)],
-                              PART_AT + 4 * KIB * i) for i in range(2)]
-        w3d_w[0] = held([P, 2, KP], I32, "w3d_w0")
-        deal_by_pairs(w3d_w[0][:], w3_w[:, :, half(0)])
+        hq[0] = quantize(h_b0, "hq0", offset=W2_HALF1_AT)
+        z_b0 = placed([P, WOVEN], BF16, "z_b0", CHAIN_AT)
+        z_rounded(z_b0, 0, slice(0, S))
+        ending = placed([P, 7 * S], F32, "ending", PART0_AT)
+        y0 = ending[:, : PACK * S].rearrange("p (t s) -> p t s", t=PACK)
+        w4_b11 = ending[:, 3 * S : 5 * S].bitcast(BF16)
+        w4_raw11 = [ending[:, first : first + 2 * S].rearrange("p (j c) -> p j c", j=PACK)
+                    for first in (5 * S, S // 2)]
+        for i in range(2):
+            src = w4[half(1), KP + KP // 2 * i : KP + KP // 2 * (i + 1)]
+            nc.sync.dma_start(out=w4_raw11[i], in_=src.rearrange("(p j) c -> p j c", j=PACK))
+        h_b1 = h_rounded(1, "h_b0")
         zq[0] = quantize(z_b0, "zq0")
+        w3_last = placed([P, 1, KP], I32, "w3_last", CHAIN_AT)
+        nc.sync.dma_start(out=w3_last[:, 0, :], in_=w3_rows[1][:, half(1)])
 
-        w3d_w[1] = held([P, 2, KP], U32, "w3d_w1", "v2_w")
-        deal_by_pairs(w3d_w[1][:], w3_w[:, :, half(1)].bitcast(U32), nc.scalar.copy)
+        w3d_early = held([P, 3, KP], U32, "w3d_early", "v2_w")
+        deal_by_pairs(w3d_early[:], w3_w[:].bitcast(U32), nc.scalar.copy)
+        w3d_w[0, 0], w3d_w[0, 1], w3d_w[1, 0] = (w3d_early[:, i, :] for i in range(3))
         w4_b00 = rounded(w4_row0[:, :, half(0)], "w4_b00", "w2q1_scales")
         w4_b01 = rounded(w4_row0[:, :, half(1)], "w4_b01", "v_w0")
         w4_b10 = rounded(w4_raw10, "w4_b10", "v2_s")
-        w4_b11 = held([P, WOVEN], BF16, "w4_b11", "w2q1_codes")
-        for i in range(2):
-            round_weight(w4_raw11[i][:], w4_b11[:], P // 2 * i)
+        round_weight(w4_raw11[0], w4_b11)
+        round_weight(w4_raw11[1][:, :, : PACK * SCALAR_LAST], w4_b11, P // 2)
 
-        h_b1 = h_rounded(1, "h_b0")
         part[1] = held([P, PACK, S], F32, "part1", "w2_raw0")
         damped(1, range(PACK - 1))
         hq[1] = quantize(h_b1, "hq1")
         damped(1, [PACK - 1])
-        w4_q[0, 0] = quantize(w4_b00, "w4q00")
         z_b1 = held([P, WOVEN], BF16, "z_b1")
         zq[1] = held([P, S], U32, "zq1_codes"), held([P, S], U8, "zq1_scales")
         entries = [slice(S // 2 * e, S // 2 * (e + 1)) for e in range(2)]
-        for cols in entries:
-            nc.vector.tensor_tensor(out=woven(z_b1[:, PACK * cols.start : PACK * cols.stop]),
-                                    in0=by_pairs(part[1][:, :, cols]), in1=by_pairs(travel_sb[1][:, :, cols]), op=ALU.add)
-        w4_q[1, 0] = quantize(w4_b10, "w4q10")
+        w4_q[0, 0] = quantize(w4_b00, "w4q00")
+        z_rounded(z_b1, 1, entries[0])
+        w4_q[0, 1] = quantize(w4_b01, "w4q01")
+        z_rounded(z_b1, 1, entries[1])
         for cols in entries:
             nc.vector.quantize_mx(out=zq[1][0][:, cols].bitcast(FP8X4), scales=zq[1][1][:, cols],
                                   in_=z_b1[:, PACK * cols.start : PACK * cols.stop])
-        w4_q[0, 1] = quantize(w4_b01, "w4q01", "w2_raw0")
+        w4_q[1, 0] = quantize(w4_b10, "w4q10")
+        nc.vector.tensor_copy(
+            out=w4_b11.rearrange("p (t m j) -> p m j t", t=PACK, j=PACK)[:, P // 2 + SCALAR_LAST :],
+            in_=w4_raw11[1][:, :, PACK * SCALAR_LAST :].rearrange("p j (m t) -> p m j t", t=PACK))
+        w3d_last = held([P, 1, KP], I32, "w3d_last", "v2_s")
+        deal_by_pairs(w3d_last[:], w3_last[:])
+        w3d_w[1, 1] = w3d_last[:, 0, :]
+        w4_q[1, 1] = quantize(w4_b11, "w4q11", offset=CHAIN_AT)
 
-        w4_q[1, 1] = quantize(w4_b11, "w4q11")
         y_scales = held([P, 2, S], U8, "y_scales")
         y0_accs = [bank(f"y0{t}", t) for t in range(PACK)]
         y1_accs = [[bank(f"y1{e}{u}", PACK + 2 * e + u) for u in range(2)] for e in range(2)]
@@ -273,7 +296,7 @@ def tile_list_rupture_site_features_kernel(
         def y_pass(acc, g, a, from_h, t, cols, start, stop):
             mine = slice(P * t, P * (t + 1))
             if from_h:
-                lw, ls = w3d_w[g][:, a, mine], w3d_s[LIVE * a : P, g, mine]
+                lw, ls = w3d_w[a, g][:, mine], w3d_s[LIVE * a : P, g, mine]
                 rw, rs = hq[a]
             else:
                 lw, ls = w4_q[a, g][0][:, mine], w4_q[a, g][1][:, mine]
@@ -288,48 +311,59 @@ def tile_list_rupture_site_features_kernel(
         def y1_passes(a, from_h, start=False, stop=False, halves=range(2), slices=range(PACK)):
             for e in halves:
                 for t in slices:
-                    y_pass(y1_accs[e][t // 2][:, entries[t % 2]], 1, a, from_h, t, entries[e],
+                    place = slice(S // 2 * (t % 2), S // 2 * (t % 2 + 1))
+                    y_pass(y1_accs[e][t // 2][:, place], 1, a, from_h, t, entries[e],
                            start and t % 2 == 0, stop and t % 2 == 1)
 
-        for a in range(2):
-            y0_passes(a, True, start=(a == 0))
-            y1_passes(a, True, start=(a == 0))
-        for a in range(2):
-            y0_passes(a, False, stop=(a == 1))
+        y0_passes(0, True, start=True)
+        y1_passes(0, True, start=True)
+        y0_passes(1, True)
+        y0_passes(0, False)
+        y1_passes(0, False)
+        y0_passes(1, False, stop=True)
 
-        def planes(g, y, slot, code_stores):
-            vals = held([P, WOVEN], BF16, f"y_b{g}", slot)
-            codes = held([P, S], U32, f"y_codes{g}")
-            for cols in entries:
-                nc.vector.tensor_copy(out=woven(vals[:, PACK * cols.start : PACK * cols.stop]),
-                                      in_=by_pairs(y[:, :, cols]))
-            for cols in entries:
-                nc.vector.quantize_mx(out=codes[:, cols].bitcast(FP8X4), scales=y_scales[:, g, cols],
-                                      in_=vals[:, PACK * cols.start : PACK * cols.stop])
-            for i in range(code_stores):
-                cols = slice(S // code_stores * i, S // code_stores * (i + 1))
-                nc.sync.dma_start(out=out_1[g, :, cols, :].rearrange("p m t -> p (m t)").bitcast(I32),
-                                  in_=codes[:, cols].bitcast(I32))
+        y_codes = [held([P, S], U32, f"y_codes{g}") for g in range(2)]
+        y_vals = [held([P, WOVEN], BF16, "y_b0", "w2_b0"), held([P, WOVEN], BF16, "y_b1", "z_b1")]
+
+        def y_weave(g, y, cols):
+            nc.vector.tensor_copy(out=woven(y_vals[g][:, PACK * cols.start : PACK * cols.stop]),
+                                  in_=by_pairs(y[:, :, cols]))
+
+        def y_quantize(g, cols):
+            nc.vector.quantize_mx(out=y_codes[g][:, cols].bitcast(FP8X4), scales=y_scales[:, g, cols],
+                                  in_=y_vals[g][:, PACK * cols.start : PACK * cols.stop])
+
+        def store_codes(g, cols):
+            nc.sync.dma_start(out=out_1[g, :, cols, :].rearrange("p m t -> p (m t)").bitcast(I32),
+                              in_=y_codes[g][:, cols].bitcast(I32))
 
         rows = [out_0[half(g), :].rearrange("(p t) s -> p t s", t=PACK) for g in range(2)]
-        y0 = held([P, PACK, S], F32, "y0", "sat0")
         for t in range(PACK):
-            copy = nc.vector.tensor_copy if t in VECTOR_BANKS else nc.scalar.copy
+            copy = nc.vector.tensor_copy if t in (3,) else nc.scalar.copy
             copy(out=y0[:, t, :], in_=y0_accs[t][:])
             nc.sync.dma_start(out=rows[0][:, t, :], in_=y0[:, t, :])
-        for u in range(2):
-            for e in range(2):
-                for a in range(2):
-                    y1_passes(a, False, stop=(a == 1), halves=[e], slices=[2 * u, 2 * u + 1])
         y1 = held([P, PACK, S], F32, "y1", "damp1")
-        for u in range(2):
-            for e in range(2):
-                pair = slice(2 * u, 2 * u + 2)
-                nc.scalar.copy(out=y1[:, pair, entries[e]], in_=y1_accs[e][u][:].rearrange("p (v s) -> p v s", v=2))
-                if e == 1:
-                    nc.sync.dma_start(out=rows[1][:, pair, :], in_=y1[:, pair, :])
-        planes(0, y0, "w2_b0", 1)
-        planes(1, y1, "z_b1", 2)
+        banks1 = [(e, u) for u in range(2) for e in range(2)]
+        for e, u in banks1:
+            y1_passes(1, True, halves=[e], slices=[2 * u, 2 * u + 1])
+            y1_passes(1, False, stop=True, halves=[e], slices=[2 * u, 2 * u + 1])
+        for cols in entries:
+            y_weave(0, y0, cols)
+        for cols in entries:
+            y_quantize(0, cols)
+        for n, (e, u) in enumerate(banks1):
+            pair = slice(2 * u, 2 * u + 2)
+            copy = nc.vector.tensor_copy if n in (9,) else nc.scalar.copy
+            copy(out=y1[:, pair, entries[e]], in_=y1_accs[e][u][:].rearrange("p (v s) -> p v s", v=2))
+            if e == 1:
+                nc.sync.dma_start(out=rows[1][:, pair, :], in_=y1[:, pair, :])
+            if n == 1:
+                store_codes(0, slice(0, S))
+        for cols in entries:
+            y_weave(1, y1, cols)
+        for cols in entries:
+            y_quantize(1, cols)
+            store_codes(1, cols)
         for r in range(LIVE):
             queue = nc.scalar if r < LIVE - 1 else nc.sync
             queue.dma_start(out=out_2[:, r : LIVE * LIVE : LIVE, :].rearrange("g q m -> q g m").bitcast(I32),

@@ -90,11 +90,10 @@ def tile_list_rupture_site_features_kernel(
                 out=dst.rearrange("p a (t c i) -> p a c t i", t=PACK, i=PAIR),
                 in_=src.rearrange("p a (c i t) -> p a c t i", t=PACK, i=PAIR))
 
-        def round_weight(raw, vals, first=0):
+        def round_weight(raw, vals, first=0, copy=nc.scalar.copy):
             count = raw.shape[2] // PACK
-            nc.scalar.copy(
-                out=vals.rearrange("p (u v m j) -> p u m j v", u=2, v=2, j=PACK)[:, :, first : first + count],
-                in_=raw.rearrange("p j (m u v) -> p u m j v", u=2, v=2))
+            copy(out=vals.rearrange("p (t m u v) -> p m u t v", t=PACK, u=2, v=2)[:, first : first + count],
+                 in_=raw.rearrange("p (u v) (m t) -> p m u t v", t=PACK, v=2))
 
         def rounded(raw, name, slot=None):
             vals = held([P, WOVEN], BF16, name, slot)
@@ -281,9 +280,7 @@ def tile_list_rupture_site_features_kernel(
             nc.vector.quantize_mx(out=zq[1][0][:, cols].bitcast(FP8X4), scales=zq[1][1][:, cols],
                                   in_=z_b1[:, PACK * cols.start : PACK * cols.stop])
         w4_q[1, 0] = quantize(w4_b10, "w4q10")
-        nc.vector.tensor_copy(
-            out=w4_b11.rearrange("p (t m j) -> p m j t", t=PACK, j=PACK)[:, P // 2 + SCALAR_LAST :],
-            in_=w4_raw11[1][:, :, PACK * SCALAR_LAST :].rearrange("p j (m t) -> p m j t", t=PACK))
+        round_weight(w4_raw11[1][:, :, PACK * SCALAR_LAST :], w4_b11, P // 2 + SCALAR_LAST, nc.vector.tensor_copy)
         w3d_last = held([P, 1, KP], I32, "w3d_last", "v2_s")
         deal_by_pairs(w3d_last[:], w3_last[:])
         w3d_w[1, 1] = w3d_last[:, 0, :]

@@ -25,7 +25,7 @@ PAIR = 2
 KIB = 1024
 ALIGN = 64
 SPREAD = 8
-SCALAR_LAST = 16
+SCALAR_THIRD = 104
 
 TAB1_AT = 0
 W1_HALF1_AT = TAB1_AT + 8 * KIB
@@ -37,7 +37,7 @@ W2_HALF1_AT = GAIN_AT + ALIGN
 TAB2_SCALES_AT = GAIN_AT - KIB // 2
 SAT1_AT = W2_HALF1_AT + 2 * KIB
 PART0_AT = SAT1_AT + 8 * KIB
-CHAIN_AT = PART0_AT + 14 * KIB
+CHAIN_AT = PART0_AT + 8 * KIB
 
 
 def tile_list_rupture_site_features_kernel(
@@ -243,11 +243,8 @@ def tile_list_rupture_site_features_kernel(
         hq[0] = quantize(h_b0, "hq0", offset=W2_HALF1_AT)
         z_b0 = placed([P, WOVEN], BF16, "z_b0", CHAIN_AT)
         z_rounded(z_b0, 0, slice(0, S))
-        ending = placed([P, 7 * S], F32, "ending", PART0_AT)
-        y0 = ending[:, : PACK * S].rearrange("p (t s) -> p t s", t=PACK)
-        w4_b11 = ending[:, 3 * S : 5 * S].bitcast(BF16)
-        w4_raw11 = [ending[:, first : first + 2 * S].rearrange("p (j c) -> p j c", j=PACK)
-                    for first in (5 * S, S // 2)]
+        last = placed([P, PACK * KP], F32, "last", PART0_AT)
+        w4_raw11 = [last[:, 2 * KP * i : 2 * KP * (i + 1)].rearrange("p (j c) -> p j c", j=PACK) for i in range(2)]
         for i in range(2):
             src = w4[half(1), KP + KP // 2 * i : KP + KP // 2 * (i + 1)]
             nc.sync.dma_start(out=w4_raw11[i], in_=src.rearrange("(p j) c -> p j c", j=PACK))
@@ -261,9 +258,6 @@ def tile_list_rupture_site_features_kernel(
         w3d_w[0, 0], w3d_w[0, 1], w3d_w[1, 0] = (w3d_early[:, i, :] for i in range(3))
         w4_b00 = rounded(w4_row0[:, :, half(0)], "w4_b00", "w2q1_scales")
         w4_b01 = rounded(w4_row0[:, :, half(1)], "w4_b01", "v_w0")
-        w4_b10 = rounded(w4_raw10, "w4_b10", "v2_s")
-        round_weight(w4_raw11[0], w4_b11)
-        round_weight(w4_raw11[1][:, :, : PACK * SCALAR_LAST], w4_b11, P // 2)
 
         part[1] = held([P, PACK, S], F32, "part1", "w2_raw0")
         damped(1, range(PACK - 1))
@@ -276,21 +270,32 @@ def tile_list_rupture_site_features_kernel(
         z_rounded(z_b1, 1, entries[0])
         w4_q[0, 1] = quantize(w4_b01, "w4q01")
         z_rounded(z_b1, 1, entries[1])
-        for cols in entries:
-            nc.vector.quantize_mx(out=zq[1][0][:, cols].bitcast(FP8X4), scales=zq[1][1][:, cols],
-                                  in_=z_b1[:, PACK * cols.start : PACK * cols.stop])
-        w4_q[1, 0] = quantize(w4_b10, "w4q10")
-        round_weight(w4_raw11[1][:, :, PACK * SCALAR_LAST :], w4_b11, P // 2 + SCALAR_LAST, nc.vector.tensor_copy)
-        w3d_last = held([P, 1, KP], I32, "w3d_last", "v2_s")
+        w4_b10 = held([P, WOVEN], BF16, "w4_b10", "v2_s")
+        round_weight(w4_raw10[:, :, : PACK * SCALAR_THIRD], w4_b10[:])
+        round_weight(w4_raw10[:, :, PACK * SCALAR_THIRD :], w4_b10[:], SCALAR_THIRD, nc.vector.tensor_copy)
+        nc.vector.quantize_mx(out=zq[1][0][:].bitcast(FP8X4), scales=zq[1][1][:], in_=z_b1[:])
+
+        def quantize_in_halves(vals, name):
+            codes, scales = held([P, KP], U32, name + "_codes"), held([P, KP], U8, name + "_scales")
+            for cols in entries:
+                nc.vector.quantize_mx(out=codes[:, cols].bitcast(FP8X4), scales=scales[:, cols],
+                                      in_=vals[:, PACK * cols.start : PACK * cols.stop])
+            return codes, scales
+
+        w4_q[1, 0] = quantize_in_halves(w4_b10, "w4q10")
+        w4_b11 = held([P, WOVEN], BF16, "w4_b11", "tab_w0")
+        round_weight(w4_raw11[0], w4_b11[:])
+        round_weight(w4_raw11[1], w4_b11[:], P // 2, nc.vector.tensor_copy)
+        w3d_last = held([P, 1, KP], I32, "w3d_last")
         deal_by_pairs(w3d_last[:], w3_last[:])
         w3d_w[1, 1] = w3d_last[:, 0, :]
-        w4_q[1, 1] = quantize(w4_b11, "w4q11", offset=CHAIN_AT)
+        w4_q[1, 1] = quantize_in_halves(w4_b11, "w4q11")
+        y_banks = [[0, 1, 2, 3], [4, 5, 6, 7]]
 
         y_scales = held([P, 2, S], U8, "y_scales")
-        y0_accs = [bank(f"y0{t}", t) for t in range(PACK)]
-        y1_accs = [[bank(f"y1{e}{u}", PACK + 2 * e + u) for u in range(2)] for e in range(2)]
+        y_accs = [[bank(f"y{g}{t}", y_banks[g][t]) for t in range(PACK)] for g in range(2)]
 
-        def y_pass(acc, g, a, from_h, t, cols, start, stop):
+        def y_pass(g, a, from_h, t, start=False, stop=False):
             mine = slice(P * t, P * (t + 1))
             if from_h:
                 lw, ls = w3d_w[a, g][:, mine], w3d_s[LIVE * a : P, g, mine]
@@ -298,68 +303,58 @@ def tile_list_rupture_site_features_kernel(
             else:
                 lw, ls = w4_q[a, g][0][:, mine], w4_q[a, g][1][:, mine]
                 rw, rs = zq[a]
-            nc.tensor.matmul_mx(out=acc, lhsT=lw.bitcast(FP8X4), lhsT_scale=ls,
-                                rhs=rw[:, cols].bitcast(FP8X4), rhs_scale=rs[:, cols], start=start, stop=stop)
+            nc.tensor.matmul_mx(out=y_accs[g][t][:], lhsT=lw.bitcast(FP8X4), lhsT_scale=ls,
+                                rhs=rw[:].bitcast(FP8X4), rhs_scale=rs[:], start=start, stop=stop)
 
-        def y0_passes(a, from_h, start=False, stop=False):
+        def y_passes(g, a, from_h, start=False, stop=False):
             for t in range(PACK):
-                y_pass(y0_accs[t][:], 0, a, from_h, t, slice(0, S), start, stop)
+                y_pass(g, a, from_h, t, start, stop)
 
-        def y1_passes(a, from_h, start=False, stop=False, halves=range(2), slices=range(PACK)):
-            for e in halves:
-                for t in slices:
-                    place = slice(S // 2 * (t % 2), S // 2 * (t % 2 + 1))
-                    y_pass(y1_accs[e][t // 2][:, place], 1, a, from_h, t, entries[e],
-                           start and t % 2 == 0, stop and t % 2 == 1)
-
-        y0_passes(0, True, start=True)
-        y1_passes(0, True, start=True)
-        y0_passes(1, True)
-        y0_passes(0, False)
-        y1_passes(0, False)
-        y0_passes(1, False, stop=True)
+        y_passes(0, 0, True, start=True)
+        y_passes(1, 0, True, start=True)
+        y_passes(0, 1, True)
+        y_passes(0, 0, False)
+        y_passes(1, 0, False)
+        y_passes(0, 1, False, stop=True)
+        for t in range(PACK):
+            y_pass(1, 1, True, t)
+            y_pass(1, 1, False, t, stop=True)
 
         y_codes = [held([P, S], U32, f"y_codes{g}") for g in range(2)]
         y_vals = [held([P, WOVEN], BF16, "y_b0", "w2_b0"), held([P, WOVEN], BF16, "y_b1", "z_b1")]
+        y = [held([P, PACK, S], F32, "y0", "damp0"), held([P, PACK, S], F32, "y1", "damp1")]
+        rows = [out_0[half(g), :].rearrange("(p t) s -> p t s", t=PACK) for g in range(2)]
 
-        def y_weave(g, y, cols):
-            nc.vector.tensor_copy(out=woven(y_vals[g][:, PACK * cols.start : PACK * cols.stop]),
-                                  in_=by_pairs(y[:, :, cols]))
+        def empty(g, t, copy):
+            copy(out=y[g][:, t, :], in_=y_accs[g][t][:])
 
-        def y_quantize(g, cols):
-            nc.vector.quantize_mx(out=y_codes[g][:, cols].bitcast(FP8X4), scales=y_scales[:, g, cols],
-                                  in_=y_vals[g][:, PACK * cols.start : PACK * cols.stop])
+        def store_rows(g, slices):
+            nc.sync.dma_start(out=rows[g][:, slices, :], in_=y[g][:, slices, :])
+
+        def planes(g):
+            for cols in entries:
+                nc.vector.tensor_copy(out=woven(y_vals[g][:, PACK * cols.start : PACK * cols.stop]),
+                                      in_=by_pairs(y[g][:, :, cols]))
+            for cols in entries:
+                nc.vector.quantize_mx(out=y_codes[g][:, cols].bitcast(FP8X4), scales=y_scales[:, g, cols],
+                                      in_=y_vals[g][:, PACK * cols.start : PACK * cols.stop])
 
         def store_codes(g, cols):
             nc.sync.dma_start(out=out_1[g, :, cols, :].rearrange("p m t -> p (m t)").bitcast(I32),
                               in_=y_codes[g][:, cols].bitcast(I32))
 
-        rows = [out_0[half(g), :].rearrange("(p t) s -> p t s", t=PACK) for g in range(2)]
         for t in range(PACK):
-            copy = nc.vector.tensor_copy if t in (3,) else nc.scalar.copy
-            copy(out=y0[:, t, :], in_=y0_accs[t][:])
-            nc.sync.dma_start(out=rows[0][:, t, :], in_=y0[:, t, :])
-        y1 = held([P, PACK, S], F32, "y1", "damp1")
-        banks1 = [(e, u) for u in range(2) for e in range(2)]
-        for e, u in banks1:
-            y1_passes(1, True, halves=[e], slices=[2 * u, 2 * u + 1])
-            y1_passes(1, False, stop=True, halves=[e], slices=[2 * u, 2 * u + 1])
+            empty(0, t, nc.vector.tensor_copy if t in [3] else nc.scalar.copy)
+            store_rows(0, slice(t, t + 1))
+        planes(0)
+        for t in range(PACK):
+            empty(1, t, nc.vector.tensor_copy if t in [] else nc.scalar.copy)
+            if t < 2:
+                store_rows(1, slice(t, t + 1))
+        store_rows(1, slice(2, PACK))
+        store_codes(0, slice(0, S))
+        planes(1)
         for cols in entries:
-            y_weave(0, y0, cols)
-        for cols in entries:
-            y_quantize(0, cols)
-        for n, (e, u) in enumerate(banks1):
-            pair = slice(2 * u, 2 * u + 2)
-            copy = nc.vector.tensor_copy if n in (9,) else nc.scalar.copy
-            copy(out=y1[:, pair, entries[e]], in_=y1_accs[e][u][:].rearrange("p (v s) -> p v s", v=2))
-            if e == 1:
-                nc.sync.dma_start(out=rows[1][:, pair, :], in_=y1[:, pair, :])
-            if n == 1:
-                store_codes(0, slice(0, S))
-        for cols in entries:
-            y_weave(1, y1, cols)
-        for cols in entries:
-            y_quantize(1, cols)
             store_codes(1, cols)
         for r in range(LIVE):
             queue = nc.scalar if r < LIVE - 1 else nc.sync

@@ -24,14 +24,13 @@ WOVEN = PACK * S
 PAIR = 2
 KIB = 1024
 ALIGN = 64
-SPREAD = 8
-SCALAR_THIRD = 104
+SPREAD = 4
 
 TAB1_AT = 0
-W1_HALF1_AT = TAB1_AT + 8 * KIB
-W3_SCALES_AT = W1_HALF1_AT + 2 * KIB
-TAB_SCALES_AT = W1_HALF1_AT - KIB // 2
-W2_CODES0_AT = W3_SCALES_AT + 2 * KIB
+W3_SCALES_AT = TAB1_AT + 8 * KIB
+W1_HALF1_AT = W3_SCALES_AT + KIB
+TAB_SCALES_AT = W3_SCALES_AT - KIB // 2
+W2_CODES0_AT = W1_HALF1_AT + 2 * KIB
 GAIN_AT = W2_CODES0_AT + 2 * KIB
 W2_HALF1_AT = GAIN_AT + ALIGN
 TAB2_SCALES_AT = GAIN_AT - KIB // 2
@@ -80,8 +79,8 @@ def tile_list_rupture_site_features_kernel(
             nc.sync.dma_start(out=rows[:], in_=src.rearrange("(p j) c -> p j c", j=PACK))
             return rows
 
-        def deal(dst, src):
-            nc.vector.tensor_copy(
+        def deal(dst, src, copy=nc.vector.tensor_copy):
+            copy(
                 out=dst.rearrange("p a (t m) -> p a t m", t=PACK),
                 in_=src.rearrange("p a (m t) -> p a t m", t=PACK))
 
@@ -115,7 +114,7 @@ def tile_list_rupture_site_features_kernel(
 
         offs_sb = lists.tile([P, S // 16], U16, name="offs_sb")
         offs2_sb = lists.tile([P, S // 16], U16, name="offs2_sb")
-        tab_s = placed([P, 2, T], U8, "tab_s", TAB_SCALES_AT)
+        tab_s = placed([P, 1, T], U8, "tab_s", TAB_SCALES_AT)
         tab2_s = placed([P, 1, T2], U8, "tab2_s", TAB2_SCALES_AT)
         w1_s = held([P, 2, H], U8, "w1_s")
         v_s = held([P, 2, S], U8, "v_s")
@@ -138,7 +137,7 @@ def tile_list_rupture_site_features_kernel(
         nc.sync.dma_start(offs2_sb[:], offs2)
         nc.sync.dma_start(out=tab2_w[:].bitcast(I32), in_=tab2_words[0].bitcast(I32))
         nc.sync.dma_start(offs_sb[:], offs)
-        nc.sync.dma_start(out=tab_s[0:P:SPREAD].bitcast(I32),
+        nc.sync.dma_start(out=tab_s[0:P:SPREAD, 0, :].bitcast(I32),
                           in_=tab_scales.rearrange("a q n -> q a n").bitcast(I32))
         load_scale_rows(tab2_s, tab2_scales, range(LIVE - 1))
         w2_raw[0] = load_rows("w2_raw0", w2[:, half(0)])
@@ -147,12 +146,12 @@ def tile_list_rupture_site_features_kernel(
         load_scale_rows(w1_s, w1_scales)
         tab_w[0] = load_tab(0)
         v2_w = held([P, S], U16, "v2_w")
-        v_g = held([P, 2, S], U8, "v_g")
+        v_g = held([P, S], U8, "v_g")
         nc.vector.tensor_copy(v2_w[:], tab2_w[:].indirect(offs2_sb[:]))
-        for a in range(2):
-            nc.vector.tensor_copy(v_g[:, a, :], tab_s[:, a, :].indirect(offs_sb[:]))
-        for r in range(LIVE):
-            nc.sync.dma_start(out=v_s[r:P:QUAD].bitcast(I32), in_=v_g[SPREAD * r : P : QUAD].bitcast(I32))
+        nc.vector.tensor_copy(v_g[:], tab_s[:, 0, :].indirect(offs_sb[:]))
+        for q in (0, 2, 1, 3):
+            nc.sync.dma_start(out=v_s[QUAD * q : QUAD * q + LIVE].bitcast(I32),
+                              in_=v_g[QUAD * q : QUAD * (q + 1) : SPREAD].bitcast(I32))
         tab_w[1] = load_tab(1)
         w1_w[1] = load_w1(1)
         w3_s = placed([P, 1, N], U8, "w3_s", W3_SCALES_AT)
@@ -167,7 +166,9 @@ def tile_list_rupture_site_features_kernel(
         w2_raw[1] = load_rows("w2_raw1", w2[:, half(1)], W2_HALF1_AT)
 
         v_w = [held([P, S], U32, f"v_w{a}") for a in range(2)]
-        w1d_w = [placed([P, 2, KP], U16, "w1d_w0", CHAIN_AT)]
+        w1d_first = placed([P, 2, KP], U16, "w1d_first", CHAIN_AT)
+        w1d_w = {(a, 0): w1d_first[:, a, :] for a in range(2)}
+        entries = [slice(S // 2 * e, S // 2 * (e + 1)) for e in range(2)]
         w1d_s = [held([P, 2, KP], U8, f"w1d_s{b}") for b in range(2)]
         sat, damp, part, w2_q, w4_q, hq, zq, w3d_w = {}, {}, {}, {}, {}, {}, {}, {}
 
@@ -177,12 +178,27 @@ def tile_list_rupture_site_features_kernel(
             for a in range(2):
                 for t in range(PACK):
                     cols = slice(P * t, P * (t + 1))
-                    nc.tensor.matmul_mx(out=accs[t][:], lhsT=w1d_w[b][:, a, cols].bitcast(FP4X4),
+                    nc.tensor.matmul_mx(out=accs[t][:], lhsT=w1d_w[a, b][:, cols].bitcast(FP4X4),
                                         lhsT_scale=w1d_s[b][:, a, cols],
                                         rhs=v_w[a][:].bitcast(FP8X4), rhs_scale=v_s[:, a, :],
                                         start=(a == 0), stop=(a == 1))
             for t in range(PACK):
                 nc.scalar.activation(out=sat[b][:, t, :], in_=accs[t][:], func=ACT.Tanh)
+
+        def slip_by_entries(b):
+            sat[b] = held([P, PACK, S], F32, f"sat{b}")
+            accs = {(e, u): bank(f"slip{b}{e}{u}", PACK + 2 * e + u) for e in range(2) for u in range(2)}
+            for a in range(2):
+                for e, u in accs:
+                    for v in range(2):
+                        cols = slice(P * (2 * u + v), P * (2 * u + v + 1))
+                        nc.tensor.matmul_mx(out=accs[e, u][:, entries[v]], lhsT=w1d_w[a, b][:, cols].bitcast(FP4X4),
+                                            lhsT_scale=w1d_s[b][:, a, cols],
+                                            rhs=v_w[a][:, entries[e]].bitcast(FP8X4), rhs_scale=v_s[:, a, entries[e]],
+                                            start=(a == 0 and v == 0), stop=(a == 1 and v == 1))
+            for e, u in accs:
+                nc.scalar.activation(out=sat[b][:, 2 * u : 2 * u + 2, entries[e]],
+                                     in_=accs[e, u][:].rearrange("p (v s) -> p v s", v=2), func=ACT.Tanh)
 
         def site(b):
             codes, scales = w2_q[b]
@@ -194,11 +210,11 @@ def tile_list_rupture_site_features_kernel(
                                     rhs=v2_w[:].bitcast(FP4X4), rhs_scale=v2_s[:], start=True, stop=True)
                 nc.scalar.activation(out=damp[b][:, t, :], in_=acc[:], func=ACT.Sigmoid, scale=-1.0)
 
-        def damped(b, slices):
+        def damped(b, slices, cols=slice(0, S)):
             for t in slices:
                 nc.vector.scalar_tensor_tensor(
-                    out=part[b][:, t, :], in0=sat[b][:, t, :], scalar=gain_sb[:, b, t : t + 1],
-                    in1=damp[b][:, t, :], op0=ALU.mult, op1=ALU.mult)
+                    out=part[b][:, t, cols], in0=sat[b][:, t, cols], scalar=gain_sb[:, b, t : t + 1],
+                    in1=damp[b][:, t, cols], op0=ALU.mult, op1=ALU.mult)
 
         def h_rounded(b, slot=None):
             vals = held([P, WOVEN], BF16, f"h_b{b}", slot)
@@ -214,7 +230,7 @@ def tile_list_rupture_site_features_kernel(
         for b in range(2):
             deal(w1d_s[b][:], w1_s[:, :, half(b)])
         w2_q[0] = quantize(rounded(w2_raw[0], "w2_b0"), "w2q0", offset=W2_CODES0_AT)
-        deal(w1d_w[0][:], w1_w[0][:])
+        deal(w1d_first[:], w1_w[0][:], nc.scalar.copy)
         site(0)
         travel_sb[0] = load_rows("travel0", travel[half(0), :], slot="w2_raw0")
         w3_rows = w3_words.rearrange("a p n t -> a p (n t)").bitcast(I32)
@@ -223,17 +239,22 @@ def tile_list_rupture_site_features_kernel(
         nc.sync.dma_start(out=w3_w[:, 2, :], in_=w3_rows[1][:, half(0)])
         nc.vector.tensor_copy(v_w[0][:], tab_w[0][:].bitcast(U32).indirect(offs_sb[:]))
         w4_row0 = load_rows("w4_row0", w4[half(0), :], slot="tab_w0")
-        nc.vector.tensor_copy(v_w[1][:], tab_w[1][:].bitcast(U32).indirect(offs_sb[:]))
-        w1d_w.append(held([P, 2, KP], U16, "w1d_w1"))
-        deal(w1d_w[1][:], w1_w[1][:])
+        for cols in entries:
+            nc.vector.tensor_copy(v_w[1][:, cols],
+                                  tab_w[1][:].bitcast(U32).indirect(offs_sb[:, cols.start // 16 : cols.stop // 16]))
+        for a, copy in enumerate((nc.scalar.copy, nc.vector.tensor_copy)):
+            words = held([P, 1, KP], U16, f"w1d_second{a}")
+            deal(words[:], w1_w[1][:, a : a + 1], copy)
+            w1d_w[a, 1] = words[:, 0, :]
         w3d_s = held([P, 2, KP], U8, "w3d_s")
         deal(w3d_s[:], w3_s[:, 0, :].rearrange("p (g n) -> p g n", g=2))
 
-        slip(0)
+        slip_by_entries(0)
         w2_b1 = placed([P, WOVEN], BF16, "w2_b1", CHAIN_AT)
         round_weight(w2_raw[1][:], w2_b1[:])
         part[0] = placed([P, PACK, S], F32, "part0", PART0_AT)
-        damped(0, range(PACK))
+        for cols in entries:
+            damped(0, range(PACK), cols)
         travel_sb[1] = load_rows("travel1", travel[half(1), :], slot="damp0")
         h_b0 = h_rounded(0)
         w4_raw10 = load_rows("w4_raw10", w4[half(1), half(0)], slot="sat0")
@@ -265,15 +286,15 @@ def tile_list_rupture_site_features_kernel(
         damped(1, [PACK - 1])
         z_b1 = held([P, WOVEN], BF16, "z_b1")
         zq[1] = held([P, S], U32, "zq1_codes"), held([P, S], U8, "zq1_scales")
-        entries = [slice(S // 2 * e, S // 2 * (e + 1)) for e in range(2)]
         w4_q[0, 0] = quantize(w4_b00, "w4q00")
         z_rounded(z_b1, 1, entries[0])
         w4_q[0, 1] = quantize(w4_b01, "w4q01")
         z_rounded(z_b1, 1, entries[1])
         w4_b10 = held([P, WOVEN], BF16, "w4_b10", "v2_s")
-        round_weight(w4_raw10[:, :, : PACK * SCALAR_THIRD], w4_b10[:])
-        round_weight(w4_raw10[:, :, PACK * SCALAR_THIRD :], w4_b10[:], SCALAR_THIRD, nc.vector.tensor_copy)
-        nc.vector.quantize_mx(out=zq[1][0][:].bitcast(FP8X4), scales=zq[1][1][:], in_=z_b1[:])
+        round_weight(w4_raw10[:], w4_b10[:])
+        for cols in entries:
+            nc.vector.quantize_mx(out=zq[1][0][:, cols].bitcast(FP8X4), scales=zq[1][1][:, cols],
+                                  in_=z_b1[:, PACK * cols.start : PACK * cols.stop])
 
         def quantize_in_halves(vals, name):
             codes, scales = held([P, KP], U32, name + "_codes"), held([P, KP], U8, name + "_scales")
@@ -345,14 +366,16 @@ def tile_list_rupture_site_features_kernel(
 
         for t in range(PACK):
             empty(0, t, nc.vector.tensor_copy if t in [3] else nc.scalar.copy)
-            store_rows(0, slice(t, t + 1))
+            if t < 2:
+                store_rows(0, slice(t, t + 1))
+        store_rows(0, slice(2, PACK))
         planes(0)
         for t in range(PACK):
             empty(1, t, nc.vector.tensor_copy if t in [] else nc.scalar.copy)
-            if t < 2:
-                store_rows(1, slice(t, t + 1))
-        store_rows(1, slice(2, PACK))
-        store_codes(0, slice(0, S))
+            if t == PACK - 1:
+                store_codes(0, slice(0, S))
+            if t % 2:
+                store_rows(1, slice(t - 1, t + 1))
         planes(1)
         for cols in entries:
             store_codes(1, cols)

@@ -1,6 +1,7 @@
 from contextlib import ExitStack
 
 import concourse.mybir as mybir
+from concourse.masks import make_identity
 
 F32 = mybir.dt.float32
 BF16 = mybir.dt.bfloat16
@@ -25,6 +26,8 @@ PAIR = 2
 KIB = 1024
 ALIGN = 64
 SPREAD = 4
+POOL_SHARE = 128
+SCALAR_THIRD = 104
 
 TAB1_AT = 0
 W3_SCALES_AT = TAB1_AT + 8 * KIB
@@ -37,6 +40,7 @@ TAB2_SCALES_AT = GAIN_AT - KIB // 2
 SAT1_AT = W2_HALF1_AT + 2 * KIB
 PART0_AT = SAT1_AT + 8 * KIB
 CHAIN_AT = PART0_AT + 8 * KIB
+DAMP1_AT = CHAIN_AT + 8 * KIB
 
 
 def tile_list_rupture_site_features_kernel(
@@ -121,6 +125,11 @@ def tile_list_rupture_site_features_kernel(
         tab2_w = held([P, T2], U16, "tab2_w")
         for plane in (tab_s, tab2_s, w1_s, v_s):
             clear(plane)
+        identity = held([P, P], F32, "identity")
+        nc.vector.memset(identity[:], 0.0)
+        make_identity(nc, identity[:], nomemset=True)
+        gain_row = held([P, KP], F32, "gain_row")
+        nc.vector.memset(gain_row[:], 0.0)
 
         def load_tab(a):
             words = placed([P, T], I32, "tab_w1", TAB1_AT) if a else held([P, T], I32, "tab_w0")
@@ -145,6 +154,7 @@ def tile_list_rupture_site_features_kernel(
         w1_w[0] = load_w1(0)
         load_scale_rows(w1_s, w1_scales)
         tab_w[0] = load_tab(0)
+        nc.sync.dma_start(out=gain_row[0:1], in_=gain[half(1)].unsqueeze(0))
         v2_w = held([P, S], U16, "v2_w")
         v_g = held([P, S], U8, "v_g")
         nc.vector.tensor_copy(v2_w[:], tab2_w[:].indirect(offs2_sb[:]))
@@ -200,12 +210,12 @@ def tile_list_rupture_site_features_kernel(
                 nc.scalar.activation(out=sat[b][:, 2 * u : 2 * u + 2, entries[e]],
                                      in_=accs[e, u][:].rearrange("p (v s) -> p v s", v=2), func=ACT.Tanh)
 
-        def site(b):
+        def site(b, banks, offset=None):
             codes, scales = w2_q[b]
-            damp[b] = held([P, PACK, S], F32, f"damp{b}")
+            damp[b] = held_or_placed([P, PACK, S], F32, f"damp{b}", None, offset)
             for t in range(PACK):
                 cols = slice(P * t, P * (t + 1))
-                acc = bank(f"site{b}{t}", PACK * b + t)
+                acc = bank(f"site{b}{t}", banks[t])
                 nc.tensor.matmul_mx(out=acc[:], lhsT=codes[:, cols].bitcast(FP8X4), lhsT_scale=scales[:, cols],
                                     rhs=v2_w[:].bitcast(FP4X4), rhs_scale=v2_s[:], start=True, stop=True)
                 nc.scalar.activation(out=damp[b][:, t, :], in_=acc[:], func=ACT.Sigmoid, scale=-1.0)
@@ -216,22 +226,21 @@ def tile_list_rupture_site_features_kernel(
                     out=part[b][:, t, cols], in0=sat[b][:, t, cols], scalar=gain_sb[:, b, t : t + 1],
                     in1=damp[b][:, t, cols], op0=ALU.mult, op1=ALU.mult)
 
-        def h_rounded(b, slot=None):
-            vals = held([P, WOVEN], BF16, f"h_b{b}", slot)
-            gains = gain_sb[:, b, :].unsqueeze(1).unsqueeze(3).to_broadcast([P, S // PAIR, PACK, PAIR])
+        def h_rounded(b, gains, offset=None):
+            vals = held_or_placed([P, WOVEN], BF16, f"h_b{b}", None, offset)
+            gains = gains.unsqueeze(1).unsqueeze(3).to_broadcast([P, S // PAIR, PACK, PAIR])
             nc.vector.tensor_tensor(out=woven(vals[:]), in0=by_pairs(sat[b][:]), in1=gains, op=ALU.mult)
             return vals
 
-        def z_rounded(vals, b, cols):
-            nc.vector.tensor_tensor(out=woven(vals[:, PACK * cols.start : PACK * cols.stop]),
-                                    in0=by_pairs(part[b][:, :, cols]), in1=by_pairs(travel_sb[b][:, :, cols]),
-                                    op=ALU.add)
+        def z_rounded(vals, b, cols, engine=nc.vector):
+            engine.tensor_tensor(out=woven(vals), in0=by_pairs(part[b][:, :, cols]),
+                                 in1=by_pairs(travel_sb[b][:, :, cols]), op=ALU.add)
 
         for b in range(2):
             deal(w1d_s[b][:], w1_s[:, :, half(b)])
         w2_q[0] = quantize(rounded(w2_raw[0], "w2_b0"), "w2q0", offset=W2_CODES0_AT)
         deal(w1d_first[:], w1_w[0][:], nc.scalar.copy)
-        site(0)
+        site(0, [0, 1, 2, 3])
         travel_sb[0] = load_rows("travel0", travel[half(0), :], slot="w2_raw0")
         w3_rows = w3_words.rearrange("a p n t -> a p (n t)").bitcast(I32)
         w3_w = held([P, 3, KP], I32, "w3_w", "w2_b0")
@@ -256,23 +265,26 @@ def tile_list_rupture_site_features_kernel(
         for cols in entries:
             damped(0, range(PACK), cols)
         travel_sb[1] = load_rows("travel1", travel[half(1), :], slot="damp0")
-        h_b0 = h_rounded(0)
+        h_b0 = h_rounded(0, gain_sb[:, 0, :])
         w4_raw10 = load_rows("w4_raw10", w4[half(1), half(0)], slot="sat0")
         w2_q[1] = quantize(w2_b1, "w2q1")
         slip(1, SAT1_AT)
-        site(1)
+        gain_bank = bank("gain_bank", 7)
+        for t in range(PACK):
+            nc.tensor.transpose(gain_bank[:, P * t : P * (t + 1)], gain_row[:, t:KP:PACK], identity[:])
+        site(1, [4, 5, 6, 0], DAMP1_AT)
         hq[0] = quantize(h_b0, "hq0", offset=W2_HALF1_AT)
-        z_b0 = placed([P, WOVEN], BF16, "z_b0", CHAIN_AT)
-        z_rounded(z_b0, 0, slice(0, S))
+        shares = [slice(0, S - POOL_SHARE), slice(S - POOL_SHARE, S)]
+        z_b0 = [placed([P, PACK * (S - POOL_SHARE)], BF16, "z_b00", CHAIN_AT),
+                held([P, PACK * POOL_SHARE], BF16, "z_b01", "h_b0")]
+        z_rounded(z_b0[0][:], 0, shares[0])
+        h_b1 = h_rounded(1, gain_bank[:, 0:S:P], CHAIN_AT + 4 * KIB - ALIGN)
+        z_rounded(z_b0[1][:], 0, shares[1], nc.gpsimd)
         last = placed([P, PACK * KP], F32, "last", PART0_AT)
         w4_raw11 = [last[:, 2 * KP * i : 2 * KP * (i + 1)].rearrange("p (j c) -> p j c", j=PACK) for i in range(2)]
         for i in range(2):
             src = w4[half(1), KP + KP // 2 * i : KP + KP // 2 * (i + 1)]
             nc.sync.dma_start(out=w4_raw11[i], in_=src.rearrange("(p j) c -> p j c", j=PACK))
-        h_b1 = h_rounded(1, "h_b0")
-        zq[0] = quantize(z_b0, "zq0")
-        w3_last = placed([P, 1, KP], I32, "w3_last", CHAIN_AT)
-        nc.sync.dma_start(out=w3_last[:, 0, :], in_=w3_rows[1][:, half(1)])
 
         w3d_early = held([P, 3, KP], U32, "w3d_early", "v2_w")
         deal_by_pairs(w3d_early[:], w3_w[:].bitcast(U32), nc.scalar.copy)
@@ -280,21 +292,22 @@ def tile_list_rupture_site_features_kernel(
         w4_b00 = rounded(w4_row0[:, :, half(0)], "w4_b00", "w2q1_scales")
         w4_b01 = rounded(w4_row0[:, :, half(1)], "w4_b01", "v_w0")
 
-        part[1] = held([P, PACK, S], F32, "part1", "w2_raw0")
-        damped(1, range(PACK - 1))
+        part[1] = held([P, PACK, S], F32, "part1")
+        damped(1, range(PACK))
         hq[1] = quantize(h_b1, "hq1")
-        damped(1, [PACK - 1])
+        zq[0] = placed([P, S], U32, "zq0_codes", DAMP1_AT), held([P, S], U8, "zq0_scales")
+        for vals, cols in zip(z_b0, shares):
+            nc.vector.quantize_mx(out=zq[0][0][:, cols].bitcast(FP8X4), scales=zq[0][1][:, cols], in_=vals[:])
+        w3_last = placed([P, 1, KP], I32, "w3_last", CHAIN_AT)
+        nc.sync.dma_start(out=w3_last[:, 0, :], in_=w3_rows[1][:, half(1)])
         z_b1 = held([P, WOVEN], BF16, "z_b1")
-        zq[1] = held([P, S], U32, "zq1_codes"), held([P, S], U8, "zq1_scales")
         w4_q[0, 0] = quantize(w4_b00, "w4q00")
-        z_rounded(z_b1, 1, entries[0])
+        z_rounded(z_b1[:], 1, slice(0, S))
         w4_q[0, 1] = quantize(w4_b01, "w4q01")
-        z_rounded(z_b1, 1, entries[1])
         w4_b10 = held([P, WOVEN], BF16, "w4_b10", "v2_s")
-        round_weight(w4_raw10[:], w4_b10[:])
-        for cols in entries:
-            nc.vector.quantize_mx(out=zq[1][0][:, cols].bitcast(FP8X4), scales=zq[1][1][:, cols],
-                                  in_=z_b1[:, PACK * cols.start : PACK * cols.stop])
+        round_weight(w4_raw10[:, :, : PACK * SCALAR_THIRD], w4_b10[:])
+        round_weight(w4_raw10[:, :, PACK * SCALAR_THIRD :], w4_b10[:], SCALAR_THIRD, nc.vector.tensor_copy)
+        zq[1] = quantize(z_b1, "zq1")
 
         def quantize_in_halves(vals, name):
             codes, scales = held([P, KP], U32, name + "_codes"), held([P, KP], U8, name + "_scales")
@@ -311,7 +324,7 @@ def tile_list_rupture_site_features_kernel(
         deal_by_pairs(w3d_last[:], w3_last[:])
         w3d_w[1, 1] = w3d_last[:, 0, :]
         w4_q[1, 1] = quantize_in_halves(w4_b11, "w4q11")
-        y_banks = [[0, 1, 2, 3], [4, 5, 6, 7]]
+        y_banks = [[1, 2, 3, 4], [5, 6, 0, 7]]
 
         y_scales = held([P, 2, S], U8, "y_scales")
         y_accs = [[bank(f"y{g}{t}", y_banks[g][t]) for t in range(PACK)] for g in range(2)]
@@ -343,7 +356,7 @@ def tile_list_rupture_site_features_kernel(
 
         y_codes = [held([P, S], U32, f"y_codes{g}") for g in range(2)]
         y_vals = [held([P, WOVEN], BF16, "y_b0", "w2_b0"), held([P, WOVEN], BF16, "y_b1", "z_b1")]
-        y = [held([P, PACK, S], F32, "y0", "damp0"), held([P, PACK, S], F32, "y1", "damp1")]
+        y = [held([P, PACK, S], F32, "y0", "damp0"), held([P, PACK, S], F32, "y1", "part1")]
         rows = [out_0[half(g), :].rearrange("(p t) s -> p t s", t=PACK) for g in range(2)]
 
         def empty(g, t, copy):

@@ -26,8 +26,7 @@ PAIR = 2
 KIB = 1024
 ALIGN = 64
 SPREAD = 4
-POOL_SHARE = 128
-SCALAR_THIRD = 104
+POOL_SHARE = 256
 
 TAB1_AT = 0
 W3_SCALES_AT = TAB1_AT + 8 * KIB
@@ -220,6 +219,23 @@ def tile_list_rupture_site_features_kernel(
                                     rhs=v2_w[:].bitcast(FP4X4), rhs_scale=v2_s[:], start=True, stop=True)
                 nc.scalar.activation(out=damp[b][:, t, :], in_=acc[:], func=ACT.Sigmoid, scale=-1.0)
 
+        def site_turned(banks, turned_banks, offset):
+            codes, scales = w2_q[1]
+            across = placed([P, PACK, PACK, P], F32, "damp_across", offset)
+            turned = {(e, u): bank(f"damp1{e}{u}", turned_banks[2 * e + u]) for e in range(2) for u in range(2)}
+            for j in range(PACK):
+                mine = slice(P * j, P * (j + 1))
+                acc = bank(f"site1{j}", banks[j])
+                nc.tensor.matmul_mx(out=acc[:], lhsT=v2_w[:, mine].bitcast(FP4X4), lhsT_scale=v2_s[:, mine],
+                                    rhs=codes[:].bitcast(FP8X4), rhs_scale=scales[:], start=True, stop=True)
+                nc.scalar.activation(out=across[:, j], in_=acc[:].rearrange("p (m t) -> p t m", t=PACK),
+                                     func=ACT.Sigmoid, scale=-1.0)
+            for j in range(PACK):
+                for t in range(PACK):
+                    first = S // 2 * (t % 2) + P * (j % 2)
+                    nc.tensor.transpose(turned[j // 2, t // 2][:, first : first + P], across[:, j, t, :], identity[:])
+            return turned
+
         def damped(b, slices, cols=slice(0, S)):
             for t in slices:
                 nc.vector.scalar_tensor_tensor(
@@ -260,7 +276,7 @@ def tile_list_rupture_site_features_kernel(
 
         slip_by_entries(0)
         w2_b1 = placed([P, WOVEN], BF16, "w2_b1", CHAIN_AT)
-        round_weight(w2_raw[1][:], w2_b1[:])
+        nc.scalar.copy(out=woven(w2_b1[:]), in_=by_pairs(w2_raw[1][:]))
         part[0] = placed([P, PACK, S], F32, "part0", PART0_AT)
         for cols in entries:
             damped(0, range(PACK), cols)
@@ -272,7 +288,7 @@ def tile_list_rupture_site_features_kernel(
         gain_bank = bank("gain_bank", 7)
         for t in range(PACK):
             nc.tensor.transpose(gain_bank[:, P * t : P * (t + 1)], gain_row[:, t:KP:PACK], identity[:])
-        site(1, [4, 5, 6, 0], DAMP1_AT)
+        turned = site_turned([4, 5, 6, 0], [1, 2, 3, 4], DAMP1_AT)
         hq[0] = quantize(h_b0, "hq0", offset=W2_HALF1_AT)
         shares = [slice(0, S - POOL_SHARE), slice(S - POOL_SHARE, S)]
         z_b0 = [placed([P, PACK * (S - POOL_SHARE)], BF16, "z_b00", CHAIN_AT),
@@ -293,8 +309,12 @@ def tile_list_rupture_site_features_kernel(
         w4_b01 = rounded(w4_row0[:, :, half(1)], "w4_b01", "v_w0")
 
         part[1] = held([P, PACK, S], F32, "part1")
-        damped(1, range(PACK))
-        hq[1] = quantize(h_b1, "hq1")
+        for e, cols in enumerate(entries):
+            for t in range(PACK):
+                nc.vector.scalar_tensor_tensor(
+                    out=part[1][:, t, cols], in0=sat[1][:, t, cols], scalar=gain_sb[:, 1, t : t + 1],
+                    in1=turned[e, t // 2][:, entries[t % 2]], op0=ALU.mult, op1=ALU.mult)
+        hq[1] = quantize(h_b1, "hq1", offset=DAMP1_AT + 2 * KIB)
         zq[0] = placed([P, S], U32, "zq0_codes", DAMP1_AT), held([P, S], U8, "zq0_scales")
         for vals, cols in zip(z_b0, shares):
             nc.vector.quantize_mx(out=zq[0][0][:, cols].bitcast(FP8X4), scales=zq[0][1][:, cols], in_=vals[:])
@@ -304,9 +324,7 @@ def tile_list_rupture_site_features_kernel(
         w4_q[0, 0] = quantize(w4_b00, "w4q00")
         z_rounded(z_b1[:], 1, slice(0, S))
         w4_q[0, 1] = quantize(w4_b01, "w4q01")
-        w4_b10 = held([P, WOVEN], BF16, "w4_b10", "v2_s")
-        round_weight(w4_raw10[:, :, : PACK * SCALAR_THIRD], w4_b10[:])
-        round_weight(w4_raw10[:, :, PACK * SCALAR_THIRD :], w4_b10[:], SCALAR_THIRD, nc.vector.tensor_copy)
+        w4_b10 = rounded(w4_raw10, "w4_b10", "v2_s")
         zq[1] = quantize(z_b1, "zq1")
 
         def quantize_in_halves(vals, name):
@@ -324,7 +342,7 @@ def tile_list_rupture_site_features_kernel(
         deal_by_pairs(w3d_last[:], w3_last[:])
         w3d_w[1, 1] = w3d_last[:, 0, :]
         w4_q[1, 1] = quantize_in_halves(w4_b11, "w4q11")
-        y_banks = [[1, 2, 3, 4], [5, 6, 0, 7]]
+        y_banks = [[5, 6, 0, 7], [1, 2, 3, 4]]
 
         y_scales = held([P, 2, S], U8, "y_scales")
         y_accs = [[bank(f"y{g}{t}", y_banks[g][t]) for t in range(PACK)] for g in range(2)]

@@ -27,6 +27,7 @@ KIB = 1024
 ALIGN = 64
 SPREAD = 4
 POOL_SHARE = 256
+SCALAR_THIRD = 104
 
 TAB1_AT = 0
 W3_SCALES_AT = TAB1_AT + 8 * KIB
@@ -324,7 +325,9 @@ def tile_list_rupture_site_features_kernel(
         w4_q[0, 0] = quantize(w4_b00, "w4q00")
         z_rounded(z_b1[:], 1, slice(0, S))
         w4_q[0, 1] = quantize(w4_b01, "w4q01")
-        w4_b10 = rounded(w4_raw10, "w4_b10", "v2_s")
+        w4_b10 = held([P, WOVEN], BF16, "w4_b10", "v2_s")
+        round_weight(w4_raw10[:, :, : PACK * SCALAR_THIRD], w4_b10[:])
+        round_weight(w4_raw10[:, :, PACK * SCALAR_THIRD :], w4_b10[:], SCALAR_THIRD, nc.vector.tensor_copy)
         zq[1] = quantize(z_b1, "zq1")
 
         def quantize_in_halves(vals, name):

@@ -170,7 +170,7 @@ def tile_list_rupture_site_features_kernel(
         nc.vector.tensor_copy(v2_s[:], tab2_s[:, 0, :].indirect(offs2_sb[:]))
         gain_sb = placed([P, 2, PACK], F32, "gain_sb", GAIN_AT)
         for q in range(P // QUAD):
-            nc.sync.dma_start(out=w3_s[QUAD * q : QUAD * q + 2 * LIVE, 0, :].bitcast(I32),
+            nc.sync.dma_start(out=w3_s[QUAD * q + LIVE : QUAD * q + 3 * LIVE, 0, :].bitcast(I32),
                               in_=w3_scales[:, LIVE * q : LIVE * (q + 1), :].bitcast(I32))
         nc.sync.dma_start(out=gain_sb[:], in_=gain.rearrange("(b p t) -> p b t", b=2, t=PACK))
         w2_raw[1] = load_rows("w2_raw1", w2[:, half(1)], W2_HALF1_AT)
@@ -353,7 +353,7 @@ def tile_list_rupture_site_features_kernel(
         def y_pass(g, a, from_h, t, start=False, stop=False):
             mine = slice(P * t, P * (t + 1))
             if from_h:
-                lw, ls = w3d_w[a, g][:, mine], w3d_s[LIVE * a : P, g, mine]
+                lw, ls = w3d_w[a, g][:, mine], w3d_s[LIVE * (a + 1) : P, g, mine]
                 rw, rs = hq[a]
             else:
                 lw, ls = w4_q[a, g][0][:, mine], w4_q[a, g][1][:, mine]

from contextlib import ExitStack

import concourse.mybir as mybir
from concourse.masks import make_identity

F32 = mybir.dt.float32
BF16 = mybir.dt.bfloat16
I32 = mybir.dt.int32
U32 = mybir.dt.uint32
U16 = mybir.dt.uint16
U8 = mybir.dt.uint8
FP8X4 = mybir.dt.float8_e4m3fn_x4
FP4X4 = mybir.dt.float4_e2m1fn_x4
ACT = mybir.ActivationFunctionType
ALU = mybir.AluOpType

P = 128
PACK = 4
KP = P * PACK
QUAD = 32
LIVE = 4
K, K2, T, T2, S, H, N = 1024, 512, 2048, 1024, 512, 1024, 1024
FLOPS = 2 * S * (K * H + K2 * H + 2 * H * N)
WOVEN = PACK * S
PAIR = 2
KIB = 1024
ALIGN = 64
SPREAD = 4
POOL_SHARE = 256
SCALAR_THIRD = 104

TAB1_AT = 0
W3_SCALES_AT = TAB1_AT + 8 * KIB
W1_HALF1_AT = W3_SCALES_AT + KIB
TAB_SCALES_AT = W3_SCALES_AT - KIB // 2
W2_CODES0_AT = W1_HALF1_AT + 2 * KIB
GAIN_AT = W2_CODES0_AT + 2 * KIB
W2_HALF1_AT = GAIN_AT + ALIGN
TAB2_SCALES_AT = GAIN_AT - KIB // 2
SAT1_AT = W2_HALF1_AT + 2 * KIB
PART0_AT = SAT1_AT + 8 * KIB
CHAIN_AT = PART0_AT + 8 * KIB
DAMP1_AT = CHAIN_AT + 8 * KIB


def tile_list_rupture_site_features_kernel(
    tc, tab_words, tab_scales, tab2_words, tab2_scales, offs, offs2,
    w1_words, w1_scales, w2, w3_words, w3_scales, w4, gain, travel,
    out_0, out_1, out_2,
):
    nc = tc.nc
    with ExitStack() as ctx:
        lists = ctx.enter_context(tc.tile_pool(name="lists", bufs=1))
        keep = ctx.enter_context(tc.tile_pool(name="keep", bufs=1))
        overlaid = ctx.enter_context(tc.tile_pool(name="overlaid", bufs=1))
        psum = ctx.enter_context(tc.psum_pool(name="psum", bufs=1))

        def held(shape, dtype, name, slot=None):
            return keep.tile(shape, dtype, name=name, tag=slot or name, align_bytes=ALIGN)

        def placed(shape, dtype, name, offset):
            return overlaid.tile(shape, dtype, name=name, align_bytes=ALIGN, offset=offset)

        def held_or_placed(shape, dtype, name, slot, offset):
            return held(shape, dtype, name, slot) if offset is None else placed(shape, dtype, name, offset)

        def bank(name, number):
            return psum.tile([P, S], F32, name=name, tag=f"bank{number}")

        def half(b):
            return slice(KP * b, KP * (b + 1))

        def clear(plane):
            nc.vector.memset(plane[:].rearrange("p a n -> p (a n)").bitcast(I32), 0)

        def load_scale_rows(plane, scales, rows=range(LIVE)):
            for r in rows:
                nc.sync.dma_start(out=plane[r:P:QUAD].bitcast(I32),
                                  in_=scales[:, r : LIVE * LIVE : LIVE, :].rearrange("a q n -> q a n").bitcast(I32))

        def load_rows(name, src, offset=None, slot=None):
            rows = held_or_placed([P, PACK, src.shape[1]], F32, name, slot, offset)
            nc.sync.dma_start(out=rows[:], in_=src.rearrange("(p j) c -> p j c", j=PACK))
            return rows

        def deal(dst, src, copy=nc.vector.tensor_copy):
            copy(
                out=dst.rearrange("p a (t m) -> p a t m", t=PACK),
                in_=src.rearrange("p a (m t) -> p a t m", t=PACK))

        def deal_by_pairs(dst, src, copy=nc.vector.tensor_copy):
            copy(
                out=dst.rearrange("p a (t c i) -> p a c t i", t=PACK, i=PAIR),
                in_=src.rearrange("p a (c i t) -> p a c t i", t=PACK, i=PAIR))

        def round_weight(raw, vals, first=0, copy=nc.scalar.copy):
            count = raw.shape[2] // PACK
            copy(out=vals.rearrange("p (t m u v) -> p m u t v", t=PACK, u=2, v=2)[:, first : first + count],
                 in_=raw.rearrange("p (u v) (m t) -> p m u t v", t=PACK, v=2))

        def rounded(raw, name, slot=None):
            vals = held([P, WOVEN], BF16, name, slot)
            round_weight(raw[:], vals[:])
            return vals

        def quantize(vals, name, slot=None, offset=None):
            width = vals.shape[1] // PACK
            codes = held_or_placed([P, width], U32, name + "_codes", slot, offset)
            scales = held([P, width], U8, name + "_scales")
            nc.vector.quantize_mx(out=codes[:].bitcast(FP8X4), scales=scales[:], in_=vals[:])
            return codes, scales

        def woven(vals):
            return vals.rearrange("p (c i t) -> p c t i", i=PAIR, t=PACK)

        def by_pairs(rows):
            return rows.rearrange("p t (c i) -> p c t i", i=PAIR)

        offs_sb = lists.tile([P, S // 16], U16, name="offs_sb")
        offs2_sb = lists.tile([P, S // 16], U16, name="offs2_sb")
        tab_s = placed([P, 1, T], U8, "tab_s", TAB_SCALES_AT)
        tab2_s = placed([P, 1, T2], U8, "tab2_s", TAB2_SCALES_AT)
        w1_s = held([P, 2, H], U8, "w1_s")
        v_s = held([P, 2, S], U8, "v_s")
        tab2_w = held([P, T2], U16, "tab2_w")
        for plane in (tab_s, tab2_s, w1_s, v_s):
            clear(plane)
        identity = held([P, P], F32, "identity")
        nc.vector.memset(identity[:], 0.0)
        make_identity(nc, identity[:], nomemset=True)
        gain_row = held([P, KP], F32, "gain_row")
        nc.vector.memset(gain_row[:], 0.0)

        def load_tab(a):
            words = placed([P, T], I32, "tab_w1", TAB1_AT) if a else held([P, T], I32, "tab_w0")
            nc.sync.dma_start(out=words[:], in_=tab_words[a].rearrange("p n t -> p (n t)").bitcast(I32))
            return words

        def load_w1(b):
            words = placed([P, 2, KP], U16, "w1_w1", W1_HALF1_AT) if b else held([P, 2, KP], U16, "w1_w0")
            nc.sync.dma_start(out=words[:].bitcast(I32),
                              in_=w1_words[:, :, 2 * KP * b : 2 * KP * (b + 1)].rearrange("a p n -> p a n").bitcast(I32))
            return words

        w2_raw, travel_sb, w1_w, tab_w = {}, {}, {}, {}
        nc.sync.dma_start(offs2_sb[:], offs2)
        nc.sync.dma_start(out=tab2_w[:].bitcast(I32), in_=tab2_words[0].bitcast(I32))
        nc.sync.dma_start(offs_sb[:], offs)
        nc.sync.dma_start(out=tab_s[0:P:SPREAD, 0, :].bitcast(I32),
                          in_=tab_scales.rearrange("a q n -> q a n").bitcast(I32))
        load_scale_rows(tab2_s, tab2_scales, range(LIVE - 1))
        w2_raw[0] = load_rows("w2_raw0", w2[:, half(0)])
        load_scale_rows(tab2_s, tab2_scales, [LIVE - 1])
        w1_w[0] = load_w1(0)
        load_scale_rows(w1_s, w1_scales)
        tab_w[0] = load_tab(0)
        nc.sync.dma_start(out=gain_row[0:1], in_=gain[half(1)].unsqueeze(0))
        v2_w = held([P, S], U16, "v2_w")
        v_g = held([P, S], U8, "v_g")
        nc.vector.tensor_copy(v2_w[:], tab2_w[:].indirect(offs2_sb[:]))
        nc.vector.tensor_copy(v_g[:], tab_s[:, 0, :].indirect(offs_sb[:]))
        for q in (0, 2, 1, 3):
            nc.sync.dma_start(out=v_s[QUAD * q : QUAD * q + LIVE].bitcast(I32),
                              in_=v_g[QUAD * q : QUAD * (q + 1) : SPREAD].bitcast(I32))
        tab_w[1] = load_tab(1)
        w1_w[1] = load_w1(1)
        w3_s = placed([P, 1, N], U8, "w3_s", W3_SCALES_AT)
        clear(w3_s)
        v2_s = held([P, S], U8, "v2_s")
        nc.vector.tensor_copy(v2_s[:], tab2_s[:, 0, :].indirect(offs2_sb[:]))
        gain_sb = placed([P, 2, PACK], F32, "gain_sb", GAIN_AT)
        for q in range(P // QUAD):
            nc.sync.dma_start(out=w3_s[QUAD * q + LIVE : QUAD * q + 3 * LIVE, 0, :].bitcast(I32),
                              in_=w3_scales[:, LIVE * q : LIVE * (q + 1), :].bitcast(I32))
        nc.sync.dma_start(out=gain_sb[:], in_=gain.rearrange("(b p t) -> p b t", b=2, t=PACK))
        w2_raw[1] = load_rows("w2_raw1", w2[:, half(1)], W2_HALF1_AT)

        v_w = [held([P, S], U32, f"v_w{a}") for a in range(2)]
        w1d_first = placed([P, 2, KP], U16, "w1d_first", CHAIN_AT)
        w1d_w = {(a, 0): w1d_first[:, a, :] for a in range(2)}
        entries = [slice(S // 2 * e, S // 2 * (e + 1)) for e in range(2)]
        w1d_s = [held([P, 2, KP], U8, f"w1d_s{b}") for b in range(2)]
        sat, damp, part, w2_q, w4_q, hq, zq, w3d_w = {}, {}, {}, {}, {}, {}, {}, {}

        def slip(b, offset=None):
            sat[b] = held_or_placed([P, PACK, S], F32, f"sat{b}", None, offset)
            accs = [bank(f"slip{b}{t}", PACK * (1 - b) + t) for t in range(PACK)]
            for a in range(2):
                for t in range(PACK):
                    cols = slice(P * t, P * (t + 1))
                    nc.tensor.matmul_mx(out=accs[t][:], lhsT=w1d_w[a, b][:, cols].bitcast(FP4X4),
                                        lhsT_scale=w1d_s[b][:, a, cols],
                                        rhs=v_w[a][:].bitcast(FP8X4), rhs_scale=v_s[:, a, :],
                                        start=(a == 0), stop=(a == 1))
            for t in range(PACK):
                nc.scalar.activation(out=sat[b][:, t, :], in_=accs[t][:], func=ACT.Tanh)

        def slip_by_entries(b):
            sat[b] = held([P, PACK, S], F32, f"sat{b}")
            accs = {(e, u): bank(f"slip{b}{e}{u}", PACK + 2 * e + u) for e in range(2) for u in range(2)}
            for a in range(2):
                for e, u in accs:
                    for v in range(2):
                        cols = slice(P * (2 * u + v), P * (2 * u + v + 1))
                        nc.tensor.matmul_mx(out=accs[e, u][:, entries[v]], lhsT=w1d_w[a, b][:, cols].bitcast(FP4X4),
                                            lhsT_scale=w1d_s[b][:, a, cols],
                                            rhs=v_w[a][:, entries[e]].bitcast(FP8X4), rhs_scale=v_s[:, a, entries[e]],
                                            start=(a == 0 and v == 0), stop=(a == 1 and v == 1))
            for e, u in accs:
                nc.scalar.activation(out=sat[b][:, 2 * u : 2 * u + 2, entries[e]],
                                     in_=accs[e, u][:].rearrange("p (v s) -> p v s", v=2), func=ACT.Tanh)

        def site(b, banks, offset=None):
            codes, scales = w2_q[b]
            damp[b] = held_or_placed([P, PACK, S], F32, f"damp{b}", None, offset)
            for t in range(PACK):
                cols = slice(P * t, P * (t + 1))
                acc = bank(f"site{b}{t}", banks[t])
                nc.tensor.matmul_mx(out=acc[:], lhsT=codes[:, cols].bitcast(FP8X4), lhsT_scale=scales[:, cols],
                                    rhs=v2_w[:].bitcast(FP4X4), rhs_scale=v2_s[:], start=True, stop=True)
                nc.scalar.activation(out=damp[b][:, t, :], in_=acc[:], func=ACT.Sigmoid, scale=-1.0)

        def site_turned(banks, turned_banks, offset):
            codes, scales = w2_q[1]
            across = placed([P, PACK, PACK, P], F32, "damp_across", offset)
            turned = {(e, u): bank(f"damp1{e}{u}", turned_banks[2 * e + u]) for e in range(2) for u in range(2)}
            for j in range(PACK):
                mine = slice(P * j, P * (j + 1))
                acc = bank(f"site1{j}", banks[j])
                nc.tensor.matmul_mx(out=acc[:], lhsT=v2_w[:, mine].bitcast(FP4X4), lhsT_scale=v2_s[:, mine],
                                    rhs=codes[:].bitcast(FP8X4), rhs_scale=scales[:], start=True, stop=True)
                nc.scalar.activation(out=across[:, j], in_=acc[:].rearrange("p (m t) -> p t m", t=PACK),
                                     func=ACT.Sigmoid, scale=-1.0)
            for j in range(PACK):
                for t in range(PACK):
                    first = S // 2 * (t % 2) + P * (j % 2)
                    nc.tensor.transpose(turned[j // 2, t // 2][:, first : first + P], across[:, j, t, :], identity[:])
            return turned

        def damped(b, slices, cols=slice(0, S)):
            for t in slices:
                nc.vector.scalar_tensor_tensor(
                    out=part[b][:, t, cols], in0=sat[b][:, t, cols], scalar=gain_sb[:, b, t : t + 1],
                    in1=damp[b][:, t, cols], op0=ALU.mult, op1=ALU.mult)

        def h_rounded(b, gains, offset=None):
            vals = held_or_placed([P, WOVEN], BF16, f"h_b{b}", None, offset)
            gains = gains.unsqueeze(1).unsqueeze(3).to_broadcast([P, S // PAIR, PACK, PAIR])
            nc.vector.tensor_tensor(out=woven(vals[:]), in0=by_pairs(sat[b][:]), in1=gains, op=ALU.mult)
            return vals

        def z_rounded(vals, b, cols, engine=nc.vector):
            engine.tensor_tensor(out=woven(vals), in0=by_pairs(part[b][:, :, cols]),
                                 in1=by_pairs(travel_sb[b][:, :, cols]), op=ALU.add)

        for b in range(2):
            deal(w1d_s[b][:], w1_s[:, :, half(b)])
        w2_q[0] = quantize(rounded(w2_raw[0], "w2_b0"), "w2q0", offset=W2_CODES0_AT)
        deal(w1d_first[:], w1_w[0][:], nc.scalar.copy)
        site(0, [0, 1, 2, 3])
        travel_sb[0] = load_rows("travel0", travel[half(0), :], slot="w2_raw0")
        w3_rows = w3_words.rearrange("a p n t -> a p (n t)").bitcast(I32)
        w3_w = held([P, 3, KP], I32, "w3_w", "w2_b0")
        nc.sync.dma_start(out=w3_w[:, 0:2, :].rearrange("p g n -> p (g n)"), in_=w3_rows[0])
        nc.sync.dma_start(out=w3_w[:, 2, :], in_=w3_rows[1][:, half(0)])
        nc.vector.tensor_copy(v_w[0][:], tab_w[0][:].bitcast(U32).indirect(offs_sb[:]))
        w4_row0 = load_rows("w4_row0", w4[half(0), :], slot="tab_w0")
        for cols in entries:
            nc.vector.tensor_copy(v_w[1][:, cols],
                                  tab_w[1][:].bitcast(U32).indirect(offs_sb[:, cols.start // 16 : cols.stop // 16]))
        for a, copy in enumerate((nc.scalar.copy, nc.vector.tensor_copy)):
            words = held([P, 1, KP], U16, f"w1d_second{a}")
            deal(words[:], w1_w[1][:, a : a + 1], copy)
            w1d_w[a, 1] = words[:, 0, :]
        w3d_s = held([P, 2, KP], U8, "w3d_s")
        deal(w3d_s[:], w3_s[:, 0, :].rearrange("p (g n) -> p g n", g=2))

        slip_by_entries(0)
        w2_b1 = placed([P, WOVEN], BF16, "w2_b1", CHAIN_AT)
        nc.scalar.copy(out=woven(w2_b1[:]), in_=by_pairs(w2_raw[1][:]))
        part[0] = placed([P, PACK, S], F32, "part0", PART0_AT)
        for cols in entries:
            damped(0, range(PACK), cols)
        travel_sb[1] = load_rows("travel1", travel[half(1), :], slot="damp0")
        h_b0 = h_rounded(0, gain_sb[:, 0, :])
        w4_raw10 = load_rows("w4_raw10", w4[half(1), half(0)], slot="sat0")
        w2_q[1] = quantize(w2_b1, "w2q1")
        slip(1, SAT1_AT)
        gain_bank = bank("gain_bank", 7)
        for t in range(PACK):
            nc.tensor.transpose(gain_bank[:, P * t : P * (t + 1)], gain_row[:, t:KP:PACK], identity[:])
        turned = site_turned([4, 5, 6, 0], [1, 2, 3, 4], DAMP1_AT)
        hq[0] = quantize(h_b0, "hq0", offset=W2_HALF1_AT)
        shares = [slice(0, S - POOL_SHARE), slice(S - POOL_SHARE, S)]
        z_b0 = [placed([P, PACK * (S - POOL_SHARE)], BF16, "z_b00", CHAIN_AT),
                held([P, PACK * POOL_SHARE], BF16, "z_b01", "h_b0")]
        z_rounded(z_b0[0][:], 0, shares[0])
        h_b1 = h_rounded(1, gain_bank[:, 0:S:P], CHAIN_AT + 4 * KIB - ALIGN)
        z_rounded(z_b0[1][:], 0, shares[1], nc.gpsimd)
        last = placed([P, PACK * KP], F32, "last", PART0_AT)
        w4_raw11 = [last[:, 2 * KP * i : 2 * KP * (i + 1)].rearrange("p (j c) -> p j c", j=PACK) for i in range(2)]
        for i in range(2):
            src = w4[half(1), KP + KP // 2 * i : KP + KP // 2 * (i + 1)]
            nc.sync.dma_start(out=w4_raw11[i], in_=src.rearrange("(p j) c -> p j c", j=PACK))

        w3d_early = held([P, 3, KP], U32, "w3d_early", "v2_w")
        deal_by_pairs(w3d_early[:], w3_w[:].bitcast(U32), nc.scalar.copy)
        w3d_w[0, 0], w3d_w[0, 1], w3d_w[1, 0] = (w3d_early[:, i, :] for i in range(3))
        w4_b00 = rounded(w4_row0[:, :, half(0)], "w4_b00", "w2q1_scales")
        w4_b01 = rounded(w4_row0[:, :, half(1)], "w4_b01", "v_w0")

        part[1] = held([P, PACK, S], F32, "part1")
        for e, cols in enumerate(entries):
            for t in range(PACK):
                nc.vector.scalar_tensor_tensor(
                    out=part[1][:, t, cols], in0=sat[1][:, t, cols], scalar=gain_sb[:, 1, t : t + 1],
                    in1=turned[e, t // 2][:, entries[t % 2]], op0=ALU.mult, op1=ALU.mult)
        hq[1] = quantize(h_b1, "hq1", offset=DAMP1_AT + 2 * KIB)
        zq[0] = placed([P, S], U32, "zq0_codes", DAMP1_AT), held([P, S], U8, "zq0_scales")
        for vals, cols in zip(z_b0, shares):
            nc.vector.quantize_mx(out=zq[0][0][:, cols].bitcast(FP8X4), scales=zq[0][1][:, cols], in_=vals[:])
        w3_last = placed([P, 1, KP], I32, "w3_last", CHAIN_AT)
        nc.sync.dma_start(out=w3_last[:, 0, :], in_=w3_rows[1][:, half(1)])
        z_b1 = held([P, WOVEN], BF16, "z_b1")
        w4_q[0, 0] = quantize(w4_b00, "w4q00")
        z_rounded(z_b1[:], 1, slice(0, S))
        w4_q[0, 1] = quantize(w4_b01, "w4q01")
        w4_b10 = held([P, WOVEN], BF16, "w4_b10", "v2_s")
        round_weight(w4_raw10[:, :, : PACK * SCALAR_THIRD], w4_b10[:])
        round_weight(w4_raw10[:, :, PACK * SCALAR_THIRD :], w4_b10[:], SCALAR_THIRD, nc.vector.tensor_copy)
        zq[1] = quantize(z_b1, "zq1")

        def quantize_in_halves(vals, name):
            codes, scales = held([P, KP], U32, name + "_codes"), held([P, KP], U8, name + "_scales")
            for cols in entries:
                nc.vector.quantize_mx(out=codes[:, cols].bitcast(FP8X4), scales=scales[:, cols],
                                      in_=vals[:, PACK * cols.start : PACK * cols.stop])
            return codes, scales

        w4_q[1, 0] = quantize_in_halves(w4_b10, "w4q10")
        w4_b11 = held([P, WOVEN], BF16, "w4_b11", "tab_w0")
        round_weight(w4_raw11[0], w4_b11[:])
        round_weight(w4_raw11[1], w4_b11[:], P // 2, nc.vector.tensor_copy)
        w3d_last = held([P, 1, KP], I32, "w3d_last")
        deal_by_pairs(w3d_last[:], w3_last[:])
        w3d_w[1, 1] = w3d_last[:, 0, :]
        w4_q[1, 1] = quantize_in_halves(w4_b11, "w4q11")
        y_banks = [[5, 6, 0, 7], [1, 2, 3, 4]]

        y_scales = held([P, 2, S], U8, "y_scales")
        y_accs = [[bank(f"y{g}{t}", y_banks[g][t]) for t in range(PACK)] for g in range(2)]

        def y_pass(g, a, from_h, t, start=False, stop=False):
            mine = slice(P * t, P * (t + 1))
            if from_h:
                lw, ls = w3d_w[a, g][:, mine], w3d_s[LIVE * (a + 1) : P, g, mine]
                rw, rs = hq[a]
            else:
                lw, ls = w4_q[a, g][0][:, mine], w4_q[a, g][1][:, mine]
                rw, rs = zq[a]
            nc.tensor.matmul_mx(out=y_accs[g][t][:], lhsT=lw.bitcast(FP8X4), lhsT_scale=ls,
                                rhs=rw[:].bitcast(FP8X4), rhs_scale=rs[:], start=start, stop=stop)

        def y_passes(g, a, from_h, start=False, stop=False):
            for t in range(PACK):
                y_pass(g, a, from_h, t, start, stop)

        y_passes(0, 0, True, start=True)
        y_passes(1, 0, True, start=True)
        y_passes(0, 1, True)
        y_passes(0, 0, False)
        y_passes(1, 0, False)
        y_passes(0, 1, False, stop=True)
        for t in range(PACK):
            y_pass(1, 1, True, t)
            y_pass(1, 1, False, t, stop=True)

        y_codes = [held([P, S], U32, f"y_codes{g}") for g in range(2)]
        y_vals = [held([P, WOVEN], BF16, "y_b0", "w2_b0"), held([P, WOVEN], BF16, "y_b1", "z_b1")]
        y = [held([P, PACK, S], F32, "y0", "damp0"), held([P, PACK, S], F32, "y1", "part1")]
        rows = [out_0[half(g), :].rearrange("(p t) s -> p t s", t=PACK) for g in range(2)]

        def empty(g, t, copy):
            copy(out=y[g][:, t, :], in_=y_accs[g][t][:])

        def store_rows(g, slices):
            nc.sync.dma_start(out=rows[g][:, slices, :], in_=y[g][:, slices, :])

        def planes(g):
            for cols in entries:
                nc.vector.tensor_copy(out=woven(y_vals[g][:, PACK * cols.start : PACK * cols.stop]),
                                      in_=by_pairs(y[g][:, :, cols]))
            for cols in entries:
                nc.vector.quantize_mx(out=y_codes[g][:, cols].bitcast(FP8X4), scales=y_scales[:, g, cols],
                                      in_=y_vals[g][:, PACK * cols.start : PACK * cols.stop])

        def store_codes(g, cols):
            nc.sync.dma_start(out=out_1[g, :, cols, :].rearrange("p m t -> p (m t)").bitcast(I32),
                              in_=y_codes[g][:, cols].bitcast(I32))

        for t in range(PACK):
            empty(0, t, nc.vector.tensor_copy if t in [3] else nc.scalar.copy)
            if t < 2:
                store_rows(0, slice(t, t + 1))
        store_rows(0, slice(2, PACK))
        planes(0)
        for t in range(PACK):
            empty(1, t, nc.vector.tensor_copy if t in [] else nc.scalar.copy)
            if t == PACK - 1:
                store_codes(0, slice(0, S))
            if t % 2:
                store_rows(1, slice(t - 1, t + 1))
        planes(1)
        for cols in entries:
            store_codes(1, cols)
        for r in range(LIVE):
            queue = nc.scalar if r < LIVE - 1 else nc.sync
            queue.dma_start(out=out_2[:, r : LIVE * LIVE : LIVE, :].rearrange("g q m -> q g m").bitcast(I32),
                            in_=y_scales[r:P:QUAD].bitcast(I32))
